import numpy as np
import ml_dtypes


def mxq(x, axis, fmt="e4m3"):
    dtype, down = {"e4m3": (ml_dtypes.float8_e4m3fn, 7), "e5m2": (ml_dtypes.float8_e5m2, 14)}[fmt]
    v = np.moveaxis(np.asarray(x, np.float32).astype(ml_dtypes.bfloat16).astype(np.float64), axis, -1)
    blocks = v.reshape(v.shape[:-1] + (-1, 32))
    amax = np.abs(blocks).max(-1, keepdims=True)
    byte = np.maximum(np.where(amax > 0, np.frexp(amax)[1] - 1 + 127, 0) - down, 1)
    scale = np.exp2(byte - 127.0)
    codes = (blocks / scale).astype(np.float32).astype(dtype).astype(np.float64)
    return np.moveaxis((codes * scale).reshape(v.shape), -1, axis)


WIDE = False


def mx_kscale(k):
    if not WIDE:
        return np.ones(k)
    levels = np.array([24, -24, 12, -12, 0])
    if k % 512:
        return np.exp2(np.random.permutation(np.resize(levels, k // 32))).repeat(32)
    a = np.empty((k // 512, 16))
    for p in range(k // 512):
        a[p, :8] = np.random.permutation(np.resize(levels, 8))
        for g in range(8):
            far = levels[np.abs(levels - a[p, g]) >= 10]
            a[p, g + 8] = far[np.random.randint(len(far))]
    return np.exp2(a.ravel()).repeat(32)


def f64(x):
    return np.asarray(x).astype(np.float64)


def striped8(idx):
    return np.concatenate([v.reshape(-1, 16).T for v in idx]).astype(np.uint16)


def unstriped8(offs):
    return np.stack([offs[16 * g:16 * g + 16].T.reshape(-1) for g in range(8)]).astype(np.int64)


E2M1 = np.array([0.0, 0.5, 1.0, 1.5, 2.0, 3.0, 4.0, 6.0, -0.0, -0.5, -1.0, -1.5, -2.0, -3.0, -4.0, -6.0])


def pack_weight(w, fmt):
    k, n = w.shape
    w = f64(np.asarray(w, np.float32).astype(ml_dtypes.bfloat16)).reshape(k // 32, 32, n)
    amax = np.abs(w).max(1)
    if fmt == "e4m3":
        byte = np.frexp(amax)[1] - 1 + 127 - 7
    else:
        mant, ex = np.frexp(amax / 6.0)
        byte = np.where(mant > 0.5, ex, ex - 1) + 127
    byte = np.clip(np.where(amax > 0, byte, 1), 1, 254)
    scaled = (w * np.exp2(127.0 - byte)[:, None, :]).reshape(k, n).astype(np.float32)
    by_word = np.ascontiguousarray(scaled.reshape(k // 512, 128, 4, n).transpose(0, 1, 3, 2))
    if fmt == "e4m3":
        words = by_word.astype(ml_dtypes.float8_e4m3fn).view(np.uint8)
    else:
        c = by_word.astype(ml_dtypes.float4_e2m1fn).view(np.uint8) & 0xF
        words = (c[..., 0::2] | (c[..., 1::2] << 4)).reshape(k // 512, 128, 2 * n)
    return np.ascontiguousarray(words), np.ascontiguousarray(byte.astype(np.uint8).reshape(k // 512, 16, n))


def unpack_weight(words, scales, fmt):
    g, _, n = scales.shape
    words = np.ascontiguousarray(words).reshape(g, 128, n, -1)
    if fmt == "e4m3":
        vals = words.view(ml_dtypes.float8_e4m3fn).astype(np.float64)
    else:
        nib = np.empty((g, 128, n, 4), np.uint8)
        nib[..., 0::2] = words & 0xF
        nib[..., 1::2] = words >> 4
        vals = E2M1[nib]
    vals = vals * np.repeat(np.exp2(scales.astype(np.float64) - 127.0), 8, axis=1)[..., None]
    return vals.transpose(0, 1, 3, 2).reshape(g * 512, n)


K, R, N, T, J = 1024, 512, 512, 2048, 1024


def setup_inputs():
    n = np.random.standard_normal
    s = mx_kscale(K)[:, None]
    u = mx_kscale(R)[:, None]
    p_wg = pack_weight(n((K, R)) / np.sqrt(K) / s, "e2m1")
    p_wu = pack_weight(n((K, R)) / np.sqrt(K) / s * u.T, "e2m1")
    p_wd = pack_weight(n((R, N)) / np.sqrt(R) / u, "e2m1")
    return {
        "xT": (n((K, T)) * s).astype(np.float32),
        "wgt": np.repeat(np.random.uniform(0.5, 2.0, (8, J)), 16, axis=0).astype(np.float32),
        "wg_words": p_wg[0],
        "wg_scales": p_wg[1],
        "wu_words": p_wu[0],
        "wu_scales": p_wu[1],
        "wd_words": p_wd[0],
        "wd_scales": p_wd[1],
        "wgo": np.repeat(np.random.uniform(0.5, 2.0, (8, J)), 16, axis=0).astype(np.float32),
        "offs": striped8(np.stack([np.random.permutation(T)[:J] for _ in range(8)])),
        "offs2": striped8(np.stack([np.random.permutation(T)[:J] for _ in range(8)])),
    }


def reference(xT, wgt, wg_words, wg_scales, wu_words, wu_scales, wd_words, wd_scales, wgo, offs, offs2):
    idx = unstriped8(offs)
    idx2 = unstriped8(offs2)
    rows = np.arange(K)
    xg = f64(wgt)[rows // 4 % 128] * f64(xT)[rows[:, None], idx[rows % 512 // 64]]
    xT_ = mxq(xg, 0, "e4m3")
    wg_ = unpack_weight(wg_words, wg_scales, "e2m1")
    wu_ = unpack_weight(wu_words, wu_scales, "e2m1")
    ga = wg_.T @ xT_
    ub = wu_.T @ xT_
    h = np.maximum(ga, 0.0) * ub
    h_ = mxq(h, 0, "e4m3")
    wd_ = unpack_weight(wd_words, wd_scales, "e2m1")
    y = wd_.T @ h_
    out = np.zeros((N, T))
    rows = np.arange(N)
    out[rows[:, None], idx2[rows % 128 // 16]] = f64(wgo)[rows % 128] * (y)
    return out

@@ -1,0 +1,178 @@
+from contextlib import ExitStack
+
+import concourse.mybir as mybir
+from concourse.masks import make_identity
+
+K, R, N, T, J = 1024, 512, 512, 2048, 1024
+FLOPS = 2 * (2 * K * R + R * N) * J
+
+F32 = mybir.dt.float32
+BF16 = mybir.dt.bfloat16
+I32 = mybir.dt.int32
+U32 = mybir.dt.uint32
+U16 = mybir.dt.uint16
+U8 = mybir.dt.uint8
+FP8X4 = mybir.dt.float8_e4m3fn_x4
+FP4X4 = mybir.dt.float4_e2m1fn_x4
+MULT = mybir.AluOpType.mult
+RELU = mybir.ActivationFunctionType.Relu
+
+P = 128
+PACK = 4
+PASSES = K // (P * PACK)
+CH = 128
+CHUNKS = J // CH
+NT = N // P
+LANE = 16
+FIRST = 256
+EARLY = 4
+
+
+def tile_list_relu_scat_kernel(
+    tc, xT, wgt, wg_words, wg_scales, wu_words, wu_scales, wd_words, wd_scales, wgo, offs, offs2, out
+):
+    nc = tc.nc
+    with ExitStack() as ctx:
+        keep = ctx.enter_context(tc.tile_pool(name="keep", bufs=1))
+        ring = ctx.enter_context(tc.tile_pool(name="ring", bufs=3))
+        psum = ctx.enter_context(tc.psum_pool(name="psum", bufs=2))
+
+        pick = keep.tile([P, J // LANE], U16, name="pick")
+        place = keep.tile([P, J // LANE], U16, name="place")
+        x_rows = xT.rearrange("(a p i) t -> a i p t", p=P, i=PACK)
+        planes = [keep.tile([P, T], F32, name=f"plane{m}") for m in range(PASSES * PACK)]
+        gain = keep.tile([P, J], F32, name="gain")
+        gain_out = keep.tile([P, J], F32, name="gain_out")
+        wg_w = [keep.tile([P, 2 * R], U8, name=f"wg_w{a}", align_bytes=64) for a in range(PASSES)]
+        wu_w = [keep.tile([P, 2 * R], U8, name=f"wu_w{a}", align_bytes=64) for a in range(PASSES)]
+        wd_w = keep.tile([P, 2 * N], U8, name="wd_w", align_bytes=64)
+        wg_s = keep.tile([P, PASSES * R], U8, name="wg_s", align_bytes=64)
+        wu_s = keep.tile([P, PASSES * R], U8, name="wu_s", align_bytes=64)
+        wd_s = keep.tile([P, N], U8, name="wd_s", align_bytes=64)
+        ident = keep.tile([P, P], F32, name="ident")
+        pages = [keep.tile([P, T], F32, name=f"page{q}") for q in range(NT)]
+
+        nc.sync.dma_start(planes[0][:], x_rows[0, 0])
+        nc.sync.dma_start(pick[:], offs)
+        for h in range(2):
+            nc.sync.dma_start(gain[:, h * (J // 2) : (h + 1) * (J // 2)], wgt[:, h * (J // 2) : (h + 1) * (J // 2)])
+        for m in range(1, PASSES * PACK):
+            nc.sync.dma_start(planes[m][:], x_rows[m // PACK, m % PACK])
+        for a in range(PASSES):
+            nc.sync.dma_start(wg_w[a][:].bitcast(I32), wg_words[a].bitcast(I32))
+            nc.sync.dma_start(wu_w[a][:].bitcast(I32), wu_words[a].bitcast(I32))
+        nc.sync.dma_start(wd_w[:].bitcast(I32), wd_words[0].bitcast(I32))
+        nc.sync.dma_start(place[:], offs2)
+        nc.sync.dma_start(gain_out[:], wgo)
+
+        for plane_s, dram_s in ((wg_s, wg_scales), (wu_s, wu_scales), (wd_s, wd_scales)):
+            nc.gpsimd.memset(plane_s[:].bitcast(I32), 0)
+            passes = dram_s.shape[0]
+            rows = dram_s.bitcast(I32).rearrange("a (q r) n -> q r a n", r=4)
+            for q in range(4):
+                nc.gpsimd.dma_start(
+                    plane_s[32 * q : 32 * q + 4, :].bitcast(I32).rearrange("p (a n) -> p a n", a=passes), rows[q]
+                )
+        make_identity(nc, ident[:])
+        for q in range(NT):
+            nc.vector.memset(pages[q][:], 0.0)
+
+        x_codes = [keep.tile([P, J], U32, name=f"x_codes{a}", align_bytes=64) for a in range(PASSES)]
+        x_scales = [keep.tile([P, J], U8, name=f"x_scales{a}", align_bytes=64) for a in range(PASSES)]
+
+        def gather(dst, m, j0, j1):
+            nc.vector.tensor_tensor(dst, planes[m][:].indirect(pick[:, j0 // LANE : j1 // LANE]), gain[:, j0:j1], MULT)
+
+        def weave(src, width, name):
+            woven = ring.tile([P, width * PACK], BF16, name=name, align_bytes=64)
+            nc.scalar.copy(
+                woven[:].rearrange("p (c i t) -> p c t i", i=4, t=PACK),
+                src.rearrange("p t (c i) -> p c t i", i=4),
+            )
+            return woven
+
+        def quantize_x(a, j0, width, woven):
+            nc.vector.quantize_mx(
+                out=x_codes[a][:, j0 : j0 + width].bitcast(FP8X4), scales=x_scales[a][:, j0 : j0 + width], in_=woven[:]
+            )
+
+        picked0 = keep.tile([P, PACK, J], F32, name="picked0")
+        gather(picked0[:, 0, : J // 2], 0, 0, J // 2)
+        gather(picked0[:, 0, J // 2 :], 0, J // 2, J)
+        for i in range(1, PACK):
+            gather(picked0[:, i, :], i, 0, J)
+        picked1a = keep.tile([P, PACK, FIRST], F32, name="picked1a")
+        picked1b = keep.tile([P, PACK, J - FIRST], F32, name="picked1b")
+        for j0 in range(0, J, 256):
+            quantize_x(0, j0, 256, weave(picked0[:, :, j0 : j0 + 256], 256, "woven0"))
+        for i in range(PACK):
+            gather(picked1a[:, i, :], PACK + i, 0, FIRST)
+            gather(picked1b[:, i, :], PACK + i, FIRST, J)
+
+        y_sb = keep.tile([P, NT, J], F32, name="y_sb")
+
+        def scatter(q, j0, j1):
+            nc.vector.tensor_tensor(
+                pages[q][:].indirect(place[:, j0 // LANE : j1 // LANE]), y_sb[:, q, j0:j1], gain_out[:, j0:j1], MULT
+            )
+
+        for c in range(CHUNKS):
+            j0 = c * CH
+            cols = slice(j0, j0 + CH)
+            src = picked1a[:, :, cols] if j0 < FIRST else picked1b[:, :, j0 - FIRST : j0 - FIRST + CH]
+            quantize_x(1, j0, CH, weave(src, CH, "woven1"))
+            g_ps = psum.tile([P, R], F32, name="g_ps")
+            u_ps = psum.tile([P, R], F32, name="u_ps")
+            for a in range(PASSES):
+                for acc, words, scales in ((g_ps, wg_w, wg_s), (u_ps, wu_w, wu_s)):
+                    nc.tensor.matmul_mx(
+                        acc[:],
+                        lhsT=x_codes[a][:, cols].bitcast(FP8X4),
+                        lhsT_scale=x_scales[a][:, cols],
+                        rhs=words[a][:].bitcast(FP4X4),
+                        rhs_scale=scales[:, a * R : (a + 1) * R],
+                        start=(a == 0),
+                        stop=(a == PASSES - 1),
+                    )
+            gate = ring.tile([P, R], F32, name="gate")
+            nc.scalar.activation(
+                gate[:].rearrange("p (u m e) -> p u m e", u=2, e=2),
+                g_ps[:].rearrange("p (m u e) -> p u m e", u=2, e=2),
+                RELU,
+            )
+            h_rows = ring.tile([P, R], BF16, name="h_rows")
+            nc.vector.tensor_tensor(
+                h_rows[:].rearrange("p (u m e) -> p u m e", u=2, e=2),
+                u_ps[:].rearrange("p (m u e) -> p u m e", u=2, e=2),
+                gate[:].rearrange("p (u m e) -> p u m e", u=2, e=2),
+                MULT,
+            )
+            pairs = h_rows[:].bitcast(F32)
+            t_ps = psum.tile([P, 2, CH], F32, name="t_ps")
+            for u in range(2):
+                nc.tensor.transpose(t_ps[:, u, :], pairs[:, u * P : (u + 1) * P], ident[:])
+            h_woven = ring.tile([P, CH * PACK], BF16, name="h_woven", align_bytes=64)
+            nc.scalar.copy(
+                h_woven[:].bitcast(F32).rearrange("p (j u) -> p j u", u=2), t_ps[:].rearrange("p u j -> p j u")
+            )
+            h_codes = ring.tile([P, CH], U32, name="h_codes", align_bytes=64)
+            h_scales = ring.tile([P, CH], U8, name="h_scales", align_bytes=64)
+            nc.vector.quantize_mx(out=h_codes[:].bitcast(FP8X4), scales=h_scales[:], in_=h_woven[:])
+            y_ps = psum.tile([P, NT, CH], F32, name="y_ps")
+            for q in range(NT):
+                nc.tensor.matmul_mx(
+                    y_ps[:, q, :],
+                    lhsT=wd_w[:, 2 * P * q : 2 * P * (q + 1)].bitcast(FP4X4),
+                    lhsT_scale=wd_s[:, P * q : P * (q + 1)],
+                    rhs=h_codes[:].bitcast(FP8X4),
+                    rhs_scale=h_scales[:],
+                    start=True,
+                    stop=True,
+                )
+            nc.scalar.copy(y_sb[:, :, cols], y_ps[:])
+            if c < EARLY:
+                for q in range(NT):
+                    scatter(q, j0, j0 + CH)
+        for q in range(NT):
+            scatter(q, EARLY * CH, J)
+            nc.sync.dma_start(out[q * P : (q + 1) * P, :], pages[q][:])

@@ -25,7 +25,9 @@ CHUNKS = J // CH
 NT = N // P
 LANE = 16
 FIRST = 256
-EARLY = 4
+EARLY = 2
+LAG = 2
+BANKS = 3
 
 
 def tile_list_relu_scat_kernel(
@@ -34,8 +36,8 @@ def tile_list_relu_scat_kernel(
     nc = tc.nc
     with ExitStack() as ctx:
         keep = ctx.enter_context(tc.tile_pool(name="keep", bufs=1))
-        ring = ctx.enter_context(tc.tile_pool(name="ring", bufs=3))
-        psum = ctx.enter_context(tc.psum_pool(name="psum", bufs=2))
+        ring = ctx.enter_context(tc.tile_pool(name="ring", bufs=4))
+        psum = ctx.enter_context(tc.psum_pool(name="psum", bufs=1))
 
         pick = keep.tile([P, J // LANE], U16, name="pick")
         place = keep.tile([P, J // LANE], U16, name="place")
@@ -52,6 +54,17 @@ def tile_list_relu_scat_kernel(
         ident = keep.tile([P, P], F32, name="ident")
         pages = [keep.tile([P, T], F32, name=f"page{q}") for q in range(NT)]
 
+        def load_scales(plane_s, dram_s, queue):
+            passes = dram_s.shape[0]
+            rows = dram_s.bitcast(I32).rearrange("a (q r) n -> q r a n", r=4)
+            for q in range(4):
+                queue.dma_start(
+                    plane_s[32 * q : 32 * q + 4, :].bitcast(I32).rearrange("p (a n) -> p a n", a=passes), rows[q]
+                )
+
+        for plane_s in (wg_s, wu_s, wd_s):
+            nc.gpsimd.memset(plane_s[:].bitcast(I32), 0)
+        make_identity(nc, ident[:])
         nc.sync.dma_start(planes[0][:], x_rows[0, 0])
         nc.sync.dma_start(pick[:], offs)
         for h in range(2):
@@ -62,20 +75,14 @@ def tile_list_relu_scat_kernel(
             nc.sync.dma_start(wg_w[a][:].bitcast(I32), wg_words[a].bitcast(I32))
             nc.sync.dma_start(wu_w[a][:].bitcast(I32), wu_words[a].bitcast(I32))
         nc.sync.dma_start(wd_w[:].bitcast(I32), wd_words[0].bitcast(I32))
+        load_scales(wd_s, wd_scales, nc.sync)
         nc.sync.dma_start(place[:], offs2)
         nc.sync.dma_start(gain_out[:], wgo)
 
-        for plane_s, dram_s in ((wg_s, wg_scales), (wu_s, wu_scales), (wd_s, wd_scales)):
-            nc.gpsimd.memset(plane_s[:].bitcast(I32), 0)
-            passes = dram_s.shape[0]
-            rows = dram_s.bitcast(I32).rearrange("a (q r) n -> q r a n", r=4)
-            for q in range(4):
-                nc.gpsimd.dma_start(
-                    plane_s[32 * q : 32 * q + 4, :].bitcast(I32).rearrange("p (a n) -> p a n", a=passes), rows[q]
-                )
-        make_identity(nc, ident[:])
+        load_scales(wg_s, wg_scales, nc.gpsimd)
+        load_scales(wu_s, wu_scales, nc.gpsimd)
         for q in range(NT):
-            nc.vector.memset(pages[q][:], 0.0)
+            (nc.vector if q < EARLY else nc.gpsimd).memset(pages[q][:], 0.0)
 
         x_codes = [keep.tile([P, J], U32, name=f"x_codes{a}", align_bytes=64) for a in range(PASSES)]
         x_scales = [keep.tile([P, J], U8, name=f"x_scales{a}", align_bytes=64) for a in range(PASSES)]
@@ -116,13 +123,15 @@ def tile_list_relu_scat_kernel(
                 pages[q][:].indirect(place[:, j0 // LANE : j1 // LANE]), y_sb[:, q, j0:j1], gain_out[:, j0:j1], MULT
             )
 
-        for c in range(CHUNKS):
+        h_quant = {}
+
+        def first_layer(c):
             j0 = c * CH
             cols = slice(j0, j0 + CH)
             src = picked1a[:, :, cols] if j0 < FIRST else picked1b[:, :, j0 - FIRST : j0 - FIRST + CH]
             quantize_x(1, j0, CH, weave(src, CH, "woven1"))
-            g_ps = psum.tile([P, R], F32, name="g_ps")
-            u_ps = psum.tile([P, R], F32, name="u_ps")
+            g_ps = psum.tile([P, R], F32, name="g_ps", tag=f"gy{c % BANKS}")
+            u_ps = psum.tile([P, R], F32, name="u_ps", tag=f"u{c % BANKS}")
             for a in range(PASSES):
                 for acc, words, scales in ((g_ps, wg_w, wg_s), (u_ps, wu_w, wu_s)):
                     nc.tensor.matmul_mx(
@@ -147,8 +156,11 @@ def tile_list_relu_scat_kernel(
                 gate[:].rearrange("p (u m e) -> p u m e", u=2, e=2),
                 MULT,
             )
+            return h_rows
+
+        def turn_h(c, h_rows):
             pairs = h_rows[:].bitcast(F32)
-            t_ps = psum.tile([P, 2, CH], F32, name="t_ps")
+            t_ps = psum.tile([P, 2, CH], F32, name="t_ps", tag=f"t{c % 2}")
             for u in range(2):
                 nc.tensor.transpose(t_ps[:, u, :], pairs[:, u * P : (u + 1) * P], ident[:])
             h_woven = ring.tile([P, CH * PACK], BF16, name="h_woven", align_bytes=64)
@@ -158,7 +170,12 @@ def tile_list_relu_scat_kernel(
             h_codes = ring.tile([P, CH], U32, name="h_codes", align_bytes=64)
             h_scales = ring.tile([P, CH], U8, name="h_scales", align_bytes=64)
             nc.vector.quantize_mx(out=h_codes[:].bitcast(FP8X4), scales=h_scales[:], in_=h_woven[:])
-            y_ps = psum.tile([P, NT, CH], F32, name="y_ps")
+            h_quant[c] = (h_codes, h_scales)
+
+        def second_layer(c):
+            h_codes, h_scales = h_quant[c]
+            cols = slice(c * CH, (c + 1) * CH)
+            y_ps = psum.tile([P, NT, CH], F32, name="y_ps", tag=f"gy{(c + LAG) % BANKS}")
             for q in range(NT):
                 nc.tensor.matmul_mx(
                     y_ps[:, q, :],
@@ -170,9 +187,16 @@ def tile_list_relu_scat_kernel(
                     stop=True,
                 )
             nc.scalar.copy(y_sb[:, :, cols], y_ps[:])
-            if c < EARLY:
-                for q in range(NT):
-                    scatter(q, j0, j0 + CH)
+            for q in range(EARLY):
+                scatter(q, c * CH, (c + 1) * CH)
+
+        for c in range(CHUNKS + LAG):
+            h_rows = first_layer(c) if c < CHUNKS else None
+            if c >= LAG:
+                second_layer(c - LAG)
+            if c < CHUNKS:
+                turn_h(c, h_rows)
         for q in range(NT):
-            scatter(q, EARLY * CH, J)
+            if q >= EARLY:
+                scatter(q, 0, J)
             nc.sync.dma_start(out[q * P : (q + 1) * P, :], pages[q][:])

@@ -24,7 +24,8 @@ CH = 128
 CHUNKS = J // CH
 NT = N // P
 LANE = 16
-FIRST = 256
+GROUPS = (0, 128, 384, 896, 1024)
+HEAD = 256
 EARLY = 2
 LAG = 2
 BANKS = 3
@@ -63,12 +64,12 @@ def tile_list_relu_scat_kernel(
                 )
 
         for plane_s in (wg_s, wu_s, wd_s):
-            nc.gpsimd.memset(plane_s[:].bitcast(I32), 0)
+            nc.vector.memset(plane_s[:].bitcast(I32), 0)
         make_identity(nc, ident[:])
         nc.sync.dma_start(planes[0][:], x_rows[0, 0])
         nc.sync.dma_start(pick[:], offs)
-        for h in range(2):
-            nc.sync.dma_start(gain[:, h * (J // 2) : (h + 1) * (J // 2)], wgt[:, h * (J // 2) : (h + 1) * (J // 2)])
+        nc.sync.dma_start(gain[:, :HEAD], wgt[:, :HEAD])
+        nc.sync.dma_start(gain[:, HEAD:], wgt[:, HEAD:])
         for m in range(1, PASSES * PACK):
             nc.sync.dma_start(planes[m][:], x_rows[m // PACK, m % PACK])
         for a in range(PASSES):
@@ -82,7 +83,7 @@ def tile_list_relu_scat_kernel(
         load_scales(wg_s, wg_scales, nc.gpsimd)
         load_scales(wu_s, wu_scales, nc.gpsimd)
         for q in range(NT):
-            (nc.vector if q < EARLY else nc.gpsimd).memset(pages[q][:], 0.0)
+            nc.vector.memset(pages[q][:], 0.0)
 
         x_codes = [keep.tile([P, J], U32, name=f"x_codes{a}", align_bytes=64) for a in range(PASSES)]
         x_scales = [keep.tile([P, J], U8, name=f"x_scales{a}", align_bytes=64) for a in range(PASSES)]
@@ -104,17 +105,17 @@ def tile_list_relu_scat_kernel(
             )
 
         picked0 = keep.tile([P, PACK, J], F32, name="picked0")
-        gather(picked0[:, 0, : J // 2], 0, 0, J // 2)
-        gather(picked0[:, 0, J // 2 :], 0, J // 2, J)
+        gather(picked0[:, 0, :HEAD], 0, 0, HEAD)
+        gather(picked0[:, 0, HEAD:], 0, HEAD, J)
         for i in range(1, PACK):
             gather(picked0[:, i, :], i, 0, J)
-        picked1a = keep.tile([P, PACK, FIRST], F32, name="picked1a")
-        picked1b = keep.tile([P, PACK, J - FIRST], F32, name="picked1b")
+        spans = list(zip(GROUPS[:-1], GROUPS[1:]))
+        picked1 = [keep.tile([P, PACK, hi - lo], F32, name=f"picked1_{lo}") for lo, hi in spans[:-1]]
         for j0 in range(0, J, 256):
             quantize_x(0, j0, 256, weave(picked0[:, :, j0 : j0 + 256], 256, "woven0"))
-        for i in range(PACK):
-            gather(picked1a[:, i, :], PACK + i, 0, FIRST)
-            gather(picked1b[:, i, :], PACK + i, FIRST, J)
+        for i in range(PACK - 1):
+            for tile, (lo, hi) in zip(picked1, spans):
+                gather(tile[:, i, :], PACK + i, lo, hi)
 
         y_sb = keep.tile([P, NT, J], F32, name="y_sb")
 
@@ -128,7 +129,15 @@ def tile_list_relu_scat_kernel(
         def first_layer(c):
             j0 = c * CH
             cols = slice(j0, j0 + CH)
-            src = picked1a[:, :, cols] if j0 < FIRST else picked1b[:, :, j0 - FIRST : j0 - FIRST + CH]
+            grp = max(g for g, (lo, hi) in enumerate(spans) if lo <= j0)
+            lo, hi = spans[grp]
+            if grp == len(spans) - 1:
+                picked1.append(keep.tile([P, PACK, hi - lo], F32, name="picked1_0"))
+                for i in range(PACK - 1):
+                    gather(picked1[grp][:, i, :], PACK + i, lo, hi)
+            if lo == j0:
+                gather(picked1[grp][:, PACK - 1, :], 2 * PACK - 1, lo, hi)
+            src = picked1[grp][:, :, j0 - lo : j0 - lo + CH]
             quantize_x(1, j0, CH, weave(src, CH, "woven1"))
             g_ps = psum.tile([P, R], F32, name="g_ps", tag=f"gy{c % BANKS}")
             u_ps = psum.tile([P, R], F32, name="u_ps", tag=f"u{c % BANKS}")

@@ -20,15 +20,24 @@ RELU = mybir.ActivationFunctionType.Relu
 P = 128
 PACK = 4
 PASSES = K // (P * PACK)
+PLANES = PASSES * PACK
 CH = 128
 CHUNKS = J // CH
-NT = N // P
+PAGES = N // P
 LANE = 16
-GROUPS = (0, 128, 384, 896, 1024)
+QUADRANT = 32
+SCALE_ROWS = 4
+RING = 4
+
 HEAD = 256
-EARLY = 2
-LAG = 2
+HALF = J // 2
 BANKS = 3
+LAG = 2
+CUTS = (0, CH, 2 * CH, 3 * CH, 5 * CH, 7 * CH)
+SPLIT = CUTS[-2]
+VECTOR_ZEROED = 2
+LOOP_PAGES = 2
+EXTRA_CHUNKS = CHUNKS - BANKS
 
 
 def tile_list_relu_scat_kernel(
@@ -37,53 +46,57 @@ def tile_list_relu_scat_kernel(
     nc = tc.nc
     with ExitStack() as ctx:
         keep = ctx.enter_context(tc.tile_pool(name="keep", bufs=1))
-        ring = ctx.enter_context(tc.tile_pool(name="ring", bufs=4))
+        ring = ctx.enter_context(tc.tile_pool(name="ring", bufs=RING))
         psum = ctx.enter_context(tc.psum_pool(name="psum", bufs=1))
 
         pick = keep.tile([P, J // LANE], U16, name="pick")
         place = keep.tile([P, J // LANE], U16, name="place")
-        x_rows = xT.rearrange("(a p i) t -> a i p t", p=P, i=PACK)
-        planes = [keep.tile([P, T], F32, name=f"plane{m}") for m in range(PASSES * PACK)]
+        x_rows = xT.rearrange("(a p t) n -> a t p n", p=P, t=PACK)
+        planes = [keep.tile([P, T], F32, name=f"plane{m}") for m in range(PLANES)]
         gain = keep.tile([P, J], F32, name="gain")
-        gain_out = keep.tile([P, J], F32, name="gain_out")
-        wg_w = [keep.tile([P, 2 * R], U8, name=f"wg_w{a}", align_bytes=64) for a in range(PASSES)]
-        wu_w = [keep.tile([P, 2 * R], U8, name=f"wu_w{a}", align_bytes=64) for a in range(PASSES)]
+        wg_w = keep.tile([P, PASSES * 2 * R], U8, name="wg_w", align_bytes=64)
+        wu_w = keep.tile([P, PASSES * 2 * R], U8, name="wu_w", align_bytes=64)
         wd_w = keep.tile([P, 2 * N], U8, name="wd_w", align_bytes=64)
         wg_s = keep.tile([P, PASSES * R], U8, name="wg_s", align_bytes=64)
         wu_s = keep.tile([P, PASSES * R], U8, name="wu_s", align_bytes=64)
         wd_s = keep.tile([P, N], U8, name="wd_s", align_bytes=64)
         ident = keep.tile([P, P], F32, name="ident")
-        pages = [keep.tile([P, T], F32, name=f"page{q}") for q in range(NT)]
+        pages = [keep.tile([P, T], F32, name=f"page{q}") for q in range(VECTOR_ZEROED)]
 
-        def load_scales(plane_s, dram_s, queue):
-            passes = dram_s.shape[0]
-            rows = dram_s.bitcast(I32).rearrange("a (q r) n -> q r a n", r=4)
-            for q in range(4):
-                queue.dma_start(
-                    plane_s[32 * q : 32 * q + 4, :].bitcast(I32).rearrange("p (a n) -> p a n", a=passes), rows[q]
-                )
+        def load_scales(scales, dram_scales):
+            passes = dram_scales.shape[0]
+            rows = dram_scales.bitcast(I32).rearrange("a (d r) n -> d r a n", r=SCALE_ROWS)
+            for d in range(P // QUADRANT):
+                live = scales[QUADRANT * d : QUADRANT * d + SCALE_ROWS, :]
+                nc.sync.dma_start(live.bitcast(I32).rearrange("p (a n) -> p a n", a=passes), rows[d])
 
-        for plane_s in (wg_s, wu_s, wd_s):
-            nc.vector.memset(plane_s[:].bitcast(I32), 0)
+        def load_words(words, dram_words):
+            nc.sync.dma_start(
+                words[:].bitcast(I32).rearrange("p (a n) -> p a n", a=dram_words.shape[0]),
+                dram_words.bitcast(I32).rearrange("a p n -> p a n"),
+            )
+
+        for scales in (wg_s, wu_s, wd_s):
+            nc.vector.memset(scales[:].bitcast(I32), 0)
         make_identity(nc, ident[:])
+
         nc.sync.dma_start(planes[0][:], x_rows[0, 0])
         nc.sync.dma_start(pick[:], offs)
         nc.sync.dma_start(gain[:, :HEAD], wgt[:, :HEAD])
         nc.sync.dma_start(gain[:, HEAD:], wgt[:, HEAD:])
-        for m in range(1, PASSES * PACK):
+        scales_behind_plane = {1: (wg_s, wg_scales), 2: (wu_s, wu_scales)}
+        for m in range(1, PLANES):
+            if m == PLANES - 1:
+                load_words(wg_w, wg_words)
             nc.sync.dma_start(planes[m][:], x_rows[m // PACK, m % PACK])
-        for a in range(PASSES):
-            nc.sync.dma_start(wg_w[a][:].bitcast(I32), wg_words[a].bitcast(I32))
-            nc.sync.dma_start(wu_w[a][:].bitcast(I32), wu_words[a].bitcast(I32))
-        nc.sync.dma_start(wd_w[:].bitcast(I32), wd_words[0].bitcast(I32))
-        load_scales(wd_s, wd_scales, nc.sync)
+            if m in scales_behind_plane:
+                load_scales(*scales_behind_plane[m])
+        load_words(wu_w, wu_words)
+        load_words(wd_w, wd_words)
+        load_scales(wd_s, wd_scales)
         nc.sync.dma_start(place[:], offs2)
-        nc.sync.dma_start(gain_out[:], wgo)
-
-        load_scales(wg_s, wg_scales, nc.gpsimd)
-        load_scales(wu_s, wu_scales, nc.gpsimd)
-        for q in range(NT):
-            nc.vector.memset(pages[q][:], 0.0)
+        for page in pages:
+            nc.vector.memset(page[:], 0.0)
 
         x_codes = [keep.tile([P, J], U32, name=f"x_codes{a}", align_bytes=64) for a in range(PASSES)]
         x_scales = [keep.tile([P, J], U8, name=f"x_scales{a}", align_bytes=64) for a in range(PASSES)]
@@ -91,33 +104,40 @@ def tile_list_relu_scat_kernel(
         def gather(dst, m, j0, j1):
             nc.vector.tensor_tensor(dst, planes[m][:].indirect(pick[:, j0 // LANE : j1 // LANE]), gain[:, j0:j1], MULT)
 
-        def weave(src, width, name):
-            woven = ring.tile([P, width * PACK], BF16, name=name, align_bytes=64)
+        def weave(src, woven):
             nc.scalar.copy(
-                woven[:].rearrange("p (c i t) -> p c t i", i=4, t=PACK),
+                woven.rearrange("p (c i t) -> p c t i", i=4, t=PACK),
                 src.rearrange("p t (c i) -> p c t i", i=4),
             )
             return woven
 
         def quantize_x(a, j0, width, woven):
             nc.vector.quantize_mx(
-                out=x_codes[a][:, j0 : j0 + width].bitcast(FP8X4), scales=x_scales[a][:, j0 : j0 + width], in_=woven[:]
+                out=x_codes[a][:, j0 : j0 + width].bitcast(FP8X4), scales=x_scales[a][:, j0 : j0 + width], in_=woven
             )
 
         picked0 = keep.tile([P, PACK, J], F32, name="picked0")
         gather(picked0[:, 0, :HEAD], 0, 0, HEAD)
         gather(picked0[:, 0, HEAD:], 0, HEAD, J)
-        for i in range(1, PACK):
-            gather(picked0[:, i, :], i, 0, J)
-        spans = list(zip(GROUPS[:-1], GROUPS[1:]))
-        picked1 = [keep.tile([P, PACK, hi - lo], F32, name=f"picked1_{lo}") for lo, hi in spans[:-1]]
-        for j0 in range(0, J, 256):
-            quantize_x(0, j0, 256, weave(picked0[:, :, j0 : j0 + 256], 256, "woven0"))
-        for i in range(PACK - 1):
-            for tile, (lo, hi) in zip(picked1, spans):
-                gather(tile[:, i, :], PACK + i, lo, hi)
+        for t in range(1, PACK - 1):
+            gather(picked0[:, t, :], t, 0, J)
+        for j0 in range(0, J, HALF):
+            gather(picked0[:, PACK - 1, j0 : j0 + HALF], PACK - 1, j0, j0 + HALF)
+        for q in range(VECTOR_ZEROED, PAGES):
+            pages.append(keep.tile([P, T], F32, name=f"plane{q - VECTOR_ZEROED}"))
+            nc.gpsimd.memset(pages[q][:], 0.0)
+        gain_out = keep.tile([P, J], F32, name="plane2")
+        nc.sync.dma_start(gain_out[:], wgo)
+        spans = ((0, SPLIT), (SPLIT, J - CH))
+        picked1 = [keep.tile([P, PACK, hi - lo], F32, name=f"picked1_{lo}", align_bytes=64) for lo, hi in spans]
+        for j0 in range(0, J, HALF):
+            woven0 = keep.tile([P, HALF * PACK], BF16, name=f"woven0_{j0}", align_bytes=64)
+            quantize_x(0, j0, HALF, weave(picked0[:, :, j0 : j0 + HALF], woven0[:]))
+        for t in range(PACK - 1):
+            for part_tile, (lo, hi) in zip(picked1, spans):
+                gather(part_tile[:, t, :], PACK + t, lo, hi)
 
-        y_sb = keep.tile([P, NT, J], F32, name="y_sb")
+        y_sb = keep.tile([P, PAGES, J], F32, name="y_sb")
 
         def scatter(q, j0, j1):
             nc.vector.tensor_tensor(
@@ -125,20 +145,28 @@ def tile_list_relu_scat_kernel(
             )
 
         h_quant = {}
+        sums = {}
 
         def first_layer(c):
             j0 = c * CH
             cols = slice(j0, j0 + CH)
-            grp = max(g for g, (lo, hi) in enumerate(spans) if lo <= j0)
-            lo, hi = spans[grp]
-            if grp == len(spans) - 1:
-                picked1.append(keep.tile([P, PACK, hi - lo], F32, name="picked1_0"))
-                for i in range(PACK - 1):
-                    gather(picked1[grp][:, i, :], PACK + i, lo, hi)
-            if lo == j0:
-                gather(picked1[grp][:, PACK - 1, :], 2 * PACK - 1, lo, hi)
-            src = picked1[grp][:, :, j0 - lo : j0 - lo + CH]
-            quantize_x(1, j0, CH, weave(src, CH, "woven1"))
+            part = int(j0 >= SPLIT)
+            lo = spans[part][0]
+            if c == CHUNKS - 1:
+                last = keep.tile([P, PACK, CH], F32, name="late", align_bytes=64)
+                for t in range(PACK):
+                    gather(last[:, t, :], PACK + t, j0, J)
+                src = last[:]
+            else:
+                if j0 in CUTS:
+                    hi = CUTS[CUTS.index(j0) + 1]
+                    gather(picked1[part][:, PACK - 1, j0 - lo : hi - lo], PLANES - 1, j0, hi)
+                src = picked1[part][:, :, j0 - lo : j0 - lo + CH]
+            if c == BANKS - 1:
+                woven = picked1[1][:, PACK - 1, : CH * PACK // 2].bitcast(BF16)
+            else:
+                woven = keep.tile([P, CH * PACK], BF16, name=f"slot{c % BANKS}", align_bytes=64)[:]
+            quantize_x(1, j0, CH, weave(src, woven))
             g_ps = psum.tile([P, R], F32, name="g_ps", tag=f"gy{c % BANKS}")
             u_ps = psum.tile([P, R], F32, name="u_ps", tag=f"u{c % BANKS}")
             for a in range(PASSES):
@@ -147,12 +175,16 @@ def tile_list_relu_scat_kernel(
                         acc[:],
                         lhsT=x_codes[a][:, cols].bitcast(FP8X4),
                         lhsT_scale=x_scales[a][:, cols],
-                        rhs=words[a][:].bitcast(FP4X4),
+                        rhs=words[:, a * 2 * R : (a + 1) * 2 * R].bitcast(FP4X4),
                         rhs_scale=scales[:, a * R : (a + 1) * R],
                         start=(a == 0),
                         stop=(a == PASSES - 1),
                     )
-            gate = ring.tile([P, R], F32, name="gate")
+            sums[c] = (g_ps, u_ps)
+
+        def gated(c):
+            g_ps, u_ps = sums[c]
+            gate = keep.tile([P, R], F32, name=f"slot{c % BANKS}", align_bytes=64)
             nc.scalar.activation(
                 gate[:].rearrange("p (u m e) -> p u m e", u=2, e=2),
                 g_ps[:].rearrange("p (m u e) -> p u m e", u=2, e=2),
@@ -172,7 +204,10 @@ def tile_list_relu_scat_kernel(
             t_ps = psum.tile([P, 2, CH], F32, name="t_ps", tag=f"t{c % 2}")
             for u in range(2):
                 nc.tensor.transpose(t_ps[:, u, :], pairs[:, u * P : (u + 1) * P], ident[:])
-            h_woven = ring.tile([P, CH * PACK], BF16, name="h_woven", align_bytes=64)
+            if c == 0:
+                h_woven = keep.tile([P, CH * PACK], BF16, name="late", align_bytes=64)
+            else:
+                h_woven = ring.tile([P, CH * PACK], BF16, name="h_woven", align_bytes=64)
             nc.scalar.copy(
                 h_woven[:].bitcast(F32).rearrange("p (j u) -> p j u", u=2), t_ps[:].rearrange("p u j -> p j u")
             )
@@ -184,8 +219,8 @@ def tile_list_relu_scat_kernel(
         def second_layer(c):
             h_codes, h_scales = h_quant[c]
             cols = slice(c * CH, (c + 1) * CH)
-            y_ps = psum.tile([P, NT, CH], F32, name="y_ps", tag=f"gy{(c + LAG) % BANKS}")
-            for q in range(NT):
+            y_ps = psum.tile([P, PAGES, CH], F32, name="y_ps", tag=f"gy{(c + LAG) % BANKS}")
+            for q in range(PAGES):
                 nc.tensor.matmul_mx(
                     y_ps[:, q, :],
                     lhsT=wd_w[:, 2 * P * q : 2 * P * (q + 1)].bitcast(FP4X4),
@@ -196,16 +231,20 @@ def tile_list_relu_scat_kernel(
                     stop=True,
                 )
             nc.scalar.copy(y_sb[:, :, cols], y_ps[:])
-            for q in range(EARLY):
+            for q in range(LOOP_PAGES + (c < EXTRA_CHUNKS)):
                 scatter(q, c * CH, (c + 1) * CH)
 
+        for c in range(BANKS):
+            first_layer(c)
         for c in range(CHUNKS + LAG):
-            h_rows = first_layer(c) if c < CHUNKS else None
+            h_rows = gated(c) if c < CHUNKS else None
             if c >= LAG:
                 second_layer(c - LAG)
             if c < CHUNKS:
                 turn_h(c, h_rows)
-        for q in range(NT):
-            if q >= EARLY:
-                scatter(q, 0, J)
+            if c + BANKS < CHUNKS:
+                first_layer(c + BANKS)
+        for q in range(PAGES):
+            if q >= LOOP_PAGES:
+                scatter(q, EXTRA_CHUNKS * CH if q == LOOP_PAGES else 0, J)
             nc.sync.dma_start(out[q * P : (q + 1) * P, :], pages[q][:])

@@ -138,11 +138,10 @@ def tile_list_relu_scat_kernel(
                 gather(part_tile[:, t, :], PACK + t, lo, hi)
 
         y_sb = keep.tile([P, PAGES, J], F32, name="y_sb")
+        y_w = keep.tile([P, PAGES, J], F32, name="y_w")
 
         def scatter(q, j0, j1):
-            nc.vector.tensor_tensor(
-                pages[q][:].indirect(place[:, j0 // LANE : j1 // LANE]), y_sb[:, q, j0:j1], gain_out[:, j0:j1], MULT
-            )
+            nc.vector.tensor_copy(pages[q][:].indirect(place[:, j0 // LANE : j1 // LANE]), y_w[:, q, j0:j1])
 
         h_quant = {}
         sums = {}
@@ -231,6 +230,13 @@ def tile_list_relu_scat_kernel(
                     stop=True,
                 )
             nc.scalar.copy(y_sb[:, :, cols], y_ps[:])
+            for q0 in range(0, PAGES, LOOP_PAGES):
+                nc.gpsimd.tensor_tensor(
+                    y_w[:, q0 : q0 + LOOP_PAGES, cols],
+                    y_sb[:, q0 : q0 + LOOP_PAGES, cols],
+                    gain_out[:, cols].unsqueeze(1).to_broadcast([P, LOOP_PAGES, CH]),
+                    MULT,
+                )
             for q in range(LOOP_PAGES + (c < EXTRA_CHUNKS)):
                 scatter(q, c * CH, (c + 1) * CH)
 

@@ -33,11 +33,20 @@ HEAD = 256
 HALF = J // 2
 BANKS = 3
 LAG = 2
-CUTS = (0, CH, 2 * CH, 3 * CH, 5 * CH, 7 * CH)
-SPLIT = CUTS[-2]
-VECTOR_ZEROED = 2
-LOOP_PAGES = 2
-EXTRA_CHUNKS = CHUNKS - BANKS
+CUTS = (0, CH, 2 * CH, 4 * CH, 8 * CH)
+GROUPS = ((0, 1), (1, 2), (2, 3), (3, 4), (4, 6), (6, 8))
+VECTOR_PRODUCTS = 8
+STEPS = (
+    ((0, 0), (1, 0), (2, 0)),
+    ((2, 1), (3, 0)),
+    ((0, 1), (1, 1)),
+    ((0, 3), (3, 2)),
+    ((2, 2),),
+    ((1, 3),),
+    ((0, 4),),
+    ((0, 7), (1, 6), (2, 5), (3, 4)),
+)
+FUSED_FROM = 0
 
 
 def tile_list_relu_scat_kernel(
@@ -54,14 +63,13 @@ def tile_list_relu_scat_kernel(
         x_rows = xT.rearrange("(a p t) n -> a t p n", p=P, t=PACK)
         planes = [keep.tile([P, T], F32, name=f"plane{m}") for m in range(PLANES)]
         gain = keep.tile([P, J], F32, name="gain")
-        wg_w = keep.tile([P, PASSES * 2 * R], U8, name="wg_w", align_bytes=64)
-        wu_w = keep.tile([P, PASSES * 2 * R], U8, name="wu_w", align_bytes=64)
+        wg_w = [keep.tile([P, 2 * R], U8, name=f"wg_w{a}", align_bytes=64) for a in range(PASSES)]
+        wu_w = [keep.tile([P, 2 * R], U8, name=f"wu_w{a}", align_bytes=64) for a in range(PASSES)]
         wd_w = keep.tile([P, 2 * N], U8, name="wd_w", align_bytes=64)
         wg_s = keep.tile([P, PASSES * R], U8, name="wg_s", align_bytes=64)
         wu_s = keep.tile([P, PASSES * R], U8, name="wu_s", align_bytes=64)
         wd_s = keep.tile([P, N], U8, name="wd_s", align_bytes=64)
         ident = keep.tile([P, P], F32, name="ident")
-        pages = [keep.tile([P, T], F32, name=f"page{q}") for q in range(VECTOR_ZEROED)]
 
         def load_scales(scales, dram_scales):
             passes = dram_scales.shape[0]
@@ -71,32 +79,50 @@ def tile_list_relu_scat_kernel(
                 nc.sync.dma_start(live.bitcast(I32).rearrange("p (a n) -> p a n", a=passes), rows[d])
 
         def load_words(words, dram_words):
-            nc.sync.dma_start(
-                words[:].bitcast(I32).rearrange("p (a n) -> p a n", a=dram_words.shape[0]),
-                dram_words.bitcast(I32).rearrange("a p n -> p a n"),
-            )
+            nc.sync.dma_start(words[:].bitcast(I32), dram_words.bitcast(I32))
 
         for scales in (wg_s, wu_s, wd_s):
             nc.vector.memset(scales[:].bitcast(I32), 0)
         make_identity(nc, ident[:])
 
+        rows = keep.tile([P, CH], F32, name="rows")
+        for w, weights in enumerate((wgt, wgo)):
+            nc.sync.dma_start(
+                rows[w * P // 2 : (w + 1) * P // 2, :], weights.rearrange("(g r) (i e) -> r g i e", r=LANE, e=CH)[0]
+            )
         nc.sync.dma_start(planes[0][:], x_rows[0, 0])
         nc.sync.dma_start(pick[:], offs)
-        nc.sync.dma_start(gain[:, :HEAD], wgt[:, :HEAD])
-        nc.sync.dma_start(gain[:, HEAD:], wgt[:, HEAD:])
         scales_behind_plane = {1: (wg_s, wg_scales), 2: (wu_s, wu_scales)}
         for m in range(1, PLANES):
-            if m == PLANES - 1:
-                load_words(wg_w, wg_words)
             nc.sync.dma_start(planes[m][:], x_rows[m // PACK, m % PACK])
             if m in scales_behind_plane:
                 load_scales(*scales_behind_plane[m])
-        load_words(wu_w, wu_words)
-        load_words(wd_w, wd_words)
-        load_scales(wd_s, wd_scales)
+            if m >= PLANES - PASSES:
+                a = m - (PLANES - PASSES)
+                load_words(wg_w[a], wg_words[a])
+                load_words(wu_w[a], wu_words[a])
         nc.sync.dma_start(place[:], offs2)
-        for page in pages:
-            nc.vector.memset(page[:], 0.0)
+        load_words(wd_w, wd_words[0])
+        load_scales(wd_s, wd_scales)
+
+        turned = psum.tile([P, P], F32, name="turned", tag="t0")
+        nc.tensor.transpose(turned[:], rows[:], ident[:])
+
+        def spread(w, dst, repeat, cuts, banks):
+            groups = turned[:, w * P // 2 : (w + 1) * P // 2].rearrange("p (g i) -> p i g", i=CHUNKS)
+            for i0, i1, bank in zip(cuts, cuts[1:], banks):
+                step = i1 - i0
+                wide = keep.tile([P, step, P], F32, name=f"wide{i0}")
+                back = psum.tile([P, step, CH], F32, name="back", tag=bank)
+                repeat(
+                    wide[:].rearrange("p i (g r) -> p i g r", r=LANE),
+                    groups[:, i0 : i0 + step, :].unsqueeze(3).to_broadcast([P, step, P // LANE, LANE]),
+                )
+                for i in range(step):
+                    nc.tensor.transpose(back[:, i, :], wide[:, i, :], ident[:])
+                nc.scalar.copy(dst[:, i0 * CH : (i0 + step) * CH], back[:].rearrange("p i e -> p (i e)"))
+
+        spread(0, gain, nc.vector.tensor_copy, (0, 1, 2, 4, 6, 8), ("u0", "u1", "u2", "t1", "g2"))
 
         x_codes = [keep.tile([P, J], U32, name=f"x_codes{a}", align_bytes=64) for a in range(PASSES)]
         x_scales = [keep.tile([P, J], U8, name=f"x_scales{a}", align_bytes=64) for a in range(PASSES)]
@@ -117,69 +143,77 @@ def tile_list_relu_scat_kernel(
             )
 
         picked0 = keep.tile([P, PACK, J], F32, name="picked0")
-        gather(picked0[:, 0, :HEAD], 0, 0, HEAD)
-        gather(picked0[:, 0, HEAD:], 0, HEAD, J)
+        for j0, j1 in zip(CUTS, CUTS[1:]):
+            gather(picked0[:, 0, j0:j1], 0, j0, j1)
         for t in range(1, PACK - 1):
             gather(picked0[:, t, :], t, 0, J)
         for j0 in range(0, J, HALF):
             gather(picked0[:, PACK - 1, j0 : j0 + HALF], PACK - 1, j0, j0 + HALF)
-        for q in range(VECTOR_ZEROED, PAGES):
-            pages.append(keep.tile([P, T], F32, name=f"plane{q - VECTOR_ZEROED}"))
-            nc.gpsimd.memset(pages[q][:], 0.0)
-        gain_out = keep.tile([P, J], F32, name="plane2")
-        nc.sync.dma_start(gain_out[:], wgo)
-        spans = ((0, SPLIT), (SPLIT, J - CH))
-        picked1 = [keep.tile([P, PACK, hi - lo], F32, name=f"picked1_{lo}", align_bytes=64) for lo, hi in spans]
+        pages = [keep.tile([P, T], F32, name=f"plane{q}") for q in range(PAGES)]
+        for page in pages:
+            nc.gpsimd.memset(page[:], 0.0)
+        gain_out = keep.tile([P, J], F32, name="gain_out")
+        spread(1, gain_out, nc.scalar.copy, (0, 4, 8), ("g0", "g1"))
+        picked1 = [keep.tile([P, PACK, HALF], F32, name=f"picked1_{half}", align_bytes=64) for half in range(2)]
         for j0 in range(0, J, HALF):
             woven0 = keep.tile([P, HALF * PACK], BF16, name=f"woven0_{j0}", align_bytes=64)
             quantize_x(0, j0, HALF, weave(picked0[:, :, j0 : j0 + HALF], woven0[:]))
         for t in range(PACK - 1):
-            for part_tile, (lo, hi) in zip(picked1, spans):
-                gather(part_tile[:, t, :], PACK + t, lo, hi)
+            for half in range(2):
+                if (t, half) != (PACK - 2, 1):
+                    gather(picked1[half][:, t, :], PACK + t, half * HALF, (half + 1) * HALF)
+
+        def borrowed(t):
+            return picked1[1][:, t, : CH * PACK // 2].bitcast(BF16)
+
+        def pass1(first, end):
+            if first == 0:
+                woven = borrowed(PACK - 1)
+            else:
+                woven = keep.tile([P, (end - first) * CH * PACK], BF16, name=f"shared{first}", align_bytes=64)[:]
+            for c in range(first, end):
+                half, lo = divmod(c * CH, HALF)
+                weave(picked1[half][:, :, lo : lo + CH], woven[:, (c - first) * CH * PACK : (c - first + 1) * CH * PACK])
+            quantize_x(1, first * CH, (end - first) * CH, woven)
+
+        def last_plane(piece):
+            j0, j1 = CUTS[piece], CUTS[piece + 1]
+            half, lo = divmod(j0, HALF)
+            gather(picked1[half][:, PACK - 1, lo : lo + j1 - j0], PLANES - 1, j0, j1)
 
         y_sb = keep.tile([P, PAGES, J], F32, name="y_sb")
         y_w = keep.tile([P, PAGES, J], F32, name="y_w")
 
-        def scatter(q, j0, j1):
-            nc.vector.tensor_copy(pages[q][:].indirect(place[:, j0 // LANE : j1 // LANE]), y_w[:, q, j0:j1])
+        def scatter(q, j0, j1, fused):
+            window = pages[q][:].indirect(place[:, j0 // LANE : j1 // LANE])
+            if fused:
+                nc.vector.tensor_tensor(window, y_sb[:, q, j0:j1], gain_out[:, j0:j1], MULT)
+            else:
+                nc.vector.tensor_copy(window, y_w[:, q, j0:j1])
+
+        weighed = [(q, c) for end in range(FUSED_FROM) for q, first in STEPS[end] for c in range(first, end + 1)]
 
         h_quant = {}
         sums = {}
 
-        def first_layer(c):
-            j0 = c * CH
-            cols = slice(j0, j0 + CH)
-            part = int(j0 >= SPLIT)
-            lo = spans[part][0]
-            if c == CHUNKS - 1:
-                last = keep.tile([P, PACK, CH], F32, name="late", align_bytes=64)
-                for t in range(PACK):
-                    gather(last[:, t, :], PACK + t, j0, J)
-                src = last[:]
-            else:
-                if j0 in CUTS:
-                    hi = CUTS[CUTS.index(j0) + 1]
-                    gather(picked1[part][:, PACK - 1, j0 - lo : hi - lo], PLANES - 1, j0, hi)
-                src = picked1[part][:, :, j0 - lo : j0 - lo + CH]
-            if c == BANKS - 1:
-                woven = picked1[1][:, PACK - 1, : CH * PACK // 2].bitcast(BF16)
-            else:
-                woven = keep.tile([P, CH * PACK], BF16, name=f"slot{c % BANKS}", align_bytes=64)[:]
-            quantize_x(1, j0, CH, weave(src, woven))
-            g_ps = psum.tile([P, R], F32, name="g_ps", tag=f"gy{c % BANKS}")
-            u_ps = psum.tile([P, R], F32, name="u_ps", tag=f"u{c % BANKS}")
-            for a in range(PASSES):
-                for acc, words, scales in ((g_ps, wg_w, wg_s), (u_ps, wu_w, wu_s)):
-                    nc.tensor.matmul_mx(
-                        acc[:],
-                        lhsT=x_codes[a][:, cols].bitcast(FP8X4),
-                        lhsT_scale=x_scales[a][:, cols],
-                        rhs=words[:, a * 2 * R : (a + 1) * 2 * R].bitcast(FP4X4),
-                        rhs_scale=scales[:, a * R : (a + 1) * R],
-                        start=(a == 0),
-                        stop=(a == PASSES - 1),
-                    )
-            sums[c] = (g_ps, u_ps)
+        def first_layer(chunks, passes=range(PASSES)):
+            for c in chunks if 0 in passes else ():
+                g_ps = psum.tile([P, R], F32, name="g_ps", tag=f"g{c % BANKS}")
+                u_ps = psum.tile([P, R], F32, name="u_ps", tag=f"u{c % BANKS}")
+                sums[c] = (g_ps, u_ps)
+            for a in passes:
+                for c in chunks:
+                    cols = slice(c * CH, (c + 1) * CH)
+                    for acc, words, scales in zip(sums[c], (wg_w, wu_w), (wg_s, wu_s)):
+                        nc.tensor.matmul_mx(
+                            acc[:],
+                            lhsT=x_codes[a][:, cols].bitcast(FP8X4),
+                            lhsT_scale=x_scales[a][:, cols],
+                            rhs=words[a][:].bitcast(FP4X4),
+                            rhs_scale=scales[:, a * R : (a + 1) * R],
+                            start=(a == 0),
+                            stop=(a == PASSES - 1),
+                        )
 
         def gated(c):
             g_ps, u_ps = sums[c]
@@ -190,12 +224,22 @@ def tile_list_relu_scat_kernel(
                 RELU,
             )
             h_rows = ring.tile([P, R], BF16, name="h_rows")
-            nc.vector.tensor_tensor(
-                h_rows[:].rearrange("p (u m e) -> p u m e", u=2, e=2),
-                u_ps[:].rearrange("p (m u e) -> p u m e", u=2, e=2),
-                gate[:].rearrange("p (u m e) -> p u m e", u=2, e=2),
-                MULT,
-            )
+            if c < VECTOR_PRODUCTS:
+                nc.vector.tensor_tensor(
+                    h_rows[:].rearrange("p (u m e) -> p u m e", u=2, e=2),
+                    u_ps[:].rearrange("p (m u e) -> p u m e", u=2, e=2),
+                    gate[:].rearrange("p (u m e) -> p u m e", u=2, e=2),
+                    MULT,
+                )
+            else:
+                up = ring.tile([P, R], F32, name="up")
+                nc.scalar.copy(
+                    up[:].rearrange("p (u m e) -> p u m e", u=2, e=2),
+                    u_ps[:].rearrange("p (m u e) -> p u m e", u=2, e=2),
+                )
+                for u in range(2):
+                    half = slice(u * R // 2, (u + 1) * R // 2)
+                    nc.gpsimd.tensor_tensor(h_rows[:, half], up[:, half], gate[:, half], MULT)
             return h_rows
 
         def turn_h(c, h_rows):
@@ -204,21 +248,26 @@ def tile_list_relu_scat_kernel(
             for u in range(2):
                 nc.tensor.transpose(t_ps[:, u, :], pairs[:, u * P : (u + 1) * P], ident[:])
             if c == 0:
-                h_woven = keep.tile([P, CH * PACK], BF16, name="late", align_bytes=64)
+                h_woven = borrowed(PACK - 2)
             else:
-                h_woven = ring.tile([P, CH * PACK], BF16, name="h_woven", align_bytes=64)
+                h_woven = ring.tile([P, CH * PACK], BF16, name="h_woven", align_bytes=64)[:]
             nc.scalar.copy(
-                h_woven[:].bitcast(F32).rearrange("p (j u) -> p j u", u=2), t_ps[:].rearrange("p u j -> p j u")
+                h_woven.bitcast(F32).rearrange("p (j u) -> p j u", u=2), t_ps[:].rearrange("p u j -> p j u")
             )
-            h_codes = ring.tile([P, CH], U32, name="h_codes", align_bytes=64)
+            if c < 2:
+                h_codes = keep.tile([P, CH], U32, name=f"shared{GROUPS[4 + c][0]}", align_bytes=64)
+            else:
+                h_codes = ring.tile([P, CH], U32, name="h_codes", align_bytes=64)
             h_scales = ring.tile([P, CH], U8, name="h_scales", align_bytes=64)
-            nc.vector.quantize_mx(out=h_codes[:].bitcast(FP8X4), scales=h_scales[:], in_=h_woven[:])
+            nc.vector.quantize_mx(out=h_codes[:].bitcast(FP8X4), scales=h_scales[:], in_=h_woven)
             h_quant[c] = (h_codes, h_scales)
+            if c == 0:
+                gather(picked1[1][:, PACK - 2, :], PLANES - 2, HALF, J)
 
         def second_layer(c):
             h_codes, h_scales = h_quant[c]
             cols = slice(c * CH, (c + 1) * CH)
-            y_ps = psum.tile([P, PAGES, CH], F32, name="y_ps", tag=f"gy{(c + LAG) % BANKS}")
+            y_ps = psum.tile([P, PAGES, CH], F32, name="y_ps", tag=f"t{(c + 1) % 2}")
             for q in range(PAGES):
                 nc.tensor.matmul_mx(
                     y_ps[:, q, :],
@@ -229,28 +278,30 @@ def tile_list_relu_scat_kernel(
                     start=True,
                     stop=True,
                 )
-            nc.scalar.copy(y_sb[:, :, cols], y_ps[:])
-            for q0 in range(0, PAGES, LOOP_PAGES):
-                nc.gpsimd.tensor_tensor(
-                    y_w[:, q0 : q0 + LOOP_PAGES, cols],
-                    y_sb[:, q0 : q0 + LOOP_PAGES, cols],
-                    gain_out[:, cols].unsqueeze(1).to_broadcast([P, LOOP_PAGES, CH]),
-                    MULT,
-                )
-            for q in range(LOOP_PAGES + (c < EXTRA_CHUNKS)):
-                scatter(q, c * CH, (c + 1) * CH)
+            for q0, q1 in ((0, 1), (1, PAGES)) if c == 0 else ((0, PAGES),):
+                nc.scalar.copy(y_sb[:, q0:q1, cols], y_ps[:, q0:q1, :])
+            for q in [q for q, chunk in weighed if chunk == c]:
+                nc.gpsimd.tensor_tensor(y_w[:, q, cols], y_sb[:, q, cols], gain_out[:, cols], MULT)
+            for q, first in STEPS[c]:
+                scatter(q, first * CH, (c + 1) * CH, c >= FUSED_FROM)
+                if c == CHUNKS - 1:
+                    nc.sync.dma_start(out[q * P : (q + 1) * P, :], pages[q][:])
 
-        for c in range(BANKS):
-            first_layer(c)
-        for c in range(CHUNKS + LAG):
-            h_rows = gated(c) if c < CHUNKS else None
-            if c >= LAG:
-                second_layer(c - LAG)
+        for piece in range(3):
+            last_plane(piece)
+        pass1(*GROUPS[0])
+        last_plane(3)
+        for group in GROUPS[1:3]:
+            pass1(*group)
+        first_layer(range(BANKS), (0,))
+        first_layer((0, 1), (1,))
+        for c in range(CHUNKS + 1):
             if c < CHUNKS:
-                turn_h(c, h_rows)
-            if c + BANKS < CHUNKS:
-                first_layer(c + BANKS)
-        for q in range(PAGES):
-            if q >= LOOP_PAGES:
-                scatter(q, EXTRA_CHUNKS * CH if q == LOOP_PAGES else 0, J)
-            nc.sync.dma_start(out[q * P : (q + 1) * P, :], pages[q][:])
+                turn_h(c, gated(c))
+            if c >= 1:
+                second_layer(c - 1)
+            if c < 3:
+                pass1(*GROUPS[c + 3])
+            for d in {0: (2, 3), 1: (), 2: (4, 5)}.get(c, (c + BANKS,)):
+                if d < CHUNKS:
+                    first_layer((d,), range(int(d < BANKS), PASSES))

@@ -92,6 +92,7 @@ def tile_list_relu_scat_kernel(
             )
         nc.sync.dma_start(planes[0][:], x_rows[0, 0])
         nc.sync.dma_start(pick[:], offs)
+        nc.sync.dma_start(gain[:, :HEAD], wgt[:, :HEAD])
         scales_behind_plane = {1: (wg_s, wg_scales), 2: (wu_s, wu_scales)}
         for m in range(1, PLANES):
             nc.sync.dma_start(planes[m][:], x_rows[m // PACK, m % PACK])
@@ -108,13 +109,13 @@ def tile_list_relu_scat_kernel(
         turned = psum.tile([P, P], F32, name="turned", tag="t0")
         nc.tensor.transpose(turned[:], rows[:], ident[:])
 
-        def spread(w, dst, repeat, cuts, banks):
+        def spread(w, dst, cuts, banks):
             groups = turned[:, w * P // 2 : (w + 1) * P // 2].rearrange("p (g i) -> p i g", i=CHUNKS)
             for i0, i1, bank in zip(cuts, cuts[1:], banks):
                 step = i1 - i0
                 wide = keep.tile([P, step, P], F32, name=f"wide{i0}")
                 back = psum.tile([P, step, CH], F32, name="back", tag=bank)
-                repeat(
+                nc.scalar.copy(
                     wide[:].rearrange("p i (g r) -> p i g r", r=LANE),
                     groups[:, i0 : i0 + step, :].unsqueeze(3).to_broadcast([P, step, P // LANE, LANE]),
                 )
@@ -122,7 +123,7 @@ def tile_list_relu_scat_kernel(
                     nc.tensor.transpose(back[:, i, :], wide[:, i, :], ident[:])
                 nc.scalar.copy(dst[:, i0 * CH : (i0 + step) * CH], back[:].rearrange("p i e -> p (i e)"))
 
-        spread(0, gain, nc.vector.tensor_copy, (0, 1, 2, 4, 6, 8), ("u0", "u1", "u2", "t1", "g2"))
+        spread(0, gain, (2, 4, 6, 8), ("u0", "u1", "u2"))
 
         x_codes = [keep.tile([P, J], U32, name=f"x_codes{a}", align_bytes=64) for a in range(PASSES)]
         x_scales = [keep.tile([P, J], U8, name=f"x_scales{a}", align_bytes=64) for a in range(PASSES)]
@@ -143,7 +144,7 @@ def tile_list_relu_scat_kernel(
             )
 
         picked0 = keep.tile([P, PACK, J], F32, name="picked0")
-        for j0, j1 in zip(CUTS, CUTS[1:]):
+        for j0, j1 in ((0, HEAD), (HEAD, J)):
             gather(picked0[:, 0, j0:j1], 0, j0, j1)
         for t in range(1, PACK - 1):
             gather(picked0[:, t, :], t, 0, J)
@@ -153,14 +154,14 @@ def tile_list_relu_scat_kernel(
         for page in pages:
             nc.gpsimd.memset(page[:], 0.0)
         gain_out = keep.tile([P, J], F32, name="gain_out")
-        spread(1, gain_out, nc.scalar.copy, (0, 4, 8), ("g0", "g1"))
+        spread(1, gain_out, (0, 4, 8), ("g0", "g1"))
         picked1 = [keep.tile([P, PACK, HALF], F32, name=f"picked1_{half}", align_bytes=64) for half in range(2)]
         for j0 in range(0, J, HALF):
             woven0 = keep.tile([P, HALF * PACK], BF16, name=f"woven0_{j0}", align_bytes=64)
             quantize_x(0, j0, HALF, weave(picked0[:, :, j0 : j0 + HALF], woven0[:]))
         for t in range(PACK - 1):
             for half in range(2):
-                if (t, half) != (PACK - 2, 1):
+                if t == 0 or half == 0:
                     gather(picked1[half][:, t, :], PACK + t, half * HALF, (half + 1) * HALF)
 
         def borrowed(t):
@@ -217,9 +218,12 @@ def tile_list_relu_scat_kernel(
 
         def gated(c):
             g_ps, u_ps = sums[c]
-            gate = keep.tile([P, R], F32, name=f"slot{c % BANKS}", align_bytes=64)
+            if c == 0:
+                gate = picked1[1][:, 1, :]
+            else:
+                gate = keep.tile([P, R], F32, name=f"slot{c % BANKS}", align_bytes=64)[:]
             nc.scalar.activation(
-                gate[:].rearrange("p (u m e) -> p u m e", u=2, e=2),
+                gate.rearrange("p (u m e) -> p u m e", u=2, e=2),
                 g_ps[:].rearrange("p (m u e) -> p u m e", u=2, e=2),
                 RELU,
             )
@@ -228,7 +232,7 @@ def tile_list_relu_scat_kernel(
                 nc.vector.tensor_tensor(
                     h_rows[:].rearrange("p (u m e) -> p u m e", u=2, e=2),
                     u_ps[:].rearrange("p (m u e) -> p u m e", u=2, e=2),
-                    gate[:].rearrange("p (u m e) -> p u m e", u=2, e=2),
+                    gate.rearrange("p (u m e) -> p u m e", u=2, e=2),
                     MULT,
                 )
             else:
@@ -240,6 +244,8 @@ def tile_list_relu_scat_kernel(
                 for u in range(2):
                     half = slice(u * R // 2, (u + 1) * R // 2)
                     nc.gpsimd.tensor_tensor(h_rows[:, half], up[:, half], gate[:, half], MULT)
+            if c == 0:
+                gather(picked1[1][:, 1, :], PACK + 1, HALF, J)
             return h_rows
 
         def turn_h(c, h_rows):

@@ -35,18 +35,7 @@ BANKS = 3
 LAG = 2
 CUTS = (0, CH, 2 * CH, 4 * CH, 8 * CH)
 GROUPS = ((0, 1), (1, 2), (2, 3), (3, 4), (4, 6), (6, 8))
-VECTOR_PRODUCTS = 8
-STEPS = (
-    ((0, 0), (1, 0), (2, 0)),
-    ((2, 1), (3, 0)),
-    ((0, 1), (1, 1)),
-    ((0, 3), (3, 2)),
-    ((2, 2),),
-    ((1, 3),),
-    ((0, 4),),
-    ((0, 7), (1, 6), (2, 5), (3, 4)),
-)
-FUSED_FROM = 0
+VECTOR_PRODUCTS = 6
 
 
 def tile_list_relu_scat_kernel(
@@ -155,6 +144,8 @@ def tile_list_relu_scat_kernel(
             nc.gpsimd.memset(page[:], 0.0)
         gain_out = keep.tile([P, J], F32, name="gain_out")
         spread(1, gain_out, (0, 4, 8), ("g0", "g1"))
+        front_gain = keep.tile([P, CH], F32, name="first_window", align_bytes=64)
+        nc.scalar.copy(front_gain[:], gain_out[:, 3 * CH : 4 * CH])
         picked1 = [keep.tile([P, PACK, HALF], F32, name=f"picked1_{half}", align_bytes=64) for half in range(2)]
         for j0 in range(0, J, HALF):
             woven0 = keep.tile([P, HALF * PACK], BF16, name=f"woven0_{j0}", align_bytes=64)
@@ -183,16 +174,24 @@ def tile_list_relu_scat_kernel(
             gather(picked1[half][:, PACK - 1, lo : lo + j1 - j0], PLANES - 1, j0, j1)
 
         y_sb = keep.tile([P, PAGES, J], F32, name="y_sb")
-        y_w = keep.tile([P, PAGES, J], F32, name="y_w")
 
-        def scatter(q, j0, j1, fused):
-            window = pages[q][:].indirect(place[:, j0 // LANE : j1 // LANE])
-            if fused:
-                nc.vector.tensor_tensor(window, y_sb[:, q, j0:j1], gain_out[:, j0:j1], MULT)
-            else:
-                nc.vector.tensor_copy(window, y_w[:, q, j0:j1])
+        def window(q, first, end):
+            return pages[q][:].indirect(place[:, first * CH // LANE : end * CH // LANE])
 
-        weighed = [(q, c) for end in range(FUSED_FROM) for q, first in STEPS[end] for c in range(first, end + 1)]
+        def scatter(q, first, end, y=None, weights=None):
+            cols = slice(first * CH, end * CH)
+            if y is None:
+                y, weights = y_sb[:, q, cols], gain_out[:, cols]
+            nc.vector.tensor_tensor(window(q, first, end), y, weights, MULT)
+
+        def weigh(dst, q0, q1, first, end):
+            cols = slice(first * CH, end * CH)
+            nc.gpsimd.tensor_tensor(
+                dst.rearrange("p (q j) -> p q j", q=q1 - q0),
+                y_sb[:, q0:q1, cols],
+                gain_out[:, cols].unsqueeze(1).to_broadcast([P, q1 - q0, (end - first) * CH]),
+                MULT,
+            )
 
         h_quant = {}
         sums = {}
@@ -216,82 +215,79 @@ def tile_list_relu_scat_kernel(
                             stop=(a == PASSES - 1),
                         )
 
-        def gated(c):
-            g_ps, u_ps = sums[c]
+        def paired(ap):
+            return ap.rearrange("p (u m e) -> p u m e", u=2, e=2)
+
+        def unpaired(bank):
+            return bank[:].rearrange("p (m u e) -> p u m e", u=2, e=2)
+
+        def relu(c):
             if c == 0:
                 gate = picked1[1][:, 1, :]
             else:
                 gate = keep.tile([P, R], F32, name=f"slot{c % BANKS}", align_bytes=64)[:]
-            nc.scalar.activation(
-                gate.rearrange("p (u m e) -> p u m e", u=2, e=2),
-                g_ps[:].rearrange("p (m u e) -> p u m e", u=2, e=2),
-                RELU,
-            )
-            h_rows = ring.tile([P, R], BF16, name="h_rows")
-            if c < VECTOR_PRODUCTS:
-                nc.vector.tensor_tensor(
-                    h_rows[:].rearrange("p (u m e) -> p u m e", u=2, e=2),
-                    u_ps[:].rearrange("p (m u e) -> p u m e", u=2, e=2),
-                    gate.rearrange("p (u m e) -> p u m e", u=2, e=2),
-                    MULT,
-                )
-            else:
-                up = ring.tile([P, R], F32, name="up")
-                nc.scalar.copy(
-                    up[:].rearrange("p (u m e) -> p u m e", u=2, e=2),
-                    u_ps[:].rearrange("p (m u e) -> p u m e", u=2, e=2),
-                )
-                for u in range(2):
-                    half = slice(u * R // 2, (u + 1) * R // 2)
-                    nc.gpsimd.tensor_tensor(h_rows[:, half], up[:, half], gate[:, half], MULT)
+            nc.scalar.activation(paired(gate), unpaired(sums[c][0]), RELU)
+            return gate
+
+        def gated(c, h_rows=None):
+            gate = relu(c)
+            if h_rows is None:
+                h_rows = ring.tile([P, R], BF16, name="h_rows")[:]
+            nc.vector.tensor_tensor(paired(h_rows), unpaired(sums[c][1]), paired(gate), MULT)
             if c == 0:
                 gather(picked1[1][:, 1, :], PACK + 1, HALF, J)
             return h_rows
 
         def turn_h(c, h_rows):
-            pairs = h_rows[:].bitcast(F32)
+            quantize_h(c, turn(c, h_rows))
+
+        def turn(c, h_rows, h_woven=None):
+            pairs = h_rows.bitcast(F32)
             t_ps = psum.tile([P, 2, CH], F32, name="t_ps", tag=f"t{c % 2}")
             for u in range(2):
                 nc.tensor.transpose(t_ps[:, u, :], pairs[:, u * P : (u + 1) * P], ident[:])
             if c == 0:
                 h_woven = borrowed(PACK - 2)
-            else:
+            elif h_woven is None:
                 h_woven = ring.tile([P, CH * PACK], BF16, name="h_woven", align_bytes=64)[:]
             nc.scalar.copy(
                 h_woven.bitcast(F32).rearrange("p (j u) -> p j u", u=2), t_ps[:].rearrange("p u j -> p j u")
             )
+            return h_woven
+
+        def quantize_h(c, h_woven):
             if c < 2:
                 h_codes = keep.tile([P, CH], U32, name=f"shared{GROUPS[4 + c][0]}", align_bytes=64)
             else:
                 h_codes = ring.tile([P, CH], U32, name="h_codes", align_bytes=64)
             h_scales = ring.tile([P, CH], U8, name="h_scales", align_bytes=64)
             nc.vector.quantize_mx(out=h_codes[:].bitcast(FP8X4), scales=h_scales[:], in_=h_woven)
-            h_quant[c] = (h_codes, h_scales)
+            h_quant[c] = (h_codes[:], h_scales[:])
             if c == 0:
                 gather(picked1[1][:, PACK - 2, :], PLANES - 2, HALF, J)
 
-        def second_layer(c):
+        def second_layer(c, bank):
             h_codes, h_scales = h_quant[c]
             cols = slice(c * CH, (c + 1) * CH)
-            y_ps = psum.tile([P, PAGES, CH], F32, name="y_ps", tag=f"t{(c + 1) % 2}")
+            y_ps = psum.tile([P, PAGES, CH], F32, name="y_ps", tag=bank)
             for q in range(PAGES):
                 nc.tensor.matmul_mx(
                     y_ps[:, q, :],
                     lhsT=wd_w[:, 2 * P * q : 2 * P * (q + 1)].bitcast(FP4X4),
                     lhsT_scale=wd_s[:, P * q : P * (q + 1)],
-                    rhs=h_codes[:].bitcast(FP8X4),
-                    rhs_scale=h_scales[:],
+                    rhs=h_codes.bitcast(FP8X4),
+                    rhs_scale=h_scales,
                     start=True,
                     stop=True,
                 )
+            if c == 3:
+                front = keep.tile([P, CH], F32, name="front", align_bytes=64)
+                nc.scalar.copy(front[:], y_ps[:, 0, :])
+                nc.scalar.copy(y_sb[:, 1:, cols], y_ps[:, 1:, :])
+                return front
             for q0, q1 in ((0, 1), (1, PAGES)) if c == 0 else ((0, PAGES),):
                 nc.scalar.copy(y_sb[:, q0:q1, cols], y_ps[:, q0:q1, :])
-            for q in [q for q, chunk in weighed if chunk == c]:
-                nc.gpsimd.tensor_tensor(y_w[:, q, cols], y_sb[:, q, cols], gain_out[:, cols], MULT)
-            for q, first in STEPS[c]:
-                scatter(q, first * CH, (c + 1) * CH, c >= FUSED_FROM)
-                if c == CHUNKS - 1:
-                    nc.sync.dma_start(out[q * P : (q + 1) * P, :], pages[q][:])
+            return None
 
         for piece in range(3):
             last_plane(piece)
@@ -301,13 +297,66 @@ def tile_list_relu_scat_kernel(
             pass1(*group)
         first_layer(range(BANKS), (0,))
         first_layer((0, 1), (1,))
-        for c in range(CHUNKS + 1):
-            if c < CHUNKS:
-                turn_h(c, gated(c))
-            if c >= 1:
-                second_layer(c - 1)
+        for c in range(5):
+            turn_h(c, gated(c))
+            if 1 <= c <= 3:
+                second_layer(c - 1, f"t{c % 2}")
+                for q in range(3):
+                    scatter(q, c - 1, c)
             if c < 3:
                 pass1(*GROUPS[c + 3])
             for d in {0: (2, 3), 1: (), 2: (4, 5)}.get(c, (c + BANKS,)):
-                if d < CHUNKS:
+                if c < 4:
                     first_layer((d,), range(int(d < BANKS), PASSES))
+        front = second_layer(3, "t0")
+        scatter(0, 3, 4, front[:], front_gain[:])
+        second_layer(4, "t0")
+        first_layer((7,))
+
+        h_rows = gated(5, keep.tile([P, R], BF16, name="front", align_bytes=64)[:])
+        first_window = keep.tile([P, 3 * CH], F32, name="first_window", align_bytes=64)
+        weigh(first_window[:, :CH], 3, 4, 0, 1)
+        weigh(first_window[:, CH:], 1, 3, 3, 4)
+        mid_window = keep.tile([P, 3 * CH], F32, name=f"slot{5 % BANKS}", align_bytes=64)
+        weigh(mid_window[:], 0, 3, 4, 5)
+        nc.vector.tensor_copy(window(3, 0, 1), first_window[:, :CH])
+        for q in (1, 2):
+            nc.vector.tensor_copy(window(q, 3, 4), first_window[:, q * CH : (q + 1) * CH])
+        pair_woven = keep.tile([P, 2 * CH * PACK], BF16, name="pair_woven", align_bytes=64)
+        turn(5, h_rows, pair_woven[:, : CH * PACK])
+        late_h = keep.tile([P, 2 * R], BF16, name="front", align_bytes=64)
+        for c in (6, 7):
+            gate = relu(c)
+            up = keep.tile([P, R], F32, name=f"up{c}", align_bytes=64)
+            nc.scalar.copy(paired(up[:]), unpaired(sums[c][1]))
+            nc.gpsimd.tensor_tensor(late_h[:, (c - 6) * R : (c - 5) * R], up[:], gate, MULT)
+        last_window = keep.tile([P, CH], F32, name="up7", align_bytes=64)
+        weigh(last_window[:], 3, 4, 1, 2)
+        for q in range(3):
+            nc.vector.tensor_copy(window(q, 4, 5), mid_window[:, q * CH : (q + 1) * CH])
+        nc.vector.tensor_copy(window(3, 1, 2), last_window[:])
+        turn(6, late_h[:, :R], pair_woven[:, CH * PACK :])
+        pair_codes = keep.tile([P, 2 * CH], U32, name="pair_codes", align_bytes=64)
+        pair_scales = keep.tile([P, 2 * CH], U8, name="pair_scales", align_bytes=64)
+        nc.vector.quantize_mx(out=pair_codes[:].bitcast(FP8X4), scales=pair_scales[:], in_=pair_woven[:])
+        scatter(3, 2, 4)
+        turn_h(7, late_h[:, R:])
+        for q0 in (0, 2):
+            y_ps = psum.tile([P, 2, 2 * CH], F32, name="y_ps", tag="t1")
+            for q in (q0, q0 + 1):
+                nc.tensor.matmul_mx(
+                    y_ps[:, q - q0, :],
+                    lhsT=wd_w[:, 2 * P * q : 2 * P * (q + 1)].bitcast(FP4X4),
+                    lhsT_scale=wd_s[:, P * q : P * (q + 1)],
+                    rhs=pair_codes[:].bitcast(FP8X4),
+                    rhs_scale=pair_scales[:],
+                    start=True,
+                    stop=True,
+                )
+            nc.scalar.copy(y_sb[:, q0 : q0 + 2, 5 * CH : 7 * CH], y_ps[:])
+        second_layer(7, "g1")
+        scatter(0, 5, 7)
+        scatter(1, 5, 6)
+        for q, first in enumerate((7, 6, 5, 4)):
+            scatter(q, first, CHUNKS)
+            nc.sync.dma_start(out[q * P : (q + 1) * P, :], pages[q][:])

@@ -35,6 +35,7 @@ BANKS = 3
 LAG = 2
 CUTS = (0, CH, 2 * CH, 4 * CH, 8 * CH)
 GROUPS = ((0, 1), (1, 2), (2, 3), (3, 4), (4, 6), (6, 8))
+VECTOR_ZEROED = 2
 VECTOR_PRODUCTS = 6
 
 
@@ -73,6 +74,9 @@ def tile_list_relu_scat_kernel(
         for scales in (wg_s, wu_s, wd_s):
             nc.vector.memset(scales[:].bitcast(I32), 0)
         make_identity(nc, ident[:])
+        pages = [keep.tile([P, T], F32, name=f"page{q}") for q in range(VECTOR_ZEROED)]
+        for page in pages:
+            nc.vector.memset(page[:], 0.0)
 
         rows = keep.tile([P, CH], F32, name="rows")
         for w, weights in enumerate((wgt, wgo)):
@@ -139,13 +143,11 @@ def tile_list_relu_scat_kernel(
             gather(picked0[:, t, :], t, 0, J)
         for j0 in range(0, J, HALF):
             gather(picked0[:, PACK - 1, j0 : j0 + HALF], PACK - 1, j0, j0 + HALF)
-        pages = [keep.tile([P, T], F32, name=f"plane{q}") for q in range(PAGES)]
-        for page in pages:
-            nc.gpsimd.memset(page[:], 0.0)
+        for q in range(VECTOR_ZEROED, PAGES):
+            pages.append(keep.tile([P, T], F32, name=f"plane{q - VECTOR_ZEROED}"))
+            nc.gpsimd.memset(pages[q][:], 0.0)
         gain_out = keep.tile([P, J], F32, name="gain_out")
         spread(1, gain_out, (0, 4, 8), ("g0", "g1"))
-        front_gain = keep.tile([P, CH], F32, name="first_window", align_bytes=64)
-        nc.scalar.copy(front_gain[:], gain_out[:, 3 * CH : 4 * CH])
         picked1 = [keep.tile([P, PACK, HALF], F32, name=f"picked1_{half}", align_bytes=64) for half in range(2)]
         for j0 in range(0, J, HALF):
             woven0 = keep.tile([P, HALF * PACK], BF16, name=f"woven0_{j0}", align_bytes=64)
@@ -266,13 +268,12 @@ def tile_list_relu_scat_kernel(
             if c == 0:
                 gather(picked1[1][:, PACK - 2, :], PLANES - 2, HALF, J)
 
-        def second_layer(c, bank):
-            h_codes, h_scales = h_quant[c]
-            cols = slice(c * CH, (c + 1) * CH)
-            y_ps = psum.tile([P, PAGES, CH], F32, name="y_ps", tag=bank)
-            for q in range(PAGES):
+        def second_layer(first, end, q0, q1, bank):
+            h_codes, h_scales = h_quant[first]
+            y_ps = psum.tile([P, q1 - q0, (end - first) * CH], F32, name="y_ps", tag=bank)
+            for q in range(q0, q1):
                 nc.tensor.matmul_mx(
-                    y_ps[:, q, :],
+                    y_ps[:, q - q0, :],
                     lhsT=wd_w[:, 2 * P * q : 2 * P * (q + 1)].bitcast(FP4X4),
                     lhsT_scale=wd_s[:, P * q : P * (q + 1)],
                     rhs=h_codes.bitcast(FP8X4),
@@ -280,14 +281,16 @@ def tile_list_relu_scat_kernel(
                     start=True,
                     stop=True,
                 )
-            if c == 3:
-                front = keep.tile([P, CH], F32, name="front", align_bytes=64)
-                nc.scalar.copy(front[:], y_ps[:, 0, :])
-                nc.scalar.copy(y_sb[:, 1:, cols], y_ps[:, 1:, :])
-                return front
-            for q0, q1 in ((0, 1), (1, PAGES)) if c == 0 else ((0, PAGES),):
-                nc.scalar.copy(y_sb[:, q0:q1, cols], y_ps[:, q0:q1, :])
-            return None
+            return y_ps
+
+        def to_sbuf(y_ps, first, end, q0, q1, base=0):
+            nc.scalar.copy(y_sb[:, q0:q1, first * CH : end * CH], y_ps[:, q0 - base : q1 - base, :])
+
+        def quantize_pair(c, woven):
+            codes = keep.tile([P, 2 * CH], U32, name=f"pair_codes{c}", align_bytes=64)
+            scales = keep.tile([P, 2 * CH], U8, name=f"pair_scales{c}", align_bytes=64)
+            nc.vector.quantize_mx(out=codes[:].bitcast(FP8X4), scales=scales[:], in_=woven[:])
+            h_quant[c] = (codes[:], scales[:])
 
         for piece in range(3):
             last_plane(piece)
@@ -297,66 +300,70 @@ def tile_list_relu_scat_kernel(
             pass1(*group)
         first_layer(range(BANKS), (0,))
         first_layer((0, 1), (1,))
-        for c in range(5):
-            turn_h(c, gated(c))
-            if 1 <= c <= 3:
-                second_layer(c - 1, f"t{c % 2}")
-                for q in range(3):
-                    scatter(q, c - 1, c)
-            if c < 3:
-                pass1(*GROUPS[c + 3])
-            for d in {0: (2, 3), 1: (), 2: (4, 5)}.get(c, (c + BANKS,)):
-                if c < 4:
-                    first_layer((d,), range(int(d < BANKS), PASSES))
-        front = second_layer(3, "t0")
-        scatter(0, 3, 4, front[:], front_gain[:])
-        second_layer(4, "t0")
-        first_layer((7,))
+        turn_h(0, gated(0))
+        pass1(*GROUPS[3])
+        first_layer((2,), (1,))
+        first_layer((3,))
+        turn_h(1, gated(1))
+        y_ps = second_layer(0, 1, 0, PAGES, "t1")
+        to_sbuf(y_ps, 0, 1, 0, 1)
+        to_sbuf(y_ps, 0, 1, 1, PAGES)
+        for q in range(3):
+            scatter(q, 0, 1)
+        pass1(*GROUPS[4])
+        turn_h(2, gated(2))
+        to_sbuf(second_layer(1, 2, 0, PAGES, "t0"), 1, 2, 0, PAGES)
+        for q in range(2):
+            scatter(q, 1, 2)
+        turn_h(3, gated(3))
+        first_layer((4,))
+        gate = relu(4)
+        pass1(*GROUPS[5])
+        first_layer((5,))
+        to_sbuf(second_layer(2, 3, 0, PAGES, "t1"), 2, 3, 0, PAGES)
+        to_sbuf(second_layer(3, 4, 0, 2, "t0"), 3, 4, 0, 2)
 
-        h_rows = gated(5, keep.tile([P, R], BF16, name="front", align_bytes=64)[:])
-        first_window = keep.tile([P, 3 * CH], F32, name="first_window", align_bytes=64)
+        opening = keep.tile([P, 5 * CH], F32, name=f"shared{GROUPS[5][0]}", align_bytes=64)
+        h_rows = opening[:, : 2 * CH].bitcast(BF16)
+        nc.vector.tensor_tensor(paired(h_rows), unpaired(sums[4][1]), paired(gate), MULT)
+        first_window = opening[:, 2 * CH :]
         weigh(first_window[:, :CH], 3, 4, 0, 1)
-        weigh(first_window[:, CH:], 1, 3, 3, 4)
-        mid_window = keep.tile([P, 3 * CH], F32, name=f"slot{5 % BANKS}", align_bytes=64)
-        weigh(mid_window[:], 0, 3, 4, 5)
+        weigh(first_window[:, CH:], 3, 4, 1, 3)
+        mid_window = keep.tile([P, 6 * CH], F32, name=f"slot{4 % BANKS}", align_bytes=64)
+        weigh(mid_window[:, : 4 * CH], 0, 2, 2, 4)
+        weigh(mid_window[:, 4 * CH :], 2, 3, 1, 3)
         nc.vector.tensor_copy(window(3, 0, 1), first_window[:, :CH])
-        for q in (1, 2):
-            nc.vector.tensor_copy(window(q, 3, 4), first_window[:, q * CH : (q + 1) * CH])
-        pair_woven = keep.tile([P, 2 * CH * PACK], BF16, name="pair_woven", align_bytes=64)
-        turn(5, h_rows, pair_woven[:, : CH * PACK])
-        late_h = keep.tile([P, 2 * R], BF16, name="front", align_bytes=64)
-        for c in (6, 7):
-            gate = relu(c)
+        nc.vector.tensor_copy(window(3, 1, 3), first_window[:, CH:])
+        for q in range(2):
+            nc.vector.tensor_copy(window(q, 2, 4), mid_window[:, 2 * q * CH : 2 * (q + 1) * CH])
+        nc.vector.tensor_copy(window(2, 1, 3), mid_window[:, 4 * CH :])
+        pair_woven = [keep.tile([P, 2 * CH * PACK], BF16, name=f"pair_woven{c}", align_bytes=64) for c in (4, 6)]
+        turn(4, h_rows, pair_woven[0][:, : CH * PACK])
+        late_h = keep.tile([P, 3 * R], BF16, name=f"shared{GROUPS[5][0]}", align_bytes=64)
+        for c in (5, 6, 7):
+            if c > 5:
+                first_layer((c,))
+            gate = keep.tile([P, R], F32, name=f"gate{c}", align_bytes=64)
+            nc.scalar.activation(paired(gate[:]), unpaired(sums[c][0]), RELU)
             up = keep.tile([P, R], F32, name=f"up{c}", align_bytes=64)
             nc.scalar.copy(paired(up[:]), unpaired(sums[c][1]))
-            nc.gpsimd.tensor_tensor(late_h[:, (c - 6) * R : (c - 5) * R], up[:], gate, MULT)
-        last_window = keep.tile([P, CH], F32, name="up7", align_bytes=64)
-        weigh(last_window[:], 3, 4, 1, 2)
-        for q in range(3):
-            nc.vector.tensor_copy(window(q, 4, 5), mid_window[:, q * CH : (q + 1) * CH])
-        nc.vector.tensor_copy(window(3, 1, 2), last_window[:])
-        turn(6, late_h[:, :R], pair_woven[:, CH * PACK :])
-        pair_codes = keep.tile([P, 2 * CH], U32, name="pair_codes", align_bytes=64)
-        pair_scales = keep.tile([P, 2 * CH], U8, name="pair_scales", align_bytes=64)
-        nc.vector.quantize_mx(out=pair_codes[:].bitcast(FP8X4), scales=pair_scales[:], in_=pair_woven[:])
-        scatter(3, 2, 4)
-        turn_h(7, late_h[:, R:])
-        for q0 in (0, 2):
-            y_ps = psum.tile([P, 2, 2 * CH], F32, name="y_ps", tag="t1")
-            for q in (q0, q0 + 1):
-                nc.tensor.matmul_mx(
-                    y_ps[:, q - q0, :],
-                    lhsT=wd_w[:, 2 * P * q : 2 * P * (q + 1)].bitcast(FP4X4),
-                    lhsT_scale=wd_s[:, P * q : P * (q + 1)],
-                    rhs=pair_codes[:].bitcast(FP8X4),
-                    rhs_scale=pair_scales[:],
-                    start=True,
-                    stop=True,
-                )
-            nc.scalar.copy(y_sb[:, q0 : q0 + 2, 5 * CH : 7 * CH], y_ps[:])
-        second_layer(7, "g1")
-        scatter(0, 5, 7)
-        scatter(1, 5, 6)
-        for q, first in enumerate((7, 6, 5, 4)):
+            nc.gpsimd.tensor_tensor(late_h[:, (c - 5) * R : (c - 4) * R], up[:], gate[:], MULT)
+        turn(5, late_h[:, :R], pair_woven[0][:, CH * PACK :])
+        quantize_pair(4, pair_woven[0])
+        to_sbuf(second_layer(3, 4, 2, PAGES, "t1"), 3, 4, 2, PAGES, 2)
+        for q in (2, 3):
+            scatter(q, 3, 4)
+        for c in (6, 7):
+            turn(c, late_h[:, (c - 5) * R : (c - 4) * R], pair_woven[1][:, (c - 6) * CH * PACK : (c - 5) * CH * PACK])
+        quantize_pair(6, pair_woven[1])
+        to_sbuf(second_layer(4, 6, 0, 1, "t0"), 4, 6, 0, 1)
+        to_sbuf(second_layer(4, 6, 1, 2, "t1"), 4, 6, 1, 2, 1)
+        to_sbuf(second_layer(6, 8, 0, 1, "g0"), 6, 8, 0, 1)
+        to_sbuf(second_layer(6, 8, 1, 2, "g2"), 6, 8, 1, 2, 1)
+        to_sbuf(second_layer(4, 6, 2, PAGES, "t0"), 4, 6, 2, PAGES, 2)
+        to_sbuf(second_layer(6, 8, 2, PAGES, "g1"), 6, 8, 2, PAGES, 2)
+        for q in range(2):
+            scatter(q, 4, 6)
+        for q, first in enumerate((6, 6, 4, 4)):
             scatter(q, first, CHUNKS)
             nc.sync.dma_start(out[q * P : (q + 1) * P, :], pages[q][:])

@@ -29,7 +29,7 @@ QUADRANT = 32
 SCALE_ROWS = 4
 RING = 4
 
-HEAD = 256
+HEAD = 128
 HALF = J // 2
 BANKS = 3
 LAG = 2
@@ -81,7 +81,7 @@ def tile_list_relu_scat_kernel(
         rows = keep.tile([P, CH], F32, name="rows")
         for w, weights in enumerate((wgt, wgo)):
             nc.sync.dma_start(
-                rows[w * P // 2 : (w + 1) * P // 2, :], weights.rearrange("(g r) (i e) -> r g i e", r=LANE, e=CH)[0]
+                rows[w * P // 2 : (w + 1) * P // 2, :], weights.rearrange("p (h n) -> (p h) n", h=2)[:: LANE + 1]
             )
         nc.sync.dma_start(planes[0][:], x_rows[0, 0])
         nc.sync.dma_start(pick[:], offs)
@@ -116,7 +116,7 @@ def tile_list_relu_scat_kernel(
                     nc.tensor.transpose(back[:, i, :], wide[:, i, :], ident[:])
                 nc.scalar.copy(dst[:, i0 * CH : (i0 + step) * CH], back[:].rearrange("p i e -> p (i e)"))
 
-        spread(0, gain, (2, 4, 6, 8), ("u0", "u1", "u2"))
+        spread(0, gain, (1, 4, 8), ("u0", "u1"))
 
         x_codes = [keep.tile([P, J], U32, name=f"x_codes{a}", align_bytes=64) for a in range(PASSES)]
         x_scales = [keep.tile([P, J], U8, name=f"x_scales{a}", align_bytes=64) for a in range(PASSES)]
@@ -137,7 +137,7 @@ def tile_list_relu_scat_kernel(
             )
 
         picked0 = keep.tile([P, PACK, J], F32, name="picked0")
-        for j0, j1 in ((0, HEAD), (HEAD, J)):
+        for j0, j1 in ((0, HEAD), (HEAD, HALF), (HALF, J)):
             gather(picked0[:, 0, j0:j1], 0, j0, j1)
         for t in range(1, PACK - 1):
             gather(picked0[:, t, :], t, 0, J)

@@ -33,7 +33,8 @@ HEAD = 128
 HALF = J // 2
 BANKS = 3
 LAG = 2
-CUTS = (0, CH, 2 * CH, 4 * CH, 8 * CH)
+CUTS = (0, CH, 2 * CH, 4 * CH)
+PARTS = (0, 4 * CH, 6 * CH, 8 * CH)
 GROUPS = ((0, 1), (1, 2), (2, 3), (3, 4), (4, 6), (6, 8))
 VECTOR_ZEROED = 2
 VECTOR_PRODUCTS = 6
@@ -148,32 +149,38 @@ def tile_list_relu_scat_kernel(
             nc.gpsimd.memset(pages[q][:], 0.0)
         gain_out = keep.tile([P, J], F32, name="gain_out")
         spread(1, gain_out, (0, 4, 8), ("g0", "g1"))
-        picked1 = [keep.tile([P, PACK, HALF], F32, name=f"picked1_{half}", align_bytes=64) for half in range(2)]
+        picked1 = [
+            keep.tile([P, PACK, hi - lo], F32, name=f"picked1_{lo}", align_bytes=64) for lo, hi in zip(PARTS, PARTS[1:])
+        ]
         for j0 in range(0, J, HALF):
             woven0 = keep.tile([P, HALF * PACK], BF16, name=f"woven0_{j0}", align_bytes=64)
             quantize_x(0, j0, HALF, weave(picked0[:, :, j0 : j0 + HALF], woven0[:]))
-        for t in range(PACK - 1):
-            for half in range(2):
-                if t == 0 or half == 0:
-                    gather(picked1[half][:, t, :], PACK + t, half * HALF, (half + 1) * HALF)
+        def gather_part(part, t):
+            gather(picked1[part][:, t, :], PACK + t, PARTS[part], PARTS[part + 1])
 
-        def borrowed(t):
-            return picked1[1][:, t, : CH * PACK // 2].bitcast(BF16)
+        for t in range(PACK - 1):
+            gather_part(0, t)
+            if t < 2:
+                gather_part(1, t)
+
+        def borrowed(part, t, width):
+            seam = (t + 1) * (PARTS[part + 1] - PARTS[part])
+            return picked1[part][:].rearrange("p t j -> p (t j)")[:, seam - width // 2 : seam + width // 2]
 
         def pass1(first, end):
             if first == 0:
-                woven = borrowed(PACK - 1)
+                woven = borrowed(1, 2, CH * PACK // 2).bitcast(BF16)
             else:
                 woven = keep.tile([P, (end - first) * CH * PACK], BF16, name=f"shared{first}", align_bytes=64)[:]
             for c in range(first, end):
-                half, lo = divmod(c * CH, HALF)
-                weave(picked1[half][:, :, lo : lo + CH], woven[:, (c - first) * CH * PACK : (c - first + 1) * CH * PACK])
+                part = max(n for n, lo in enumerate(PARTS) if lo <= c * CH)
+                lo = c * CH - PARTS[part]
+                weave(picked1[part][:, :, lo : lo + CH], woven[:, (c - first) * CH * PACK : (c - first + 1) * CH * PACK])
             quantize_x(1, first * CH, (end - first) * CH, woven)
 
         def last_plane(piece):
             j0, j1 = CUTS[piece], CUTS[piece + 1]
-            half, lo = divmod(j0, HALF)
-            gather(picked1[half][:, PACK - 1, lo : lo + j1 - j0], PLANES - 1, j0, j1)
+            gather(picked1[0][:, PACK - 1, j0:j1], PLANES - 1, j0, j1)
 
         y_sb = keep.tile([P, PAGES, J], F32, name="y_sb")
 
@@ -225,7 +232,7 @@ def tile_list_relu_scat_kernel(
 
         def relu(c):
             if c == 0:
-                gate = picked1[1][:, 1, :]
+                gate = borrowed(2, 2, R)
             else:
                 gate = keep.tile([P, R], F32, name=f"slot{c % BANKS}", align_bytes=64)[:]
             nc.scalar.activation(paired(gate), unpaired(sums[c][0]), RELU)
@@ -237,7 +244,8 @@ def tile_list_relu_scat_kernel(
                 h_rows = ring.tile([P, R], BF16, name="h_rows")[:]
             nc.vector.tensor_tensor(paired(h_rows), unpaired(sums[c][1]), paired(gate), MULT)
             if c == 0:
-                gather(picked1[1][:, 1, :], PACK + 1, HALF, J)
+                gather_part(2, 3)
+                gather_part(2, 2)
             return h_rows
 
         def turn_h(c, h_rows):
@@ -249,7 +257,7 @@ def tile_list_relu_scat_kernel(
             for u in range(2):
                 nc.tensor.transpose(t_ps[:, u, :], pairs[:, u * P : (u + 1) * P], ident[:])
             if c == 0:
-                h_woven = borrowed(PACK - 2)
+                h_woven = borrowed(2, 0, CH * PACK // 2).bitcast(BF16)
             elif h_woven is None:
                 h_woven = ring.tile([P, CH * PACK], BF16, name="h_woven", align_bytes=64)[:]
             nc.scalar.copy(
@@ -258,15 +266,16 @@ def tile_list_relu_scat_kernel(
             return h_woven
 
         def quantize_h(c, h_woven):
-            if c < 2:
-                h_codes = keep.tile([P, CH], U32, name=f"shared{GROUPS[4 + c][0]}", align_bytes=64)
+            if c == 0:
+                h_codes = keep.tile([P, CH], U32, name=f"shared{GROUPS[5][0]}", align_bytes=64)
             else:
                 h_codes = ring.tile([P, CH], U32, name="h_codes", align_bytes=64)
             h_scales = ring.tile([P, CH], U8, name="h_scales", align_bytes=64)
             nc.vector.quantize_mx(out=h_codes[:].bitcast(FP8X4), scales=h_scales[:], in_=h_woven)
             h_quant[c] = (h_codes[:], h_scales[:])
             if c == 0:
-                gather(picked1[1][:, PACK - 2, :], PLANES - 2, HALF, J)
+                gather_part(2, 1)
+                gather_part(2, 0)
 
         def second_layer(first, end, q0, q1, bank):
             h_codes, h_scales = h_quant[first]
@@ -295,7 +304,8 @@ def tile_list_relu_scat_kernel(
         for piece in range(3):
             last_plane(piece)
         pass1(*GROUPS[0])
-        last_plane(3)
+        gather_part(1, 3)
+        gather_part(1, 2)
         for group in GROUPS[1:3]:
             pass1(*group)
         first_layer(range(BANKS), (0,))
@@ -313,9 +323,8 @@ def tile_list_relu_scat_kernel(
         pass1(*GROUPS[4])
         turn_h(2, gated(2))
         to_sbuf(second_layer(1, 2, 0, PAGES, "t0"), 1, 2, 0, PAGES)
-        for q in range(2):
-            scatter(q, 1, 2)
-        turn_h(3, gated(3))
+        h_woven = keep.tile([P, CH * PACK], BF16, name="opening", align_bytes=64)
+        quantize_h(3, turn(3, gated(3), h_woven[:]))
         first_layer((4,))
         gate = relu(4)
         pass1(*GROUPS[5])
@@ -323,23 +332,25 @@ def tile_list_relu_scat_kernel(
         to_sbuf(second_layer(2, 3, 0, PAGES, "t1"), 2, 3, 0, PAGES)
         to_sbuf(second_layer(3, 4, 0, 2, "t0"), 3, 4, 0, 2)
 
-        opening = keep.tile([P, 5 * CH], F32, name=f"shared{GROUPS[5][0]}", align_bytes=64)
+        opening = keep.tile([P, 5 * CH], F32, name="opening", align_bytes=64)
         h_rows = opening[:, : 2 * CH].bitcast(BF16)
         nc.vector.tensor_tensor(paired(h_rows), unpaired(sums[4][1]), paired(gate), MULT)
         first_window = opening[:, 2 * CH :]
         weigh(first_window[:, :CH], 3, 4, 0, 1)
-        weigh(first_window[:, CH:], 3, 4, 1, 3)
-        mid_window = keep.tile([P, 6 * CH], F32, name=f"slot{4 % BANKS}", align_bytes=64)
-        weigh(mid_window[:, : 4 * CH], 0, 2, 2, 4)
-        weigh(mid_window[:, 4 * CH :], 2, 3, 1, 3)
+        weigh(first_window[:, CH:], 2, 4, 1, 2)
+        mid_window = keep.tile([P, 8 * CH], F32, name=f"slot{4 % BANKS}", align_bytes=64)
+        weigh(mid_window[:, : 2 * CH], 2, 4, 2, 3)
+        weigh(mid_window[:, 2 * CH :], 0, 2, 1, 4)
         nc.vector.tensor_copy(window(3, 0, 1), first_window[:, :CH])
-        nc.vector.tensor_copy(window(3, 1, 3), first_window[:, CH:])
+        for q in (2, 3):
+            nc.vector.tensor_copy(window(q, 1, 2), first_window[:, (q - 1) * CH : q * CH])
+        for q in (2, 3):
+            nc.vector.tensor_copy(window(q, 2, 3), mid_window[:, (q - 2) * CH : (q - 1) * CH])
         for q in range(2):
-            nc.vector.tensor_copy(window(q, 2, 4), mid_window[:, 2 * q * CH : 2 * (q + 1) * CH])
-        nc.vector.tensor_copy(window(2, 1, 3), mid_window[:, 4 * CH :])
+            nc.vector.tensor_copy(window(q, 1, 4), mid_window[:, (2 + 3 * q) * CH : (5 + 3 * q) * CH])
         pair_woven = [keep.tile([P, 2 * CH * PACK], BF16, name=f"pair_woven{c}", align_bytes=64) for c in (4, 6)]
         turn(4, h_rows, pair_woven[0][:, : CH * PACK])
-        late_h = keep.tile([P, 3 * R], BF16, name=f"shared{GROUPS[5][0]}", align_bytes=64)
+        late_h = keep.tile([P, 3 * R], BF16, name="opening", align_bytes=64)
         for c in (5, 6, 7):
             if c > 5:
                 first_layer((c,))

@@ -1,7 +1,6 @@
 from contextlib import ExitStack
 
 import concourse.mybir as mybir
-from concourse.masks import make_identity
 
 K, R, N, T, J = 1024, 512, 512, 2048, 1024
 FLOPS = 2 * (2 * K * R + R * N) * J
@@ -74,12 +73,21 @@ def tile_list_relu_scat_kernel(
 
         for scales in (wg_s, wu_s, wd_s):
             nc.vector.memset(scales[:].bitcast(I32), 0)
-        make_identity(nc, ident[:])
-        pages = [keep.tile([P, T], F32, name=f"page{q}") for q in range(VECTOR_ZEROED)]
-        for page in pages:
-            nc.vector.memset(page[:], 0.0)
+        blank = keep.tile([P, P], F32, name="page0")
+        nc.gpsimd.memset(blank[:], 0.0)
+        nc.gpsimd.affine_select(
+            out=ident[:],
+            in_=blank[:],
+            compare_op=mybir.AluOpType.not_equal,
+            fill=1.0,
+            base=0,
+            pattern=[[-1, P]],
+            channel_multiplier=1,
+        )
+        pages = [keep.tile([P, T], F32, name="page0")]
+        nc.gpsimd.memset(pages[0][:], 0.0)
 
-        rows = keep.tile([P, CH], F32, name="rows")
+        rows = keep.tile([P, CH], F32, name="page1")
         for w, weights in enumerate((wgt, wgo)):
             nc.sync.dma_start(
                 rows[w * P // 2 : (w + 1) * P // 2, :], weights.rearrange("p (h n) -> (p h) n", h=2)[:: LANE + 1]
@@ -102,6 +110,8 @@ def tile_list_relu_scat_kernel(
 
         turned = psum.tile([P, P], F32, name="turned", tag="t0")
         nc.tensor.transpose(turned[:], rows[:], ident[:])
+        pages.append(keep.tile([P, T], F32, name="page1"))
+        nc.gpsimd.memset(pages[1][:], 0.0)
 
         def spread(w, dst, cuts, banks):
             groups = turned[:, w * P // 2 : (w + 1) * P // 2].rearrange("p (g i) -> p i g", i=CHUNKS)

@@ -26,17 +26,10 @@ PAGES = N // P
 LANE = 16
 QUADRANT = 32
 SCALE_ROWS = 4
-RING = 4
-
 HEAD = 128
 HALF = J // 2
+QUARTER = J // 4
 BANKS = 3
-LAG = 2
-CUTS = (0, CH, 2 * CH, 4 * CH)
-PARTS = (0, 4 * CH, 6 * CH, 8 * CH)
-GROUPS = ((0, 1), (1, 2), (2, 3), (3, 4), (4, 6), (6, 8))
-VECTOR_ZEROED = 2
-VECTOR_PRODUCTS = 6
 
 
 def tile_list_relu_scat_kernel(
@@ -45,7 +38,6 @@ def tile_list_relu_scat_kernel(
     nc = tc.nc
     with ExitStack() as ctx:
         keep = ctx.enter_context(tc.tile_pool(name="keep", bufs=1))
-        ring = ctx.enter_context(tc.tile_pool(name="ring", bufs=RING))
         psum = ctx.enter_context(tc.psum_pool(name="psum", bufs=1))
 
         pick = keep.tile([P, J // LANE], U16, name="pick")
@@ -53,25 +45,17 @@ def tile_list_relu_scat_kernel(
         x_rows = xT.rearrange("(a p t) n -> a t p n", p=P, t=PACK)
         planes = [keep.tile([P, T], F32, name=f"plane{m}") for m in range(PLANES)]
         gain = keep.tile([P, J], F32, name="gain")
-        wg_w = [keep.tile([P, 2 * R], U8, name=f"wg_w{a}", align_bytes=64) for a in range(PASSES)]
-        wu_w = [keep.tile([P, 2 * R], U8, name=f"wu_w{a}", align_bytes=64) for a in range(PASSES)]
+        raw_w = [[keep.tile([P, R], U16, name=f"raw_w{w}{a}") for a in range(PASSES)] for w in range(2)]
+        w_words = [[keep.tile([P, 2 * R], U8, name=f"w_words{w}{a}", align_bytes=64) for a in range(PASSES)] for w in range(2)]
+        w_scales = [keep.tile([P, PASSES * R], U8, name=f"w_scales{w}", align_bytes=64) for w in range(2)]
+        raw_s = keep.tile([P, R], U8, name="page1")
+        dealt_s = keep.tile([P, R], U8, name="dealt_s")
         wd_w = keep.tile([P, 2 * N], U8, name="wd_w", align_bytes=64)
-        wg_s = keep.tile([P, PASSES * R], U8, name="wg_s", align_bytes=64)
-        wu_s = keep.tile([P, PASSES * R], U8, name="wu_s", align_bytes=64)
         wd_s = keep.tile([P, N], U8, name="wd_s", align_bytes=64)
         ident = keep.tile([P, P], F32, name="ident")
 
-        def load_scales(scales, dram_scales):
-            passes = dram_scales.shape[0]
-            rows = dram_scales.bitcast(I32).rearrange("a (d r) n -> d r a n", r=SCALE_ROWS)
-            for d in range(P // QUADRANT):
-                live = scales[QUADRANT * d : QUADRANT * d + SCALE_ROWS, :]
-                nc.sync.dma_start(live.bitcast(I32).rearrange("p (a n) -> p a n", a=passes), rows[d])
-
-        def load_words(words, dram_words):
-            nc.sync.dma_start(words[:].bitcast(I32), dram_words.bitcast(I32))
-
-        for scales in (wg_s, wu_s, wd_s):
+        nc.vector.memset(raw_s[2 * QUADRANT :, :].bitcast(I32), 0)
+        for scales in (*w_scales, wd_s):
             nc.vector.memset(scales[:].bitcast(I32), 0)
         blank = keep.tile([P, P], F32, name="page0")
         nc.gpsimd.memset(blank[:], 0.0)
@@ -87,7 +71,7 @@ def tile_list_relu_scat_kernel(
         pages = [keep.tile([P, T], F32, name="page0")]
         nc.gpsimd.memset(pages[0][:], 0.0)
 
-        rows = keep.tile([P, CH], F32, name="page1")
+        rows = keep.tile([P, CH], F32, name="rows")
         for w, weights in enumerate((wgt, wgo)):
             nc.sync.dma_start(
                 rows[w * P // 2 : (w + 1) * P // 2, :], weights.rearrange("p (h n) -> (p h) n", h=2)[:: LANE + 1]
@@ -95,18 +79,36 @@ def tile_list_relu_scat_kernel(
         nc.sync.dma_start(planes[0][:], x_rows[0, 0])
         nc.sync.dma_start(pick[:], offs)
         nc.sync.dma_start(gain[:, :HEAD], wgt[:, :HEAD])
-        scales_behind_plane = {1: (wg_s, wg_scales), 2: (wu_s, wu_scales)}
+        for w, dram_scales in enumerate((wg_scales, wu_scales)):
+            nc.scalar.dma_start(
+                raw_s[QUADRANT * w : QUADRANT * (w + 1), :].bitcast(I32),
+                dram_scales.bitcast(I32).rearrange("a q n -> q a n"),
+            )
+        nc.vector.tensor_copy(
+            dealt_s[:].rearrange("p (t m) -> p t m", t=PACK), raw_s[:].rearrange("p (m t) -> p t m", t=PACK)
+        )
+
+        def move_scales(w):
+            for d in range(P // QUADRANT):
+                first = QUADRANT * w + 2 * SCALE_ROWS * d
+                live = w_scales[w][QUADRANT * d : QUADRANT * d + SCALE_ROWS, :]
+                nc.sync.dma_start(
+                    live.bitcast(I32).rearrange("p (a n) -> p a n", a=PASSES),
+                    dealt_s[first : first + 2 * SCALE_ROWS, :].bitcast(I32),
+                )
+
         for m in range(1, PLANES):
             nc.sync.dma_start(planes[m][:], x_rows[m // PACK, m % PACK])
-            if m in scales_behind_plane:
-                load_scales(*scales_behind_plane[m])
-            if m >= PLANES - PASSES:
-                a = m - (PLANES - PASSES)
-                load_words(wg_w[a], wg_words[a])
-                load_words(wu_w[a], wu_words[a])
+            if m in (1, 2):
+                move_scales(m - 1)
+            if m in (5, 6):
+                for w, dram_words in enumerate((wg_words, wu_words)):
+                    nc.sync.dma_start(raw_w[w][m - 5][:].bitcast(I32), dram_words[m - 5].bitcast(I32))
         nc.sync.dma_start(place[:], offs2)
-        load_words(wd_w, wd_words[0])
-        load_scales(wd_s, wd_scales)
+        nc.sync.dma_start(wd_w[:].bitcast(I32), wd_words[0].bitcast(I32))
+        wd_rows = wd_scales.bitcast(I32).rearrange("a (d r) n -> d r (a n)", r=SCALE_ROWS)
+        for d in range(P // QUADRANT):
+            nc.sync.dma_start(wd_s[QUADRANT * d : QUADRANT * d + SCALE_ROWS, :].bitcast(I32), wd_rows[d])
 
         turned = psum.tile([P, P], F32, name="turned", tag="t0")
         nc.tensor.transpose(turned[:], rows[:], ident[:])
@@ -142,10 +144,8 @@ def tile_list_relu_scat_kernel(
             )
             return woven
 
-        def quantize_x(a, j0, width, woven):
-            nc.vector.quantize_mx(
-                out=x_codes[a][:, j0 : j0 + width].bitcast(FP8X4), scales=x_scales[a][:, j0 : j0 + width], in_=woven
-            )
+        def quantize_x(a, j0, j1, woven):
+            nc.vector.quantize_mx(out=x_codes[a][:, j0:j1].bitcast(FP8X4), scales=x_scales[a][:, j0:j1], in_=woven)
 
         picked0 = keep.tile([P, PACK, J], F32, name="picked0")
         for j0, j1 in ((0, HEAD), (HEAD, HALF), (HALF, J)):
@@ -154,237 +154,202 @@ def tile_list_relu_scat_kernel(
             gather(picked0[:, t, :], t, 0, J)
         for j0 in range(0, J, HALF):
             gather(picked0[:, PACK - 1, j0 : j0 + HALF], PACK - 1, j0, j0 + HALF)
-        for q in range(VECTOR_ZEROED, PAGES):
-            pages.append(keep.tile([P, T], F32, name=f"plane{q - VECTOR_ZEROED}"))
+        for q in range(2, PAGES):
+            pages.append(keep.tile([P, T], F32, name=f"plane{q - 2}"))
             nc.gpsimd.memset(pages[q][:], 0.0)
         gain_out = keep.tile([P, J], F32, name="gain_out")
         spread(1, gain_out, (0, 4, 8), ("g0", "g1"))
-        picked1 = [
-            keep.tile([P, PACK, hi - lo], F32, name=f"picked1_{lo}", align_bytes=64) for lo, hi in zip(PARTS, PARTS[1:])
-        ]
         for j0 in range(0, J, HALF):
             woven0 = keep.tile([P, HALF * PACK], BF16, name=f"woven0_{j0}", align_bytes=64)
-            quantize_x(0, j0, HALF, weave(picked0[:, :, j0 : j0 + HALF], woven0[:]))
-        def gather_part(part, t):
-            gather(picked1[part][:, t, :], PACK + t, PARTS[part], PARTS[part + 1])
+            quantize_x(0, j0, j0 + HALF, weave(picked0[:, :, j0 : j0 + HALF], woven0[:]))
+        for a in range(PASSES):
+            for w in range(2):
+                nc.scalar.copy(
+                    w_words[w][a][:].bitcast(U16).rearrange("p (t m) -> p t m", t=PACK),
+                    raw_w[w][a][:].rearrange("p (m t) -> p t m", t=PACK),
+                )
 
+        picked1 = keep.tile([P, 7 * HALF], F32, name="picked1", align_bytes=64)
+
+        def rows_from(start):
+            return picked1[:, start : start + PACK * HALF].rearrange("p (t j) -> p t j", t=PACK)
+
+        front = rows_from(3 * HALF)
+        third = rows_from(0)[:, :, :QUARTER]
+        fourth = rows_from(3 * HALF - QUARTER)[:, :, :QUARTER]
         for t in range(PACK - 1):
-            gather_part(0, t)
-            if t < 2:
-                gather_part(1, t)
+            gather(front[:, t, :], PACK + t, 0, HALF)
+            gather(third[:, t, :], PACK + t, HALF, HALF + QUARTER)
+            if t == 0:
+                gather(fourth[:, t, :], PACK + t, HALF + QUARTER, J)
+        for j0, j1 in ((0, CH), (CH, 2 * CH), (2 * CH, HALF)):
+            gather(front[:, PACK - 1, j0:j1], PLANES - 1, j0, j1)
 
-        def borrowed(part, t, width):
-            seam = (t + 1) * (PARTS[part + 1] - PARTS[part])
-            return picked1[part][:].rearrange("p t j -> p (t j)")[:, seam - width // 2 : seam + width // 2]
+        def pass1(src, j0, j1):
+            woven = keep.tile([P, (j1 - j0) * PACK], BF16, name=f"woven1_{j0}", align_bytes=64)
+            quantize_x(1, j0, j1, weave(src, woven[:]))
 
-        def pass1(first, end):
-            if first == 0:
-                woven = borrowed(1, 2, CH * PACK // 2).bitcast(BF16)
-            else:
-                woven = keep.tile([P, (end - first) * CH * PACK], BF16, name=f"shared{first}", align_bytes=64)[:]
-            for c in range(first, end):
-                part = max(n for n, lo in enumerate(PARTS) if lo <= c * CH)
-                lo = c * CH - PARTS[part]
-                weave(picked1[part][:, :, lo : lo + CH], woven[:, (c - first) * CH * PACK : (c - first + 1) * CH * PACK])
-            quantize_x(1, first * CH, (end - first) * CH, woven)
+        sums = {}
 
-        def last_plane(piece):
-            j0, j1 = CUTS[piece], CUTS[piece + 1]
-            gather(picked1[0][:, PACK - 1, j0:j1], PLANES - 1, j0, j1)
+        def first_layer(c, passes=range(PASSES)):
+            if 0 in passes:
+                g_ps = psum.tile([P, PACK, CH], F32, name="g_ps", tag=f"g{c % BANKS}")
+                u_ps = psum.tile([P, PACK, CH], F32, name="u_ps", tag=f"u{c % BANKS}")
+                sums[c] = (g_ps, u_ps)
+            cols = slice(c * CH, (c + 1) * CH)
+            for a in passes:
+                for w in range(2):
+                    for t in range(PACK):
+                        nc.tensor.matmul_mx(
+                            sums[c][w][:, t, :],
+                            lhsT=w_words[w][a][:, 2 * P * t : 2 * P * (t + 1)].bitcast(FP4X4),
+                            lhsT_scale=w_scales[w][:, a * R + P * t : a * R + P * (t + 1)],
+                            rhs=x_codes[a][:, cols].bitcast(FP8X4),
+                            rhs_scale=x_scales[a][:, cols],
+                            start=(a == 0 and t == 0),
+                            stop=(a == PASSES - 1 and t == PACK - 1),
+                        )
 
-        y_sb = keep.tile([P, PAGES, J], F32, name="y_sb")
+        def by_pick(bank):
+            return bank[:].rearrange("p t j -> p j t")
+
+        def words(ap):
+            return ap.rearrange("p (j t) -> p j t", t=PACK)
+
+        def quantize_h(first, end, woven):
+            codes = keep.tile([P, (end - first) * CH], U32, name=f"h_codes{first}", align_bytes=64)
+            scales = keep.tile([P, (end - first) * CH], U8, name=f"h_scales{first}", align_bytes=64)
+            nc.vector.quantize_mx(out=codes[:].bitcast(FP8X4), scales=scales[:], in_=woven)
+            return codes, scales
+
+        def second_layer(dst, q, quantised, lo, hi):
+            codes, scales = quantised
+            nc.tensor.matmul_mx(
+                dst,
+                lhsT=wd_w[:, 2 * P * q : 2 * P * (q + 1)].bitcast(FP4X4),
+                lhsT_scale=wd_s[:, P * q : P * (q + 1)],
+                rhs=codes[:, lo:hi].bitcast(FP8X4),
+                rhs_scale=scales[:, lo:hi],
+                start=True,
+                stop=True,
+            )
+
+        def chunk_y(quantised, lo, bank):
+            y_ps = psum.tile([P, PAGES, CH], F32, name="y_ps", tag=bank)
+            for q in range(PAGES):
+                second_layer(y_ps[:, q, :], q, quantised, lo, lo + CH)
+            return y_ps
+
+        def relu(c):
+            gate = keep.tile([P, R], F32, name=f"gate{c}")
+            nc.scalar.activation(words(gate[:]), by_pick(sums[c][0]), RELU)
+            return gate
+
+        def vector_h(c, gate):
+            woven = keep.tile([P, R], BF16, name=f"h_woven{c}", align_bytes=64)
+            nc.vector.tensor_tensor(words(woven[:]), by_pick(sums[c][1]), words(gate[:]), MULT)
+            return quantize_h(c, c + 1, woven[:])
+
+        def factors(c, gate, up):
+            nc.scalar.activation(words(gate), by_pick(sums[c][0]), RELU)
+            nc.scalar.copy(words(up), by_pick(sums[c][1]))
+
+        def weigh(engine, dst, src, j0):
+            count, width = src.shape[1], src.shape[2]
+            engine.tensor_tensor(
+                dst.rearrange("p (q j) -> p q j", q=count),
+                src,
+                gain_out[:, j0 : j0 + width].unsqueeze(1).to_broadcast([P, count, width]),
+                MULT,
+            )
 
         def window(q, first, end):
             return pages[q][:].indirect(place[:, first * CH // LANE : end * CH // LANE])
 
-        def scatter(q, first, end, y=None, weights=None):
-            cols = slice(first * CH, end * CH)
-            if y is None:
-                y, weights = y_sb[:, q, cols], gain_out[:, cols]
-            nc.vector.tensor_tensor(window(q, first, end), y, weights, MULT)
+        def put(q, first, end, src):
+            nc.vector.tensor_copy(window(q, first, end), src)
 
-        def weigh(dst, q0, q1, first, end):
-            cols = slice(first * CH, end * CH)
-            nc.gpsimd.tensor_tensor(
-                dst.rearrange("p (q j) -> p q j", q=q1 - q0),
-                y_sb[:, q0:q1, cols],
-                gain_out[:, cols].unsqueeze(1).to_broadcast([P, q1 - q0, (end - first) * CH]),
-                MULT,
-            )
+        def put_weighed(q, first, end, src):
+            nc.vector.tensor_tensor(window(q, first, end), src, gain_out[:, first * CH : end * CH], MULT)
 
-        h_quant = {}
-        sums = {}
+        for c in range(BANKS):
+            first_layer(c, (0,))
+        for c in range(2):
+            pass1(front[:, :, c * CH : (c + 1) * CH], c * CH, (c + 1) * CH)
+            first_layer(c, (1,))
+        gather(third[:, PACK - 1, :], PLANES - 1, HALF, HALF + QUARTER)
+        pass1(front[:, :, 2 * CH : 3 * CH], 2 * CH, 3 * CH)
+        first_layer(2, (1,))
+        h0 = vector_h(0, relu(0))
+        pass1(front[:, :, 3 * CH :], 3 * CH, HALF)
+        for t in (3, 2, 1):
+            gather(fourth[:, t, :], PACK + t, HALF + QUARTER, J)
+        h1 = vector_h(1, relu(1))
+        h2 = vector_h(2, relu(2))
+        y0_ps = chunk_y(h0, 0, "t0")
+        y1_ps = chunk_y(h1, 0, "t1")
+        pass1(third, HALF, HALF + QUARTER)
+        pass1(fourth, HALF + QUARTER, J)
+        for c in (3, 4):
+            first_layer(c)
 
-        def first_layer(chunks, passes=range(PASSES)):
-            for c in chunks if 0 in passes else ():
-                g_ps = psum.tile([P, R], F32, name="g_ps", tag=f"g{c % BANKS}")
-                u_ps = psum.tile([P, R], F32, name="u_ps", tag=f"u{c % BANKS}")
-                sums[c] = (g_ps, u_ps)
-            for a in passes:
-                for c in chunks:
-                    cols = slice(c * CH, (c + 1) * CH)
-                    for acc, words, scales in zip(sums[c], (wg_w, wu_w), (wg_s, wu_s)):
-                        nc.tensor.matmul_mx(
-                            acc[:],
-                            lhsT=x_codes[a][:, cols].bitcast(FP8X4),
-                            lhsT_scale=x_scales[a][:, cols],
-                            rhs=words[a][:].bitcast(FP4X4),
-                            rhs_scale=scales[:, a * R : (a + 1) * R],
-                            start=(a == 0),
-                            stop=(a == PASSES - 1),
-                        )
+        mid = keep.tile([P, 5 * R], F32, name="picked1", align_bytes=64)
+        y_early = mid[:, :R].rearrange("p (q j) -> p q j", q=2)
+        gate34, up34 = mid[:, R : 3 * R], mid[:, 3 * R :]
+        y_sb = keep.tile([P, PAGES, J], F32, name="y_sb")
+        nc.scalar.copy(y_early[:, :, :CH], y0_ps[:, 2:, :])
+        nc.scalar.copy(y_early[:, :, CH:], y1_ps[:, 2:, :])
+        nc.scalar.copy(y_sb[:, :2, CH : 2 * CH], y1_ps[:, :2, :])
+        opening = keep.tile([P, 2 * CH], F32, name="opening")
+        weigh(nc.vector, opening[:], y0_ps[:, :2, :], 0)
+        for i in range(2):
+            factors(3 + i, gate34[:, i * R : (i + 1) * R], up34[:, i * R : (i + 1) * R])
+        nc.scalar.copy(y_sb[:, :, 2 * CH : 3 * CH], chunk_y(h2, 0, "t0")[:])
 
-        def paired(ap):
-            return ap.rearrange("p (u m e) -> p u m e", u=2, e=2)
-
-        def unpaired(bank):
-            return bank[:].rearrange("p (m u e) -> p u m e", u=2, e=2)
-
-        def relu(c):
-            if c == 0:
-                gate = borrowed(2, 2, R)
-            else:
-                gate = keep.tile([P, R], F32, name=f"slot{c % BANKS}", align_bytes=64)[:]
-            nc.scalar.activation(paired(gate), unpaired(sums[c][0]), RELU)
-            return gate
-
-        def gated(c, h_rows=None):
-            gate = relu(c)
-            if h_rows is None:
-                h_rows = ring.tile([P, R], BF16, name="h_rows")[:]
-            nc.vector.tensor_tensor(paired(h_rows), unpaired(sums[c][1]), paired(gate), MULT)
-            if c == 0:
-                gather_part(2, 3)
-                gather_part(2, 2)
-            return h_rows
-
-        def turn_h(c, h_rows):
-            quantize_h(c, turn(c, h_rows))
-
-        def turn(c, h_rows, h_woven=None):
-            pairs = h_rows.bitcast(F32)
-            t_ps = psum.tile([P, 2, CH], F32, name="t_ps", tag=f"t{c % 2}")
-            for u in range(2):
-                nc.tensor.transpose(t_ps[:, u, :], pairs[:, u * P : (u + 1) * P], ident[:])
-            if c == 0:
-                h_woven = borrowed(2, 0, CH * PACK // 2).bitcast(BF16)
-            elif h_woven is None:
-                h_woven = ring.tile([P, CH * PACK], BF16, name="h_woven", align_bytes=64)[:]
-            nc.scalar.copy(
-                h_woven.bitcast(F32).rearrange("p (j u) -> p j u", u=2), t_ps[:].rearrange("p u j -> p j u")
-            )
-            return h_woven
-
-        def quantize_h(c, h_woven):
-            if c == 0:
-                h_codes = keep.tile([P, CH], U32, name=f"shared{GROUPS[5][0]}", align_bytes=64)
-            else:
-                h_codes = ring.tile([P, CH], U32, name="h_codes", align_bytes=64)
-            h_scales = ring.tile([P, CH], U8, name="h_scales", align_bytes=64)
-            nc.vector.quantize_mx(out=h_codes[:].bitcast(FP8X4), scales=h_scales[:], in_=h_woven)
-            h_quant[c] = (h_codes[:], h_scales[:])
-            if c == 0:
-                gather_part(2, 1)
-                gather_part(2, 0)
-
-        def second_layer(first, end, q0, q1, bank):
-            h_codes, h_scales = h_quant[first]
-            y_ps = psum.tile([P, q1 - q0, (end - first) * CH], F32, name="y_ps", tag=bank)
-            for q in range(q0, q1):
-                nc.tensor.matmul_mx(
-                    y_ps[:, q - q0, :],
-                    lhsT=wd_w[:, 2 * P * q : 2 * P * (q + 1)].bitcast(FP4X4),
-                    lhsT_scale=wd_s[:, P * q : P * (q + 1)],
-                    rhs=h_codes.bitcast(FP8X4),
-                    rhs_scale=h_scales,
-                    start=True,
-                    stop=True,
-                )
-            return y_ps
-
-        def to_sbuf(y_ps, first, end, q0, q1, base=0):
-            nc.scalar.copy(y_sb[:, q0:q1, first * CH : end * CH], y_ps[:, q0 - base : q1 - base, :])
-
-        def quantize_pair(c, woven):
-            codes = keep.tile([P, 2 * CH], U32, name=f"pair_codes{c}", align_bytes=64)
-            scales = keep.tile([P, 2 * CH], U8, name=f"pair_scales{c}", align_bytes=64)
-            nc.vector.quantize_mx(out=codes[:].bitcast(FP8X4), scales=scales[:], in_=woven[:])
-            h_quant[c] = (codes[:], scales[:])
-
-        for piece in range(3):
-            last_plane(piece)
-        pass1(*GROUPS[0])
-        gather_part(1, 3)
-        gather_part(1, 2)
-        for group in GROUPS[1:3]:
-            pass1(*group)
-        first_layer(range(BANKS), (0,))
-        first_layer((0, 1), (1,))
-        turn_h(0, gated(0))
-        pass1(*GROUPS[3])
-        first_layer((2,), (1,))
-        first_layer((3,))
-        turn_h(1, gated(1))
-        y_ps = second_layer(0, 1, 0, PAGES, "t1")
-        to_sbuf(y_ps, 0, 1, 0, 1)
-        to_sbuf(y_ps, 0, 1, 1, PAGES)
-        for q in range(3):
-            scatter(q, 0, 1)
-        pass1(*GROUPS[4])
-        turn_h(2, gated(2))
-        to_sbuf(second_layer(1, 2, 0, PAGES, "t0"), 1, 2, 0, PAGES)
-        h_woven = keep.tile([P, CH * PACK], BF16, name="opening", align_bytes=64)
-        quantize_h(3, turn(3, gated(3), h_woven[:]))
-        first_layer((4,))
-        gate = relu(4)
-        pass1(*GROUPS[5])
-        first_layer((5,))
-        to_sbuf(second_layer(2, 3, 0, PAGES, "t1"), 2, 3, 0, PAGES)
-        to_sbuf(second_layer(3, 4, 0, 2, "t0"), 3, 4, 0, 2)
-
-        opening = keep.tile([P, 5 * CH], F32, name="opening", align_bytes=64)
-        h_rows = opening[:, : 2 * CH].bitcast(BF16)
-        nc.vector.tensor_tensor(paired(h_rows), unpaired(sums[4][1]), paired(gate), MULT)
-        first_window = opening[:, 2 * CH :]
-        weigh(first_window[:, :CH], 3, 4, 0, 1)
-        weigh(first_window[:, CH:], 2, 4, 1, 2)
-        mid_window = keep.tile([P, 8 * CH], F32, name=f"slot{4 % BANKS}", align_bytes=64)
-        weigh(mid_window[:, : 2 * CH], 2, 4, 2, 3)
-        weigh(mid_window[:, 2 * CH :], 0, 2, 1, 4)
-        nc.vector.tensor_copy(window(3, 0, 1), first_window[:, :CH])
-        for q in (2, 3):
-            nc.vector.tensor_copy(window(q, 1, 2), first_window[:, (q - 1) * CH : q * CH])
-        for q in (2, 3):
-            nc.vector.tensor_copy(window(q, 2, 3), mid_window[:, (q - 2) * CH : (q - 1) * CH])
+        burst = keep.tile([P, 10 * CH], F32, name=f"woven1_{HALF + QUARTER}", align_bytes=64)
+        weigh(nc.gpsimd, burst[:, : 4 * CH], y_early, 0)
+        weigh(nc.gpsimd, burst[:, 4 * CH : 6 * CH], y_sb[:, :2, CH : 2 * CH], CH)
+        woven34 = burst[:, 6 * CH :].bitcast(BF16)
+        nc.gpsimd.tensor_tensor(woven34, up34, gate34, MULT)
+        weighed2 = gate34[:, :R]
+        weigh(nc.gpsimd, weighed2, y_sb[:, :, 2 * CH : 3 * CH], 2 * CH)
         for q in range(2):
-            nc.vector.tensor_copy(window(q, 1, 4), mid_window[:, (2 + 3 * q) * CH : (5 + 3 * q) * CH])
-        pair_woven = [keep.tile([P, 2 * CH * PACK], BF16, name=f"pair_woven{c}", align_bytes=64) for c in (4, 6)]
-        turn(4, h_rows, pair_woven[0][:, : CH * PACK])
-        late_h = keep.tile([P, 3 * R], BF16, name="opening", align_bytes=64)
+            put(q, 0, 1, opening[:, q * CH : (q + 1) * CH])
+        for q in (2, 3):
+            put(q, 0, 2, burst[:, 2 * (q - 2) * CH : 2 * (q - 1) * CH])
+        for q in range(2):
+            put(q, 1, 2, burst[:, (4 + q) * CH : (5 + q) * CH])
+        h34 = quantize_h(3, 5, woven34)
+        for q in range(PAGES):
+            put(q, 2, 3, weighed2[:, q * CH : (q + 1) * CH])
+
+        late = keep.tile([P, 6 * R], F32, name="picked0")
+        gates, ups = late[:, : 3 * R], late[:, 3 * R :]
         for c in (5, 6, 7):
-            if c > 5:
-                first_layer((c,))
-            gate = keep.tile([P, R], F32, name=f"gate{c}", align_bytes=64)
-            nc.scalar.activation(paired(gate[:]), unpaired(sums[c][0]), RELU)
-            up = keep.tile([P, R], F32, name=f"up{c}", align_bytes=64)
-            nc.scalar.copy(paired(up[:]), unpaired(sums[c][1]))
-            nc.gpsimd.tensor_tensor(late_h[:, (c - 5) * R : (c - 4) * R], up[:], gate[:], MULT)
-        turn(5, late_h[:, :R], pair_woven[0][:, CH * PACK :])
-        quantize_pair(4, pair_woven[0])
-        to_sbuf(second_layer(3, 4, 2, PAGES, "t1"), 3, 4, 2, PAGES, 2)
-        for q in (2, 3):
-            scatter(q, 3, 4)
-        for c in (6, 7):
-            turn(c, late_h[:, (c - 5) * R : (c - 4) * R], pair_woven[1][:, (c - 6) * CH * PACK : (c - 5) * CH * PACK])
-        quantize_pair(6, pair_woven[1])
-        to_sbuf(second_layer(4, 6, 0, 1, "t0"), 4, 6, 0, 1)
-        to_sbuf(second_layer(4, 6, 1, 2, "t1"), 4, 6, 1, 2, 1)
-        to_sbuf(second_layer(6, 8, 0, 1, "g0"), 6, 8, 0, 1)
-        to_sbuf(second_layer(6, 8, 1, 2, "g2"), 6, 8, 1, 2, 1)
-        to_sbuf(second_layer(4, 6, 2, PAGES, "t0"), 4, 6, 2, PAGES, 2)
-        to_sbuf(second_layer(6, 8, 2, PAGES, "g1"), 6, 8, 2, PAGES, 2)
+            first_layer(c)
+            factors(c, gates[:, (c - 5) * R : (c - 4) * R], ups[:, (c - 5) * R : (c - 4) * R])
+
+        burst = keep.tile([P, 10 * CH], F32, name=f"woven1_{HALF + QUARTER}", align_bytes=64)
+        woven_end = burst[:, 4 * CH :].bitcast(BF16)
+        nc.gpsimd.tensor_tensor(woven_end[:, :R], ups[:, :R], gates[:, :R], MULT)
+        y3 = burst[:, 6 * CH :].rearrange("p (q j) -> p q j", q=PAGES)
+        nc.scalar.copy(y3, chunk_y(h34, 0, "t1")[:])
+        weigh(nc.gpsimd, burst[:, : 4 * CH], y3, 3 * CH)
+        nc.gpsimd.tensor_tensor(woven_end[:, R:], ups[:, R:], gates[:, R:], MULT)
+        for q in range(PAGES):
+            put(q, 3, 4, burst[:, q * CH : (q + 1) * CH])
+        h_end = quantize_h(5, 8, woven_end)
+        y4_ps = chunk_y(h34, CH, "t0")
+        nc.scalar.copy(y_sb[:, 2:, 4 * CH : 5 * CH], y4_ps[:, 2:, :])
+        y4 = ups[:, R : R + 2 * CH].rearrange("p (q j) -> p q j", q=2)
+        nc.scalar.copy(y4, y4_ps[:, :2, :])
         for q in range(2):
-            scatter(q, 4, 6)
-        for q, first in enumerate((6, 6, 4, 4)):
-            scatter(q, first, CHUNKS)
+            put_weighed(q, 4, 5, y4[:, q, :])
+        for q, bank in enumerate(("g0", "u0", "g1", "u1")):
+            y_ps = psum.tile([P, 3 * CH], F32, name="y_ps", tag=bank)
+            for lo, hi in ((0, CH), (CH, 3 * CH)):
+                second_layer(y_ps[:, lo:hi], q, h_end, lo, hi)
+            nc.scalar.copy(y_sb[:, q, 5 * CH :], y_ps[:])
+        for q, first in enumerate((5, 5, 4, 4)):
+            put_weighed(q, first, CHUNKS, y_sb[:, q, first * CH :])
             nc.sync.dma_start(out[q * P : (q + 1) * P, :], pages[q][:])

@@ -210,11 +210,14 @@ def tile_list_relu_scat_kernel(
                             stop=(a == PASSES - 1 and t == PACK - 1),
                         )
 
-        def by_pick(bank):
-            return bank[:].rearrange("p t j -> p j t")
+        def by_pairs(bank):
+            return bank[:].rearrange("p t (c i) -> p c t i", i=2)
+
+        def walk(ap):
+            return ap.rearrange("p (c t i) -> p c t i", t=PACK, i=2)
 
         def words(ap):
-            return ap.rearrange("p (j t) -> p j t", t=PACK)
+            return ap.rearrange("p (c i t) -> p c t i", t=PACK, i=2)
 
         def quantize_h(first, end, woven):
             codes = keep.tile([P, (end - first) * CH], U32, name=f"h_codes{first}", align_bytes=64)
@@ -242,17 +245,17 @@ def tile_list_relu_scat_kernel(
 
         def relu(c):
             gate = keep.tile([P, R], F32, name=f"gate{c}")
-            nc.scalar.activation(words(gate[:]), by_pick(sums[c][0]), RELU)
+            nc.scalar.activation(walk(gate[:]), by_pairs(sums[c][0]), RELU)
             return gate
 
         def vector_h(c, gate):
             woven = keep.tile([P, R], BF16, name=f"h_woven{c}", align_bytes=64)
-            nc.vector.tensor_tensor(words(woven[:]), by_pick(sums[c][1]), words(gate[:]), MULT)
+            nc.vector.tensor_tensor(words(woven[:]), by_pairs(sums[c][1]), walk(gate[:]), MULT)
             return quantize_h(c, c + 1, woven[:])
 
         def factors(c, gate, up):
-            nc.scalar.activation(words(gate), by_pick(sums[c][0]), RELU)
-            nc.scalar.copy(words(up), by_pick(sums[c][1]))
+            nc.scalar.activation(words(gate), by_pairs(sums[c][0]), RELU)
+            nc.scalar.copy(words(up), by_pairs(sums[c][1]))
 
         def weigh(engine, dst, src, j0):
             count, width = src.shape[1], src.shape[2]

@@ -292,59 +292,70 @@ def tile_list_relu_scat_kernel(
         y0_ps = chunk_y(h0, 0, "t0")
         y1_ps = chunk_y(h1, 0, "t1")
         pass1(third, HALF, HALF + QUARTER)
-        pass1(fourth, HALF + QUARTER, J)
         for c in (3, 4):
             first_layer(c)
 
-        mid = keep.tile([P, 5 * R], F32, name="picked1", align_bytes=64)
-        y_early = mid[:, :R].rearrange("p (q j) -> p q j", q=2)
-        gate34, up34 = mid[:, R : 3 * R], mid[:, 3 * R :]
+        y_early = third[:, :2, :]
+        factors34 = keep.tile([P, 4 * R], F32, name="factors34")
+        gate34, up34 = factors34[:, : 2 * R], factors34[:, 2 * R :]
         y_sb = keep.tile([P, PAGES, J], F32, name="y_sb")
         nc.scalar.copy(y_early[:, :, :CH], y0_ps[:, 2:, :])
         nc.scalar.copy(y_early[:, :, CH:], y1_ps[:, 2:, :])
-        nc.scalar.copy(y_sb[:, :2, CH : 2 * CH], y1_ps[:, :2, :])
+        between = keep.tile([P, R], F32, name="between", align_bytes=64)
+        y1 = between[:, : 2 * CH].rearrange("p (q j) -> p q j", q=2)
+        nc.scalar.copy(y1, y1_ps[:, :2, :])
         opening = keep.tile([P, 2 * CH], F32, name="opening")
         weigh(nc.vector, opening[:], y0_ps[:, :2, :], 0)
         for i in range(2):
             factors(3 + i, gate34[:, i * R : (i + 1) * R], up34[:, i * R : (i + 1) * R])
-        nc.scalar.copy(y_sb[:, :, 2 * CH : 3 * CH], chunk_y(h2, 0, "t0")[:])
 
-        burst = keep.tile([P, 10 * CH], F32, name=f"woven1_{HALF + QUARTER}", align_bytes=64)
+        burst = keep.tile([P, 10 * CH], F32, name=f"woven1_{HALF}", align_bytes=64)
         weigh(nc.gpsimd, burst[:, : 4 * CH], y_early, 0)
-        weigh(nc.gpsimd, burst[:, 4 * CH : 6 * CH], y_sb[:, :2, CH : 2 * CH], CH)
+        weigh(nc.gpsimd, burst[:, 4 * CH : 6 * CH], y1, CH)
+        woven67 = weave(fourth, between[:].bitcast(BF16))
+        y2 = fourth[:, :, :CH]
+        nc.scalar.copy(y2, chunk_y(h2, 0, "t0")[:])
         woven34 = burst[:, 6 * CH :].bitcast(BF16)
         nc.gpsimd.tensor_tensor(woven34, up34, gate34, MULT)
         weighed2 = gate34[:, :R]
-        weigh(nc.gpsimd, weighed2, y_sb[:, :, 2 * CH : 3 * CH], 2 * CH)
+        weigh(nc.gpsimd, weighed2, y2, 2 * CH)
         for q in range(2):
             put(q, 0, 1, opening[:, q * CH : (q + 1) * CH])
         for q in (2, 3):
             put(q, 0, 2, burst[:, 2 * (q - 2) * CH : 2 * (q - 1) * CH])
         for q in range(2):
             put(q, 1, 2, burst[:, (4 + q) * CH : (5 + q) * CH])
+        quantize_x(1, HALF + QUARTER, J, woven67)
         h34 = quantize_h(3, 5, woven34)
+        y3_ps = chunk_y(h34, 0, "t1")
         for q in range(PAGES):
             put(q, 2, 3, weighed2[:, q * CH : (q + 1) * CH])
 
         late = keep.tile([P, 6 * R], F32, name="picked0")
         gates, ups = late[:, : 3 * R], late[:, 3 * R :]
-        for c in (5, 6, 7):
+
+        def late_factors(c):
             first_layer(c)
             factors(c, gates[:, (c - 5) * R : (c - 4) * R], ups[:, (c - 5) * R : (c - 4) * R])
 
-        burst = keep.tile([P, 10 * CH], F32, name=f"woven1_{HALF + QUARTER}", align_bytes=64)
+        late_factors(5)
+
+        burst = keep.tile([P, 10 * CH], F32, name=f"woven1_{HALF}", align_bytes=64)
         woven_end = burst[:, 4 * CH :].bitcast(BF16)
         nc.gpsimd.tensor_tensor(woven_end[:, :R], ups[:, :R], gates[:, :R], MULT)
         y3 = burst[:, 6 * CH :].rearrange("p (q j) -> p q j", q=PAGES)
-        nc.scalar.copy(y3, chunk_y(h34, 0, "t1")[:])
+        nc.scalar.copy(y3, y3_ps[:])
         weigh(nc.gpsimd, burst[:, : 4 * CH], y3, 3 * CH)
-        nc.gpsimd.tensor_tensor(woven_end[:, R:], ups[:, R:], gates[:, R:], MULT)
+        for c in (6, 7):
+            late_factors(c)
+            part = slice((c - 5) * R, (c - 4) * R)
+            nc.gpsimd.tensor_tensor(woven_end[:, part], ups[:, part], gates[:, part], MULT)
         for q in range(PAGES):
             put(q, 3, 4, burst[:, q * CH : (q + 1) * CH])
         h_end = quantize_h(5, 8, woven_end)
         y4_ps = chunk_y(h34, CH, "t0")
         nc.scalar.copy(y_sb[:, 2:, 4 * CH : 5 * CH], y4_ps[:, 2:, :])
-        y4 = ups[:, R : R + 2 * CH].rearrange("p (q j) -> p q j", q=2)
+        y4 = ups[:, 2 * R : 2 * R + 2 * CH].rearrange("p (q j) -> p q j", q=2)
         nc.scalar.copy(y4, y4_ps[:, :2, :])
         for q in range(2):
             put_weighed(q, 4, 5, y4[:, q, :])

@@ -176,11 +176,11 @@ def tile_list_relu_scat_kernel(
 
         front = rows_from(3 * HALF)
         third = rows_from(0)[:, :, :QUARTER]
-        fourth = rows_from(3 * HALF - QUARTER)[:, :, :QUARTER]
+        fourth = rows_from(2 * HALF - QUARTER)[:, :, :QUARTER]
         for t in range(PACK - 1):
             gather(front[:, t, :], PACK + t, 0, HALF)
             gather(third[:, t, :], PACK + t, HALF, HALF + QUARTER)
-            if t == 0:
+            if t < 2:
                 gather(fourth[:, t, :], PACK + t, HALF + QUARTER, J)
         for j0, j1 in ((0, CH), (CH, 2 * CH), (2 * CH, HALF)):
             gather(front[:, PACK - 1, j0:j1], PLANES - 1, j0, j1)
@@ -285,7 +285,7 @@ def tile_list_relu_scat_kernel(
         first_layer(2, (1,))
         h0 = vector_h(0, relu(0))
         pass1(front[:, :, 3 * CH :], 3 * CH, HALF)
-        for t in (3, 2, 1):
+        for t in (3, 2):
             gather(fourth[:, t, :], PACK + t, HALF + QUARTER, J)
         h1 = vector_h(1, relu(1))
         h2 = vector_h(2, relu(2))

@@ -30,6 +30,7 @@ HEAD = 128
 HALF = J // 2
 QUARTER = J // 4
 BANKS = 3
+FRONT = 5 * CH
 
 
 def tile_list_relu_scat_kernel(
@@ -169,20 +170,20 @@ def tile_list_relu_scat_kernel(
                     raw_w[w][a][:].rearrange("p (m t) -> p t m", t=PACK),
                 )
 
-        picked1 = keep.tile([P, 7 * HALF], F32, name="picked1", align_bytes=64)
+        back_pitch = FRONT + 2 * CH
+        front_start = 2 * CH + 2 * back_pitch
+        picked1 = keep.tile([P, front_start + PACK * FRONT], F32, name="picked1", align_bytes=64)
 
-        def rows_from(start):
-            return picked1[:, start : start + PACK * HALF].rearrange("p (t j) -> p t j", t=PACK)
+        def rows_from(start, count, pitch, width):
+            return picked1[:, start : start + count * pitch].rearrange("p (t j) -> p t j", t=count)[:, :, :width]
 
-        front = rows_from(3 * HALF)
-        third = rows_from(0)[:, :, :QUARTER]
-        fourth = rows_from(2 * HALF - QUARTER)[:, :, :QUARTER]
+        back = rows_from(CH, PACK, back_pitch, J - FRONT)
+        front = rows_from(front_start, PACK, FRONT, FRONT)
         for t in range(PACK - 1):
-            gather(front[:, t, :], PACK + t, 0, HALF)
-            gather(third[:, t, :], PACK + t, HALF, HALF + QUARTER)
+            gather(front[:, t, :], PACK + t, 0, FRONT)
             if t < 2:
-                gather(fourth[:, t, :], PACK + t, HALF + QUARTER, J)
-        for j0, j1 in ((0, CH), (CH, 2 * CH), (2 * CH, HALF)):
+                gather(back[:, t, :], PACK + t, FRONT, J)
+        for j0, j1 in ((0, CH), (CH, 2 * CH), (2 * CH, FRONT)):
             gather(front[:, PACK - 1, j0:j1], PLANES - 1, j0, j1)
 
         def pass1(src, j0, j1):
@@ -248,10 +249,8 @@ def tile_list_relu_scat_kernel(
             nc.scalar.activation(walk(gate[:]), by_pairs(sums[c][0]), RELU)
             return gate
 
-        def vector_h(c, gate):
-            woven = keep.tile([P, R], BF16, name=f"h_woven{c}", align_bytes=64)
-            nc.vector.tensor_tensor(words(woven[:]), by_pairs(sums[c][1]), walk(gate[:]), MULT)
-            return quantize_h(c, c + 1, woven[:])
+        def vector_h(c, woven):
+            nc.vector.tensor_tensor(words(woven), by_pairs(sums[c][1]), walk(relu(c)[:]), MULT)
 
         def factors(c, gate, up):
             nc.scalar.activation(words(gate), by_pairs(sums[c][0]), RELU)
@@ -277,25 +276,30 @@ def tile_list_relu_scat_kernel(
 
         for c in range(BANKS):
             first_layer(c, (0,))
-        for c in range(2):
+        for c in range(BANKS):
             pass1(front[:, :, c * CH : (c + 1) * CH], c * CH, (c + 1) * CH)
             first_layer(c, (1,))
-        gather(third[:, PACK - 1, :], PLANES - 1, HALF, HALF + QUARTER)
-        pass1(front[:, :, 2 * CH : 3 * CH], 2 * CH, 3 * CH)
-        first_layer(2, (1,))
-        h0 = vector_h(0, relu(0))
-        pass1(front[:, :, 3 * CH :], 3 * CH, HALF)
-        for t in (3, 2):
-            gather(fourth[:, t, :], PACK + t, HALF + QUARTER, J)
-        h1 = vector_h(1, relu(1))
-        h2 = vector_h(2, relu(2))
+            if c == 1:
+                gather(back[:, 2, :], PACK + 2, FRONT, J)
+        woven_early = keep.tile([P, 3 * R], BF16, name="woven_early", align_bytes=64)
+        vector_h(0, woven_early[:, :R])
+        pass1(front[:, :, 3 * CH : 4 * CH], 3 * CH, 4 * CH)
+        gather(back[:, 3, :], PACK + 3, FRONT, J)
+        h0 = quantize_h(0, 1, woven_early[:, :R])
+        vector_h(1, woven_early[:, R : 2 * R])
+        h1 = quantize_h(1, 2, woven_early[:, R : 2 * R])
+        vector_h(2, woven_early[:, 2 * R :])
+        h2 = quantize_h(2, 3, woven_early[:, 2 * R :])
         y0_ps = chunk_y(h0, 0, "t0")
         y1_ps = chunk_y(h1, 0, "t1")
-        pass1(third, HALF, HALF + QUARTER)
+        woven45 = keep.tile([P, 2 * R], BF16, name="burst", align_bytes=64)
+        weave(front[:, :, 4 * CH :], woven45[:, :R])
+        weave(back[:, :, :CH], woven45[:, R:])
+        quantize_x(1, 4 * CH, 6 * CH, woven45[:])
         for c in (3, 4):
             first_layer(c)
 
-        y_early = third[:, :2, :]
+        y_early = rows_from(0, 2, back_pitch, 2 * CH)
         factors34 = keep.tile([P, 4 * R], F32, name="factors34")
         gate34, up34 = factors34[:, : 2 * R], factors34[:, 2 * R :]
         y_sb = keep.tile([P, PAGES, J], F32, name="y_sb")
@@ -309,11 +313,11 @@ def tile_list_relu_scat_kernel(
         for i in range(2):
             factors(3 + i, gate34[:, i * R : (i + 1) * R], up34[:, i * R : (i + 1) * R])
 
-        burst = keep.tile([P, 10 * CH], F32, name=f"woven1_{HALF}", align_bytes=64)
+        burst = keep.tile([P, 10 * CH], F32, name="burst", align_bytes=64)
         weigh(nc.gpsimd, burst[:, : 4 * CH], y_early, 0)
         weigh(nc.gpsimd, burst[:, 4 * CH : 6 * CH], y1, CH)
-        woven67 = weave(fourth, between[:].bitcast(BF16))
-        y2 = fourth[:, :, :CH]
+        woven67 = weave(back[:, :, CH:], between[:].bitcast(BF16))
+        y2 = back[:, :, CH : 2 * CH]
         nc.scalar.copy(y2, chunk_y(h2, 0, "t0")[:])
         woven34 = burst[:, 6 * CH :].bitcast(BF16)
         nc.gpsimd.tensor_tensor(woven34, up34, gate34, MULT)
@@ -340,7 +344,7 @@ def tile_list_relu_scat_kernel(
 
         late_factors(5)
 
-        burst = keep.tile([P, 10 * CH], F32, name=f"woven1_{HALF}", align_bytes=64)
+        burst = keep.tile([P, 10 * CH], F32, name="burst", align_bytes=64)
         woven_end = burst[:, 4 * CH :].bitcast(BF16)
         nc.gpsimd.tensor_tensor(woven_end[:, :R], ups[:, :R], gates[:, :R], MULT)
         y3 = burst[:, 6 * CH :].rearrange("p (q j) -> p q j", q=PAGES)

@@ -320,8 +320,9 @@ def tile_list_relu_scat_kernel(
         y2 = back[:, :, CH : 2 * CH]
         nc.scalar.copy(y2, chunk_y(h2, 0, "t0")[:])
         woven34 = burst[:, 6 * CH :].bitcast(BF16)
-        nc.gpsimd.tensor_tensor(woven34, up34, gate34, MULT)
-        weighed2 = gate34[:, :R]
+        for half in (slice(0, R), slice(R, 2 * R)):
+            nc.gpsimd.tensor_tensor(woven34[:, half], up34[:, half], gate34[:, half], MULT)
+        weighed2 = gate34[:, R:]
         weigh(nc.gpsimd, weighed2, y2, 2 * CH)
         for q in range(2):
             put(q, 0, 1, opening[:, q * CH : (q + 1) * CH])
@@ -331,7 +332,9 @@ def tile_list_relu_scat_kernel(
             put(q, 1, 2, burst[:, (4 + q) * CH : (5 + q) * CH])
         quantize_x(1, HALF + QUARTER, J, woven67)
         h34 = quantize_h(3, 5, woven34)
-        y3_ps = chunk_y(h34, 0, "t1")
+        y34_ps = [psum.tile([P, 2, 2 * CH], F32, name="y34_ps", tag=bank) for bank in ("t1", "t0")]
+        for q in range(PAGES):
+            second_layer(y34_ps[q // 2][:, q % 2, :], q, h34, 0, 2 * CH)
         for q in range(PAGES):
             put(q, 2, 3, weighed2[:, q * CH : (q + 1) * CH])
 
@@ -347,27 +350,25 @@ def tile_list_relu_scat_kernel(
         burst = keep.tile([P, 10 * CH], F32, name="burst", align_bytes=64)
         woven_end = burst[:, 4 * CH :].bitcast(BF16)
         nc.gpsimd.tensor_tensor(woven_end[:, :R], ups[:, :R], gates[:, :R], MULT)
-        y3 = burst[:, 6 * CH :].rearrange("p (q j) -> p q j", q=PAGES)
-        nc.scalar.copy(y3, y3_ps[:])
-        weigh(nc.gpsimd, burst[:, : 4 * CH], y3, 3 * CH)
+        y34 = burst[:, 6 * CH :].rearrange("p (q j) -> p q j", q=2)
+        nc.scalar.copy(y34, y34_ps[0][:])
+        weigh(nc.gpsimd, burst[:, : 4 * CH], y34, 3 * CH)
         for c in (6, 7):
             late_factors(c)
             part = slice((c - 5) * R, (c - 4) * R)
             nc.gpsimd.tensor_tensor(woven_end[:, part], ups[:, part], gates[:, part], MULT)
-        for q in range(PAGES):
-            put(q, 3, 4, burst[:, q * CH : (q + 1) * CH])
-        h_end = quantize_h(5, 8, woven_end)
-        y4_ps = chunk_y(h34, CH, "t0")
-        nc.scalar.copy(y_sb[:, 2:, 4 * CH : 5 * CH], y4_ps[:, 2:, :])
-        y4 = ups[:, 2 * R : 2 * R + 2 * CH].rearrange("p (q j) -> p q j", q=2)
-        nc.scalar.copy(y4, y4_ps[:, :2, :])
         for q in range(2):
-            put_weighed(q, 4, 5, y4[:, q, :])
+            put(q, 3, 5, burst[:, 2 * q * CH : 2 * (q + 1) * CH])
+        h_end = quantize_h(5, 8, woven_end)
+        nc.scalar.copy(y_sb[:, 3, 3 * CH : 5 * CH], y34_ps[1][:, 1, :])
+        filler = ups[:, 2 * R : 2 * R + 2 * CH]
+        nc.scalar.copy(filler, y34_ps[1][:, 0, :])
+        put_weighed(2, 3, 5, filler)
         for q, bank in enumerate(("g0", "u0", "g1", "u1")):
             y_ps = psum.tile([P, 3 * CH], F32, name="y_ps", tag=bank)
             for lo, hi in ((0, CH), (CH, 3 * CH)):
                 second_layer(y_ps[:, lo:hi], q, h_end, lo, hi)
             nc.scalar.copy(y_sb[:, q, 5 * CH :], y_ps[:])
-        for q, first in enumerate((5, 5, 4, 4)):
+        for q, first in enumerate((5, 5, 5, 3)):
             put_weighed(q, first, CHUNKS, y_sb[:, q, first * CH :])
             nc.sync.dma_start(out[q * P : (q + 1) * P, :], pages[q][:])

@@ -322,7 +322,7 @@ def tile_list_relu_scat_kernel(
         woven34 = burst[:, 6 * CH :].bitcast(BF16)
         for half in (slice(0, R), slice(R, 2 * R)):
             nc.gpsimd.tensor_tensor(woven34[:, half], up34[:, half], gate34[:, half], MULT)
-        weighed2 = gate34[:, R:]
+        weighed2 = keep.tile([P, PAGES * CH], F32, name="weighed2")[:]
         weigh(nc.gpsimd, weighed2, y2, 2 * CH)
         for q in range(2):
             put(q, 0, 1, opening[:, q * CH : (q + 1) * CH])
@@ -350,7 +350,7 @@ def tile_list_relu_scat_kernel(
         burst = keep.tile([P, 10 * CH], F32, name="burst", align_bytes=64)
         woven_end = burst[:, 4 * CH :].bitcast(BF16)
         nc.gpsimd.tensor_tensor(woven_end[:, :R], ups[:, :R], gates[:, :R], MULT)
-        y34 = burst[:, 6 * CH :].rearrange("p (q j) -> p q j", q=2)
+        y34 = y_sb[:, :2, 3 * CH : 5 * CH]
         nc.scalar.copy(y34, y34_ps[0][:])
         weigh(nc.gpsimd, burst[:, : 4 * CH], y34, 3 * CH)
         for c in (6, 7):

@@ -26,11 +26,9 @@ PAGES = N // P
 LANE = 16
 QUADRANT = 32
 SCALE_ROWS = 4
-HEAD = 128
 HALF = J // 2
-QUARTER = J // 4
 BANKS = 3
-FRONT = 5 * CH
+HEAD = 1
 
 
 def tile_list_relu_scat_kernel(
@@ -46,19 +44,17 @@ def tile_list_relu_scat_kernel(
         x_rows = xT.rearrange("(a p t) n -> a t p n", p=P, t=PACK)
         planes = [keep.tile([P, T], F32, name=f"plane{m}") for m in range(PLANES)]
         gain = keep.tile([P, J], F32, name="gain")
+        gain_out = keep.tile([P, J], F32, name="gain_out")
         raw_w = [[keep.tile([P, R], U16, name=f"raw_w{w}{a}") for a in range(PASSES)] for w in range(2)]
         w_words = [[keep.tile([P, 2 * R], U8, name=f"w_words{w}{a}", align_bytes=64) for a in range(PASSES)] for w in range(2)]
         w_scales = [keep.tile([P, PASSES * R], U8, name=f"w_scales{w}", align_bytes=64) for w in range(2)]
-        raw_s = keep.tile([P, R], U8, name="page1")
-        dealt_s = keep.tile([P, R], U8, name="dealt_s")
+        raw_s = keep.tile([P, R], U8, name="page0")
         wd_w = keep.tile([P, 2 * N], U8, name="wd_w", align_bytes=64)
         wd_s = keep.tile([P, N], U8, name="wd_s", align_bytes=64)
         ident = keep.tile([P, P], F32, name="ident")
+        blank = keep.tile([P, P], F32, name="blank")
+        rows = keep.tile([P, CH], F32, name="rows")
 
-        nc.vector.memset(raw_s[2 * QUADRANT :, :].bitcast(I32), 0)
-        for scales in (*w_scales, wd_s):
-            nc.vector.memset(scales[:].bitcast(I32), 0)
-        blank = keep.tile([P, P], F32, name="page0")
         nc.gpsimd.memset(blank[:], 0.0)
         nc.gpsimd.affine_select(
             out=ident[:],
@@ -69,25 +65,48 @@ def tile_list_relu_scat_kernel(
             pattern=[[-1, P]],
             channel_multiplier=1,
         )
-        pages = [keep.tile([P, T], F32, name="page0")]
-        nc.gpsimd.memset(pages[0][:], 0.0)
+        nc.vector.memset(raw_s[2 * QUADRANT :, :].bitcast(I32), 0)
+        for scales in (*w_scales, wd_s):
+            nc.vector.memset(scales[:].bitcast(I32), 0)
 
-        rows = keep.tile([P, CH], F32, name="rows")
         for w, weights in enumerate((wgt, wgo)):
             nc.sync.dma_start(
                 rows[w * P // 2 : (w + 1) * P // 2, :], weights.rearrange("p (h n) -> (p h) n", h=2)[:: LANE + 1]
             )
         nc.sync.dma_start(planes[0][:], x_rows[0, 0])
         nc.sync.dma_start(pick[:], offs)
-        nc.sync.dma_start(gain[:, :HEAD], wgt[:, :HEAD])
+        nc.sync.dma_start(gain[:, : HEAD * CH], wgt[:, : HEAD * CH])
         for w, dram_scales in enumerate((wg_scales, wu_scales)):
             nc.scalar.dma_start(
                 raw_s[QUADRANT * w : QUADRANT * (w + 1), :].bitcast(I32),
                 dram_scales.bitcast(I32).rearrange("a q n -> q a n"),
             )
+
+        dealt_s = keep.tile([P, R], U8, name="dealt_s")
         nc.vector.tensor_copy(
             dealt_s[:].rearrange("p (t m) -> p t m", t=PACK), raw_s[:].rearrange("p (m t) -> p t m", t=PACK)
         )
+        turned = psum.tile([P, P], F32, name="turned", tag="t0")
+        nc.tensor.transpose(turned[:], rows[:], ident[:])
+
+        def spread(w, dst, cuts, banks, names):
+            groups = turned[:, w * P // 2 : (w + 1) * P // 2].rearrange("p (g i) -> p i g", i=CHUNKS)
+            for i0, i1, bank, name in zip(cuts, cuts[1:], banks, names):
+                step = i1 - i0
+                wide = keep.tile([P, step, P], F32, name=name)
+                back = psum.tile([P, step, CH], F32, name="back", tag=bank)
+                nc.scalar.copy(
+                    wide[:].rearrange("p i (g r) -> p i g r", r=LANE),
+                    groups[:, i0:i1, :].unsqueeze(3).to_broadcast([P, step, P // LANE, LANE]),
+                )
+                for i in range(step):
+                    nc.tensor.transpose(back[:, i, :], wide[:, i, :], ident[:])
+                nc.scalar.copy(dst[:, i0 * CH : i1 * CH], back[:].rearrange("p i e -> p (i e)"))
+
+        spread(0, gain, (HEAD, CHUNKS // 2, CHUNKS), ("u0", "u1"), ("page1", "wide4"))
+        pages = [keep.tile([P, T], F32, name=f"page{q}") for q in range(2)]
+        for page in pages:
+            nc.gpsimd.memset(page[:], 0.0)
 
         def move_scales(w):
             for d in range(P // QUADRANT):
@@ -111,58 +130,45 @@ def tile_list_relu_scat_kernel(
         for d in range(P // QUADRANT):
             nc.sync.dma_start(wd_s[QUADRANT * d : QUADRANT * d + SCALE_ROWS, :].bitcast(I32), wd_rows[d])
 
-        turned = psum.tile([P, P], F32, name="turned", tag="t0")
-        nc.tensor.transpose(turned[:], rows[:], ident[:])
-        pages.append(keep.tile([P, T], F32, name="page1"))
-        nc.gpsimd.memset(pages[1][:], 0.0)
+        def gather(dst, m, c0, c1):
+            nc.vector.tensor_tensor(
+                dst, planes[m][:].indirect(pick[:, c0 * CH // LANE : c1 * CH // LANE]), gain[:, c0 * CH : c1 * CH], MULT
+            )
 
-        def spread(w, dst, cuts, banks):
-            groups = turned[:, w * P // 2 : (w + 1) * P // 2].rearrange("p (g i) -> p i g", i=CHUNKS)
-            for i0, i1, bank in zip(cuts, cuts[1:], banks):
-                step = i1 - i0
-                wide = keep.tile([P, step, P], F32, name=f"wide{i0}")
-                back = psum.tile([P, step, CH], F32, name="back", tag=bank)
-                nc.scalar.copy(
-                    wide[:].rearrange("p i (g r) -> p i g r", r=LANE),
-                    groups[:, i0 : i0 + step, :].unsqueeze(3).to_broadcast([P, step, P // LANE, LANE]),
-                )
-                for i in range(step):
-                    nc.tensor.transpose(back[:, i, :], wide[:, i, :], ident[:])
-                nc.scalar.copy(dst[:, i0 * CH : (i0 + step) * CH], back[:].rearrange("p i e -> p (i e)"))
-
-        spread(0, gain, (1, 4, 8), ("u0", "u1"))
-
-        x_codes = [keep.tile([P, J], U32, name=f"x_codes{a}", align_bytes=64) for a in range(PASSES)]
-        x_scales = [keep.tile([P, J], U8, name=f"x_scales{a}", align_bytes=64) for a in range(PASSES)]
-
-        def gather(dst, m, j0, j1):
-            nc.vector.tensor_tensor(dst, planes[m][:].indirect(pick[:, j0 // LANE : j1 // LANE]), gain[:, j0:j1], MULT)
-
-        def weave(src, woven):
+        def weave(woven, picked, c0, c1):
             nc.scalar.copy(
                 woven.rearrange("p (c i t) -> p c t i", i=4, t=PACK),
-                src.rearrange("p t (c i) -> p c t i", i=4),
+                picked[:, :, c0 * CH : c1 * CH].rearrange("p t (c i) -> p c t i", i=4),
             )
-            return woven
 
-        def quantize_x(a, j0, j1, woven):
-            nc.vector.quantize_mx(out=x_codes[a][:, j0:j1].bitcast(FP8X4), scales=x_scales[a][:, j0:j1], in_=woven)
+        quantised = {}
+
+        def quantize(kind, c0, c1, woven, codes_name=None):
+            codes = keep.tile([P, (c1 - c0) * CH], U32, name=codes_name or f"{kind}_codes{c0}", align_bytes=64)
+            scales = keep.tile([P, (c1 - c0) * CH], U8, name=f"{kind}_scales{c0}", align_bytes=64)
+            nc.vector.quantize_mx(out=codes[:].bitcast(FP8X4), scales=scales[:], in_=woven)
+            for c in range(c0, c1):
+                quantised[kind, c] = (codes, scales, (c - c0) * CH)
+
+        def moving(kind, c0, c1):
+            codes, scales, lo = quantised[kind, c0]
+            cols = slice(lo, lo + (c1 - c0) * CH)
+            return dict(rhs=codes[:, cols].bitcast(FP8X4), rhs_scale=scales[:, cols])
 
         picked0 = keep.tile([P, PACK, J], F32, name="picked0")
-        for j0, j1 in ((0, HEAD), (HEAD, HALF), (HALF, J)):
-            gather(picked0[:, 0, j0:j1], 0, j0, j1)
+        for c0, c1 in ((0, HEAD), (HEAD, CHUNKS // 2), (CHUNKS // 2, CHUNKS)):
+            gather(picked0[:, 0, c0 * CH : c1 * CH], 0, c0, c1)
         for t in range(1, PACK - 1):
-            gather(picked0[:, t, :], t, 0, J)
-        for j0 in range(0, J, HALF):
-            gather(picked0[:, PACK - 1, j0 : j0 + HALF], PACK - 1, j0, j0 + HALF)
+            gather(picked0[:, t, :], t, 0, CHUNKS)
+        for h in range(2):
+            gather(picked0[:, PACK - 1, h * HALF : (h + 1) * HALF], PACK - 1, h * CHUNKS // 2, (h + 1) * CHUNKS // 2)
+        spread(1, gain_out, (0, CHUNKS // 2, CHUNKS), ("g0", "g1"), ("wide0", "wide4"))
         for q in range(2, PAGES):
             pages.append(keep.tile([P, T], F32, name=f"plane{q - 2}"))
             nc.gpsimd.memset(pages[q][:], 0.0)
-        gain_out = keep.tile([P, J], F32, name="gain_out")
-        spread(1, gain_out, (0, 4, 8), ("g0", "g1"))
-        for j0 in range(0, J, HALF):
-            woven0 = keep.tile([P, HALF * PACK], BF16, name=f"woven0_{j0}", align_bytes=64)
-            quantize_x(0, j0, j0 + HALF, weave(picked0[:, :, j0 : j0 + HALF], woven0[:]))
+        woven0 = [keep.tile([P, HALF * PACK], BF16, name=f"woven0_{h}", align_bytes=64) for h in range(2)]
+        for h in range(2):
+            weave(woven0[h][:], picked0[:], h * CHUNKS // 2, (h + 1) * CHUNKS // 2)
         for a in range(PASSES):
             for w in range(2):
                 nc.scalar.copy(
@@ -170,25 +176,11 @@ def tile_list_relu_scat_kernel(
                     raw_w[w][a][:].rearrange("p (m t) -> p t m", t=PACK),
                 )
 
-        back_pitch = FRONT + 2 * CH
-        front_start = 2 * CH + 2 * back_pitch
-        picked1 = keep.tile([P, front_start + PACK * FRONT], F32, name="picked1", align_bytes=64)
-
-        def rows_from(start, count, pitch, width):
-            return picked1[:, start : start + count * pitch].rearrange("p (t j) -> p t j", t=count)[:, :, :width]
-
-        back = rows_from(CH, PACK, back_pitch, J - FRONT)
-        front = rows_from(front_start, PACK, FRONT, FRONT)
+        picked1_flat = keep.tile([P, PACK * J], F32, name="picked1", align_bytes=64)
+        picked1 = picked1_flat[:].rearrange("p (t j) -> p t j", t=PACK)
         for t in range(PACK - 1):
-            gather(front[:, t, :], PACK + t, 0, FRONT)
-            if t < 2:
-                gather(back[:, t, :], PACK + t, FRONT, J)
-        for j0, j1 in ((0, CH), (CH, 2 * CH), (2 * CH, FRONT)):
-            gather(front[:, PACK - 1, j0:j1], PLANES - 1, j0, j1)
-
-        def pass1(src, j0, j1):
-            woven = keep.tile([P, (j1 - j0) * PACK], BF16, name=f"woven1_{j0}", align_bytes=64)
-            quantize_x(1, j0, j1, weave(src, woven[:]))
+            gather(picked1[:, t, :], PACK + t, 0, CHUNKS)
+        quantize("x0", 0, CHUNKS // 2, woven0[0][:])
 
         sums = {}
 
@@ -197,7 +189,6 @@ def tile_list_relu_scat_kernel(
                 g_ps = psum.tile([P, PACK, CH], F32, name="g_ps", tag=f"g{c % BANKS}")
                 u_ps = psum.tile([P, PACK, CH], F32, name="u_ps", tag=f"u{c % BANKS}")
                 sums[c] = (g_ps, u_ps)
-            cols = slice(c * CH, (c + 1) * CH)
             for a in passes:
                 for w in range(2):
                     for t in range(PACK):
@@ -205,10 +196,9 @@ def tile_list_relu_scat_kernel(
                             sums[c][w][:, t, :],
                             lhsT=w_words[w][a][:, 2 * P * t : 2 * P * (t + 1)].bitcast(FP4X4),
                             lhsT_scale=w_scales[w][:, a * R + P * t : a * R + P * (t + 1)],
-                            rhs=x_codes[a][:, cols].bitcast(FP8X4),
-                            rhs_scale=x_scales[a][:, cols],
                             start=(a == 0 and t == 0),
                             stop=(a == PASSES - 1 and t == PACK - 1),
+                            **moving(f"x{a}", c, c + 1),
                         )
 
         def by_pairs(bank):
@@ -220,155 +210,156 @@ def tile_list_relu_scat_kernel(
         def words(ap):
             return ap.rearrange("p (c i t) -> p c t i", t=PACK, i=2)
 
-        def quantize_h(first, end, woven):
-            codes = keep.tile([P, (end - first) * CH], U32, name=f"h_codes{first}", align_bytes=64)
-            scales = keep.tile([P, (end - first) * CH], U8, name=f"h_scales{first}", align_bytes=64)
-            nc.vector.quantize_mx(out=codes[:].bitcast(FP8X4), scales=scales[:], in_=woven)
-            return codes, scales
-
-        def second_layer(dst, q, quantised, lo, hi):
-            codes, scales = quantised
+        def second_layer(dst, q, c0, c1):
             nc.tensor.matmul_mx(
                 dst,
                 lhsT=wd_w[:, 2 * P * q : 2 * P * (q + 1)].bitcast(FP4X4),
                 lhsT_scale=wd_s[:, P * q : P * (q + 1)],
-                rhs=codes[:, lo:hi].bitcast(FP8X4),
-                rhs_scale=scales[:, lo:hi],
                 start=True,
                 stop=True,
+                **moving("h", c0, c1),
             )
 
-        def chunk_y(quantised, lo, bank):
+        def chunk_y(c, bank):
             y_ps = psum.tile([P, PAGES, CH], F32, name="y_ps", tag=bank)
             for q in range(PAGES):
-                second_layer(y_ps[:, q, :], q, quantised, lo, lo + CH)
+                second_layer(y_ps[:, q, :], q, c, c + 1)
             return y_ps
 
-        def relu(c):
-            gate = keep.tile([P, R], F32, name=f"gate{c}")
-            nc.scalar.activation(walk(gate[:]), by_pairs(sums[c][0]), RELU)
-            return gate
-
         def vector_h(c, woven):
-            nc.vector.tensor_tensor(words(woven), by_pairs(sums[c][1]), walk(relu(c)[:]), MULT)
+            gate = keep.tile([P, R], F32, name=f"gate{c}", align_bytes=64)
+            nc.scalar.activation(walk(gate[:]), by_pairs(sums[c][0]), RELU)
+            nc.vector.tensor_tensor(words(woven), by_pairs(sums[c][1]), walk(gate[:]), MULT)
 
-        def factors(c, gate, up):
-            nc.scalar.activation(words(gate), by_pairs(sums[c][0]), RELU)
-            nc.scalar.copy(words(up), by_pairs(sums[c][1]))
+        def factors(c, both):
+            nc.scalar.activation(words(both[:, :R]), by_pairs(sums[c][0]), RELU)
+            nc.scalar.copy(words(both[:, R:]), by_pairs(sums[c][1]))
 
-        def weigh(engine, dst, src, j0):
+        def gpsimd_h(both, woven):
+            nc.gpsimd.tensor_tensor(woven, both[:, R:], both[:, :R], MULT)
+
+        def weigh(engine, dst, src, c0):
             count, width = src.shape[1], src.shape[2]
             engine.tensor_tensor(
                 dst.rearrange("p (q j) -> p q j", q=count),
                 src,
-                gain_out[:, j0 : j0 + width].unsqueeze(1).to_broadcast([P, count, width]),
+                gain_out[:, c0 * CH : c0 * CH + width].unsqueeze(1).to_broadcast([P, count, width]),
                 MULT,
             )
 
-        def window(q, first, end):
-            return pages[q][:].indirect(place[:, first * CH // LANE : end * CH // LANE])
+        def window(q, c0, c1):
+            return pages[q][:].indirect(place[:, c0 * CH // LANE : c1 * CH // LANE])
 
-        def put(q, first, end, src):
-            nc.vector.tensor_copy(window(q, first, end), src)
+        def put(q, c0, c1, src):
+            nc.vector.tensor_copy(window(q, c0, c1), src)
 
-        def put_weighed(q, first, end, src):
-            nc.vector.tensor_tensor(window(q, first, end), src, gain_out[:, first * CH : end * CH], MULT)
+        def put_weighed(q, c0, c1, src):
+            nc.vector.tensor_tensor(window(q, c0, c1), src, gain_out[:, c0 * CH : c1 * CH], MULT)
+
+        def paged(ap, count):
+            return ap.rearrange("p (q j) -> p q j", q=count)
 
         for c in range(BANKS):
             first_layer(c, (0,))
-        for c in range(BANKS):
-            pass1(front[:, :, c * CH : (c + 1) * CH], c * CH, (c + 1) * CH)
+        last = picked1[:, PACK - 1, :]
+        gather(last[:, :CH], PLANES - 1, 0, 1)
+        gather(last[:, CH : 3 * CH], PLANES - 1, 1, 3)
+        woven1_0 = last[:, 3 * CH : 5 * CH].bitcast(BF16)
+        weave(woven1_0, picked1, 0, 1)
+        quantize("x1", 0, 1, woven1_0)
+        first_layer(0, (1,))
+        gather(last[:, 3 * CH :], PLANES - 1, 3, CHUNKS)
+        woven1_12 = keep.tile([P, 2 * R], BF16, name="woven1_12", align_bytes=64)
+        for c in (1, 2):
+            weave(woven1_12[:, (c - 1) * R : c * R], picked1, c, c + 1)
+        quantize("x1", 1, 3, woven1_12[:])
+        for c in (1, 2):
             first_layer(c, (1,))
-            if c == 1:
-                gather(back[:, 2, :], PACK + 2, FRONT, J)
-        woven_early = keep.tile([P, 3 * R], BF16, name="woven_early", align_bytes=64)
-        vector_h(0, woven_early[:, :R])
-        pass1(front[:, :, 3 * CH : 4 * CH], 3 * CH, 4 * CH)
-        gather(back[:, 3, :], PACK + 3, FRONT, J)
-        h0 = quantize_h(0, 1, woven_early[:, :R])
-        vector_h(1, woven_early[:, R : 2 * R])
-        h1 = quantize_h(1, 2, woven_early[:, R : 2 * R])
-        vector_h(2, woven_early[:, 2 * R :])
-        h2 = quantize_h(2, 3, woven_early[:, 2 * R :])
-        y0_ps = chunk_y(h0, 0, "t0")
-        y1_ps = chunk_y(h1, 0, "t1")
-        woven45 = keep.tile([P, 2 * R], BF16, name="burst", align_bytes=64)
-        weave(front[:, :, 4 * CH :], woven45[:, :R])
-        weave(back[:, :, :CH], woven45[:, R:])
-        quantize_x(1, 4 * CH, 6 * CH, woven45[:])
-        for c in (3, 4):
-            first_layer(c)
+        woven_h0 = keep.tile([P, R], BF16, name="woven_h0", align_bytes=64)
+        vector_h(0, woven_h0[:])
+        woven1_3 = keep.tile([P, R], BF16, name="woven1_3", align_bytes=64)
+        weave(woven1_3[:], picked1, 3, 4)
+        quantize("x1", 3, 4, woven1_3[:])
+        quantize("h", 0, 1, woven_h0[:])
+        quantize("x0", CHUNKS // 2, CHUNKS, woven0[1][:], codes_name="gate0")
+        y0_ps = chunk_y(0, "t0")
 
-        y_early = rows_from(0, 2, back_pitch, 2 * CH)
-        factors34 = keep.tile([P, 4 * R], F32, name="factors34")
-        gate34, up34 = factors34[:, : 2 * R], factors34[:, 2 * R :]
-        y_sb = keep.tile([P, PAGES, J], F32, name="y_sb")
-        nc.scalar.copy(y_early[:, :, :CH], y0_ps[:, 2:, :])
-        nc.scalar.copy(y_early[:, :, CH:], y1_ps[:, 2:, :])
-        between = keep.tile([P, R], F32, name="between", align_bytes=64)
-        y1 = between[:, : 2 * CH].rearrange("p (q j) -> p q j", q=2)
-        nc.scalar.copy(y1, y1_ps[:, :2, :])
-        opening = keep.tile([P, 2 * CH], F32, name="opening")
-        weigh(nc.vector, opening[:], y0_ps[:, :2, :], 0)
-        for i in range(2):
-            factors(3 + i, gate34[:, i * R : (i + 1) * R], up34[:, i * R : (i + 1) * R])
+        opening = keep.tile([P, 4 * R], BF16, name="burst1", align_bytes=64)
+        woven_h12, woven1_45 = opening[:, : 2 * R], opening[:, 2 * R :]
+        for c in (1, 2):
+            vector_h(c, woven_h12[:, (c - 1) * R : c * R])
+        for c in (4, 5):
+            weave(woven1_45[:, (c - 4) * R : (c - 3) * R], picked1, c, c + 1)
+        quantize("x1", 4, 6, woven1_45)
+        quantize("h", 1, 3, woven_h12)
+        y0b = keep.tile([P, 2, CH], F32, name="y0b")
+        nc.scalar.copy(y0b[:], y0_ps[:, 2:, :])
+        weighed0 = keep.tile([P, R], F32, name="burst1", align_bytes=64)
+        weigh(nc.vector, weighed0[:, : 2 * CH], y0_ps[:, :2, :], 0)
+        y1 = keep.tile([P, R], F32, name="y1", align_bytes=64)
+        nc.scalar.copy(paged(y1[:], PAGES), chunk_y(1, "t1")[:])
+        first_layer(3)
+        factors3 = keep.tile([P, 2 * R], F32, name="factors3")
+        factors(3, factors3)
+        y2_ps = chunk_y(2, "t0")
+        first_layer(4)
+        y2 = keep.tile([P, PAGES, CH], F32, name="y2")
+        nc.scalar.copy(y2[:], y2_ps[:])
+        factors4 = keep.tile([P, 2 * R], F32, name="factors4")
+        factors(4, factors4)
 
-        burst = keep.tile([P, 10 * CH], F32, name="burst", align_bytes=64)
-        weigh(nc.gpsimd, burst[:, : 4 * CH], y_early, 0)
-        weigh(nc.gpsimd, burst[:, 4 * CH : 6 * CH], y1, CH)
-        woven67 = weave(back[:, :, CH:], between[:].bitcast(BF16))
-        y2 = back[:, :, CH : 2 * CH]
-        nc.scalar.copy(y2, chunk_y(h2, 0, "t0")[:])
-        woven34 = burst[:, 6 * CH :].bitcast(BF16)
-        for half in (slice(0, R), slice(R, 2 * R)):
-            nc.gpsimd.tensor_tensor(woven34[:, half], up34[:, half], gate34[:, half], MULT)
-        weighed2 = keep.tile([P, PAGES * CH], F32, name="weighed2")[:]
-        weigh(nc.gpsimd, weighed2, y2, 2 * CH)
-        for q in range(2):
-            put(q, 0, 1, opening[:, q * CH : (q + 1) * CH])
-        for q in (2, 3):
-            put(q, 0, 2, burst[:, 2 * (q - 2) * CH : 2 * (q - 1) * CH])
-        for q in range(2):
-            put(q, 1, 2, burst[:, (4 + q) * CH : (5 + q) * CH])
-        quantize_x(1, HALF + QUARTER, J, woven67)
-        h34 = quantize_h(3, 5, woven34)
+        weigh(nc.gpsimd, weighed0[:, 2 * CH :], y0b[:], 0)
+        weighed1 = keep.tile([P, R], F32, name="weighed1")
+        weigh(nc.gpsimd, weighed1[:], paged(y1[:], PAGES), 1)
+        between = keep.tile([P, 4 * R], BF16, name="y1", align_bytes=64)
+        woven_h34, woven1_67 = between[:, : 2 * R], between[:, 2 * R :]
+        gpsimd_h(factors3, woven_h34[:, :R])
+        weighed2a = keep.tile([P, CH], F32, name="weighed2a", align_bytes=64)
+        weigh(nc.gpsimd, weighed2a[:], y2[:, :1, :], 2)
+        gpsimd_h(factors4, woven_h34[:, R:])
+        weighed2b = keep.tile([P, 3 * CH], F32, name="factors4")
+        weigh(nc.gpsimd, weighed2b[:], y2[:, 1:, :], 2)
+        weave(woven1_67, picked1, 6, 8)
+        for q in range(PAGES):
+            put(q, 0, 1, weighed0[:, q * CH : (q + 1) * CH])
+        for q in range(PAGES):
+            put(q, 1, 2, weighed1[:, q * CH : (q + 1) * CH])
+        put(0, 2, 3, weighed2a[:])
+        quantize("h", 3, 5, woven_h34)
+        quantize("x1", 6, 8, woven1_67, codes_name="weighed2a")
         y34_ps = [psum.tile([P, 2, 2 * CH], F32, name="y34_ps", tag=bank) for bank in ("t1", "t0")]
         for q in range(PAGES):
-            second_layer(y34_ps[q // 2][:, q % 2, :], q, h34, 0, 2 * CH)
-        for q in range(PAGES):
-            put(q, 2, 3, weighed2[:, q * CH : (q + 1) * CH])
+            second_layer(y34_ps[q // 2][:, q % 2, :], q, 3, 5)
+        for q in range(1, PAGES):
+            put(q, 2, 3, weighed2b[:, (q - 1) * CH : q * CH])
 
-        late = keep.tile([P, 6 * R], F32, name="picked0")
-        gates, ups = late[:, : 3 * R], late[:, 3 * R :]
-
-        def late_factors(c):
-            first_layer(c)
-            factors(c, gates[:, (c - 5) * R : (c - 4) * R], ups[:, (c - 5) * R : (c - 4) * R])
-
-        late_factors(5)
-
-        burst = keep.tile([P, 10 * CH], F32, name="burst", align_bytes=64)
-        woven_end = burst[:, 4 * CH :].bitcast(BF16)
-        nc.gpsimd.tensor_tensor(woven_end[:, :R], ups[:, :R], gates[:, :R], MULT)
-        y34 = y_sb[:, :2, 3 * CH : 5 * CH]
-        nc.scalar.copy(y34, y34_ps[0][:])
-        weigh(nc.gpsimd, burst[:, : 4 * CH], y34, 3 * CH)
+        late = keep.tile([P, 3, 2 * R], F32, name="picked0")
+        first_layer(5)
+        factors(5, late[:, 0, :])
+        woven_end = keep.tile([P, 3 * R], BF16, name="y1", align_bytes=64)
+        gpsimd_h(late[:, 0, :], woven_end[:, :R])
+        y34 = keep.tile([P, 3, 2 * CH], F32, name="y34")
+        weighed34 = keep.tile([P, 3, 2 * CH], F32, name="weighed34")
+        nc.scalar.copy(y34[:, :2, :], y34_ps[0][:])
+        nc.scalar.copy(y34[:, 2, :], y34_ps[1][:, 0, :])
+        for q in range(3):
+            weigh(nc.gpsimd, weighed34[:, q, :], y34[:, q : q + 1, :], 3)
         for c in (6, 7):
-            late_factors(c)
-            part = slice((c - 5) * R, (c - 4) * R)
-            nc.gpsimd.tensor_tensor(woven_end[:, part], ups[:, part], gates[:, part], MULT)
-        for q in range(2):
-            put(q, 3, 5, burst[:, 2 * q * CH : 2 * (q + 1) * CH])
-        h_end = quantize_h(5, 8, woven_end)
-        nc.scalar.copy(y_sb[:, 3, 3 * CH : 5 * CH], y34_ps[1][:, 1, :])
-        filler = ups[:, 2 * R : 2 * R + 2 * CH]
-        nc.scalar.copy(filler, y34_ps[1][:, 0, :])
-        put_weighed(2, 3, 5, filler)
+            first_layer(c)
+            factors(c, late[:, c - 5, :])
+            gpsimd_h(late[:, c - 5, :], woven_end[:, (c - 5) * R : (c - 4) * R])
+        for q in range(3):
+            put(q, 3, 5, weighed34[:, q, :])
+        quantize("h", 5, 8, woven_end[:])
+        filler = late[:, 2, : 2 * CH]
+        nc.scalar.copy(filler, y34_ps[1][:, 1, :])
+        put_weighed(3, 3, 5, filler)
+        y_end = keep.tile([P, PAGES, 3 * CH], F32, name="y_end")
         for q, bank in enumerate(("g0", "u0", "g1", "u1")):
             y_ps = psum.tile([P, 3 * CH], F32, name="y_ps", tag=bank)
-            for lo, hi in ((0, CH), (CH, 3 * CH)):
-                second_layer(y_ps[:, lo:hi], q, h_end, lo, hi)
-            nc.scalar.copy(y_sb[:, q, 5 * CH :], y_ps[:])
-        for q, first in enumerate((5, 5, 5, 3)):
-            put_weighed(q, first, CHUNKS, y_sb[:, q, first * CH :])
+            second_layer(y_ps[:, :CH], q, 5, 6)
+            second_layer(y_ps[:, CH:], q, 6, 8)
+            nc.scalar.copy(y_end[:, q, :], y_ps[:])
+        for q in range(PAGES):
+            put_weighed(q, 5, CHUNKS, y_end[:, q, :])
             nc.sync.dma_start(out[q * P : (q + 1) * P, :], pages[q][:])

@@ -29,6 +29,7 @@ SCALE_ROWS = 4
 HALF = J // 2
 BANKS = 3
 HEAD = 1
+WORDS_BEHIND = {2: (0, 1), 3: (1, 1), 4: (0, 0), 5: (1, 0)}
 
 
 def tile_list_relu_scat_kernel(
@@ -121,9 +122,9 @@ def tile_list_relu_scat_kernel(
             nc.sync.dma_start(planes[m][:], x_rows[m // PACK, m % PACK])
             if m in (1, 2):
                 move_scales(m - 1)
-            if m in (5, 6):
-                for w, dram_words in enumerate((wg_words, wu_words)):
-                    nc.sync.dma_start(raw_w[w][m - 5][:].bitcast(I32), dram_words[m - 5].bitcast(I32))
+            if m in WORDS_BEHIND:
+                w, a = WORDS_BEHIND[m]
+                nc.sync.dma_start(raw_w[w][a][:].bitcast(I32), (wg_words, wu_words)[w][a].bitcast(I32))
         nc.sync.dma_start(place[:], offs2)
         nc.sync.dma_start(wd_w[:].bitcast(I32), wd_words[0].bitcast(I32))
         wd_rows = wd_scales.bitcast(I32).rearrange("a (d r) n -> d r (a n)", r=SCALE_ROWS)
@@ -135,10 +136,10 @@ def tile_list_relu_scat_kernel(
                 dst, planes[m][:].indirect(pick[:, c0 * CH // LANE : c1 * CH // LANE]), gain[:, c0 * CH : c1 * CH], MULT
             )
 
-        def weave(woven, picked, c0, c1):
+        def weave(woven, picked, c0, c1, t0=0, t1=PACK):
             nc.scalar.copy(
-                woven.rearrange("p (c i t) -> p c t i", i=4, t=PACK),
-                picked[:, :, c0 * CH : c1 * CH].rearrange("p t (c i) -> p c t i", i=4),
+                woven.rearrange("p (c i t) -> p c t i", i=4, t=PACK)[:, :, t0:t1, :],
+                picked[:, t0:t1, c0 * CH : c1 * CH].rearrange("p t (c i) -> p c t i", i=4),
             )
 
         quantised = {}
@@ -169,28 +170,27 @@ def tile_list_relu_scat_kernel(
         woven0 = [keep.tile([P, HALF * PACK], BF16, name=f"woven0_{h}", align_bytes=64) for h in range(2)]
         for h in range(2):
             weave(woven0[h][:], picked0[:], h * CHUNKS // 2, (h + 1) * CHUNKS // 2)
-        for a in range(PASSES):
-            for w in range(2):
-                nc.scalar.copy(
-                    w_words[w][a][:].bitcast(U16).rearrange("p (t m) -> p t m", t=PACK),
-                    raw_w[w][a][:].rearrange("p (m t) -> p t m", t=PACK),
-                )
+        for w, a in [WORDS_BEHIND[m] for m in sorted(WORDS_BEHIND)]:
+            nc.scalar.copy(
+                w_words[w][a][:].bitcast(U16).rearrange("p (t m) -> p t m", t=PACK),
+                raw_w[w][a][:].rearrange("p (m t) -> p t m", t=PACK),
+            )
 
-        picked1_flat = keep.tile([P, PACK * J], F32, name="picked1", align_bytes=64)
-        picked1 = picked1_flat[:].rearrange("p (t j) -> p t j", t=PACK)
+        picked1_flat = keep.tile([P, PACK * J + 5 * CH], F32, name="picked1")
+        picked1 = picked1_flat[:, : PACK * J].rearrange("p (t j) -> p t j", t=PACK)
         for t in range(PACK - 1):
             gather(picked1[:, t, :], PACK + t, 0, CHUNKS)
         quantize("x0", 0, CHUNKS // 2, woven0[0][:])
 
         sums = {}
 
-        def first_layer(c, passes=range(PASSES)):
+        def first_layer(c, passes=range(PASSES), sides=range(2)):
             if 0 in passes:
                 g_ps = psum.tile([P, PACK, CH], F32, name="g_ps", tag=f"g{c % BANKS}")
                 u_ps = psum.tile([P, PACK, CH], F32, name="u_ps", tag=f"u{c % BANKS}")
                 sums[c] = (g_ps, u_ps)
             for a in passes:
-                for w in range(2):
+                for w in sides:
                     for t in range(PACK):
                         nc.tensor.matmul_mx(
                             sums[c][w][:, t, :],
@@ -262,40 +262,42 @@ def tile_list_relu_scat_kernel(
         for c in range(BANKS):
             first_layer(c, (0,))
         last = picked1[:, PACK - 1, :]
+        woven1_0 = keep.tile([P, R], BF16, name="woven1_0", align_bytes=64)
+        woven1_12 = keep.tile([P, 2 * R], BF16, name="woven1_12", align_bytes=64)[:]
+        opening = keep.tile([P, 5 * R], BF16, name="burst1", align_bytes=64)
+        woven_h12, woven1_345 = opening[:, : 2 * R], opening[:, 2 * R :]
+        for woven, c0, c1 in ((woven1_0[:], 0, 1), (woven1_12, 1, 3), (woven1_345, 3, 6)):
+            weave(woven, picked1, c0, c1, 0, 2)
         gather(last[:, :CH], PLANES - 1, 0, 1)
-        gather(last[:, CH : 3 * CH], PLANES - 1, 1, 3)
-        woven1_0 = last[:, 3 * CH : 5 * CH].bitcast(BF16)
-        weave(woven1_0, picked1, 0, 1)
-        quantize("x1", 0, 1, woven1_0)
+        gather(last[:, 3 * CH : 5 * CH], PLANES - 1, 1, 3)
+        weave(woven1_0[:], picked1, 0, 1, 2)
+        quantize("x1", 0, 1, woven1_0[:])
         first_layer(0, (1,))
+        moved = picked1_flat[:, 2 * J + CH : 2 * J + CH + 2 * (J + 2 * CH)].rearrange("p (t j) -> p t j", t=2)
+        nc.scalar.copy(
+            woven1_12.rearrange("p (c i t) -> p c t i", i=4, t=PACK)[:, :, 2:, :],
+            moved[:, :, : 2 * CH].rearrange("p t (c i) -> p c t i", i=4),
+        )
+        quantize("x0", CHUNKS // 2, CHUNKS, woven0[1][:], codes_name="woven1_0")
+        quantize("x1", 1, 3, woven1_12)
+        for w in range(2):
+            for c in (1, 2):
+                first_layer(c, (1,), (w,))
         gather(last[:, 3 * CH :], PLANES - 1, 3, CHUNKS)
-        woven1_12 = keep.tile([P, 2 * R], BF16, name="woven1_12", align_bytes=64)
-        for c in (1, 2):
-            weave(woven1_12[:, (c - 1) * R : c * R], picked1, c, c + 1)
-        quantize("x1", 1, 3, woven1_12[:])
-        for c in (1, 2):
-            first_layer(c, (1,))
         woven_h0 = keep.tile([P, R], BF16, name="woven_h0", align_bytes=64)
         vector_h(0, woven_h0[:])
-        woven1_3 = keep.tile([P, R], BF16, name="woven1_3", align_bytes=64)
-        weave(woven1_3[:], picked1, 3, 4)
-        quantize("x1", 3, 4, woven1_3[:])
+        vector_h(1, woven_h12[:, :R])
         quantize("h", 0, 1, woven_h0[:])
-        quantize("x0", CHUNKS // 2, CHUNKS, woven0[1][:], codes_name="gate0")
         y0_ps = chunk_y(0, "t0")
-
-        opening = keep.tile([P, 4 * R], BF16, name="burst1", align_bytes=64)
-        woven_h12, woven1_45 = opening[:, : 2 * R], opening[:, 2 * R :]
-        for c in (1, 2):
-            vector_h(c, woven_h12[:, (c - 1) * R : c * R])
-        for c in (4, 5):
-            weave(woven1_45[:, (c - 4) * R : (c - 3) * R], picked1, c, c + 1)
-        quantize("x1", 4, 6, woven1_45)
-        quantize("h", 1, 3, woven_h12)
+        vector_h(2, woven_h12[:, R:])
+        weave(woven1_345, picked1, 3, 6, 2)
+        quantize("x1", 3, 6, woven1_345)
         y0b = keep.tile([P, 2, CH], F32, name="y0b")
         nc.scalar.copy(y0b[:], y0_ps[:, 2:, :])
-        weighed0 = keep.tile([P, R], F32, name="burst1", align_bytes=64)
-        weigh(nc.vector, weighed0[:, : 2 * CH], y0_ps[:, :2, :], 0)
+        weighed0a = keep.tile([P, 2 * CH], F32, name="weighed0a")
+        weigh(nc.vector, weighed0a[:], y0_ps[:, :2, :], 0)
+        quantize("h", 1, 3, woven_h12)
+        weighed0b = keep.tile([P, 2 * CH], F32, name="burst1", align_bytes=64)
         y1 = keep.tile([P, R], F32, name="y1", align_bytes=64)
         nc.scalar.copy(paged(y1[:], PAGES), chunk_y(1, "t1")[:])
         first_layer(3)
@@ -303,30 +305,32 @@ def tile_list_relu_scat_kernel(
         factors(3, factors3)
         y2_ps = chunk_y(2, "t0")
         first_layer(4)
-        y2 = keep.tile([P, PAGES, CH], F32, name="y2")
-        nc.scalar.copy(y2[:], y2_ps[:])
-        factors4 = keep.tile([P, 2 * R], F32, name="factors4")
-        factors(4, factors4)
 
-        weigh(nc.gpsimd, weighed0[:, 2 * CH :], y0b[:], 0)
+        weigh(nc.gpsimd, weighed0b[:], y0b[:], 0)
         weighed1 = keep.tile([P, R], F32, name="weighed1")
         weigh(nc.gpsimd, weighed1[:], paged(y1[:], PAGES), 1)
         between = keep.tile([P, 4 * R], BF16, name="y1", align_bytes=64)
         woven_h34, woven1_67 = between[:, : 2 * R], between[:, 2 * R :]
+        y2a = paged(woven1_67[:, : 2 * CH].bitcast(F32), 1)
+        nc.scalar.copy(y2a, y2_ps[:, :1, :])
+        y2b = keep.tile([P, PAGES - 1, CH], F32, name="y2b")
+        nc.scalar.copy(y2b[:], y2_ps[:, 1:, :])
+        factors4 = keep.tile([P, 2 * R], F32, name="factors4")
+        factors(4, factors4)
         gpsimd_h(factors3, woven_h34[:, :R])
-        weighed2a = keep.tile([P, CH], F32, name="weighed2a", align_bytes=64)
-        weigh(nc.gpsimd, weighed2a[:], y2[:, :1, :], 2)
+        weighed2a = keep.tile([P, CH], F32, name="weighed2a")
+        weigh(nc.gpsimd, weighed2a[:], y2a, 2)
         gpsimd_h(factors4, woven_h34[:, R:])
         weighed2b = keep.tile([P, 3 * CH], F32, name="factors4")
-        weigh(nc.gpsimd, weighed2b[:], y2[:, 1:, :], 2)
+        weigh(nc.gpsimd, weighed2b[:], y2b[:], 2)
         weave(woven1_67, picked1, 6, 8)
         for q in range(PAGES):
-            put(q, 0, 1, weighed0[:, q * CH : (q + 1) * CH])
+            put(q, 0, 1, (weighed0a, weighed0b)[q // 2][:, q % 2 * CH : (q % 2 + 1) * CH])
         for q in range(PAGES):
             put(q, 1, 2, weighed1[:, q * CH : (q + 1) * CH])
         put(0, 2, 3, weighed2a[:])
         quantize("h", 3, 5, woven_h34)
-        quantize("x1", 6, 8, woven1_67, codes_name="weighed2a")
+        quantize("x1", 6, 8, woven1_67)
         y34_ps = [psum.tile([P, 2, 2 * CH], F32, name="y34_ps", tag=bank) for bank in ("t1", "t0")]
         for q in range(PAGES):
             second_layer(y34_ps[q // 2][:, q % 2, :], q, 3, 5)

@@ -49,11 +49,11 @@ def tile_list_relu_scat_kernel(
         raw_w = [[keep.tile([P, R], U16, name=f"raw_w{w}{a}") for a in range(PASSES)] for w in range(2)]
         w_words = [[keep.tile([P, 2 * R], U8, name=f"w_words{w}{a}", align_bytes=64) for a in range(PASSES)] for w in range(2)]
         w_scales = [keep.tile([P, PASSES * R], U8, name=f"w_scales{w}", align_bytes=64) for w in range(2)]
-        raw_s = keep.tile([P, R], U8, name="page0")
+        raw_s = keep.tile([P, R], U8, name="page1")
         wd_w = keep.tile([P, 2 * N], U8, name="wd_w", align_bytes=64)
         wd_s = keep.tile([P, N], U8, name="wd_s", align_bytes=64)
         ident = keep.tile([P, P], F32, name="ident")
-        blank = keep.tile([P, P], F32, name="blank")
+        blank = keep.tile([P, P], F32, name="page0")
         rows = keep.tile([P, CH], F32, name="rows")
 
         nc.gpsimd.memset(blank[:], 0.0)
@@ -104,7 +104,7 @@ def tile_list_relu_scat_kernel(
                     nc.tensor.transpose(back[:, i, :], wide[:, i, :], ident[:])
                 nc.scalar.copy(dst[:, i0 * CH : i1 * CH], back[:].rearrange("p i e -> p (i e)"))
 
-        spread(0, gain, (HEAD, CHUNKS // 2, CHUNKS), ("u0", "u1"), ("page1", "wide4"))
+        spread(0, gain, (HEAD, CHUNKS // 2, CHUNKS), ("u0", "u1"), ("wide1", "wide4"))
         pages = [keep.tile([P, T], F32, name=f"page{q}") for q in range(2)]
         for page in pages:
             nc.gpsimd.memset(page[:], 0.0)
@@ -256,16 +256,13 @@ def tile_list_relu_scat_kernel(
         def put_weighed(q, c0, c1, src):
             nc.vector.tensor_tensor(window(q, c0, c1), src, gain_out[:, c0 * CH : c1 * CH], MULT)
 
-        def paged(ap, count):
-            return ap.rearrange("p (q j) -> p q j", q=count)
-
         for c in range(BANKS):
             first_layer(c, (0,))
         last = picked1[:, PACK - 1, :]
         woven1_0 = keep.tile([P, R], BF16, name="woven1_0", align_bytes=64)
         woven1_12 = keep.tile([P, 2 * R], BF16, name="woven1_12", align_bytes=64)[:]
-        opening = keep.tile([P, 5 * R], BF16, name="burst1", align_bytes=64)
-        woven_h12, woven1_345 = opening[:, : 2 * R], opening[:, 2 * R :]
+        opening = keep.tile([P, 4 * R], BF16, name="burst", align_bytes=64)
+        woven_h2, woven1_345 = opening[:, :R], opening[:, R:]
         for woven, c0, c1 in ((woven1_0[:], 0, 1), (woven1_12, 1, 3), (woven1_345, 3, 6)):
             weave(woven, picked1, c0, c1, 0, 2)
         gather(last[:, :CH], PLANES - 1, 0, 1)
@@ -284,86 +281,81 @@ def tile_list_relu_scat_kernel(
             for c in (1, 2):
                 first_layer(c, (1,), (w,))
         gather(last[:, 3 * CH :], PLANES - 1, 3, CHUNKS)
-        woven_h0 = keep.tile([P, R], BF16, name="woven_h0", align_bytes=64)
-        vector_h(0, woven_h0[:])
-        vector_h(1, woven_h12[:, :R])
-        quantize("h", 0, 1, woven_h0[:])
-        y0_ps = chunk_y(0, "t0")
-        vector_h(2, woven_h12[:, R:])
+        woven_h = [keep.tile([P, R], BF16, name=f"woven_h{c}", align_bytes=64)[:] for c in range(2)] + [woven_h2]
+        for c in range(2):
+            vector_h(c, woven_h[c])
+        for c in range(2):
+            quantize("h", c, c + 1, woven_h[c])
+        y0_ps, y1_ps = chunk_y(0, "t0"), chunk_y(1, "t1")
+        vector_h(2, woven_h2)
         weave(woven1_345, picked1, 3, 6, 2)
         quantize("x1", 3, 6, woven1_345)
-        y0b = keep.tile([P, 2, CH], F32, name="y0b")
-        nc.scalar.copy(y0b[:], y0_ps[:, 2:, :])
-        weighed0a = keep.tile([P, 2 * CH], F32, name="weighed0a")
-        weigh(nc.vector, weighed0a[:], y0_ps[:, :2, :], 0)
-        quantize("h", 1, 3, woven_h12)
-        weighed0b = keep.tile([P, 2 * CH], F32, name="burst1", align_bytes=64)
-        y1 = keep.tile([P, R], F32, name="y1", align_bytes=64)
-        nc.scalar.copy(paged(y1[:], PAGES), chunk_y(1, "t1")[:])
-        first_layer(3)
-        factors3 = keep.tile([P, 2 * R], F32, name="factors3")
-        factors(3, factors3)
-        y2_ps = chunk_y(2, "t0")
-        first_layer(4)
+        y01_high = keep.tile([P, 2, 2 * CH], F32, name="y01_high")
+        y1_low = keep.tile([P, 2, CH], F32, name="y1_low")
+        nc.scalar.copy(y01_high[:, :, :CH], y0_ps[:, 2:, :])
+        nc.scalar.copy(y01_high[:, :, CH:], y1_ps[:, 2:, :])
+        nc.scalar.copy(y1_low[:], y1_ps[:, :2, :])
+        weighed0 = keep.tile([P, 2 * CH], F32, name="weighed0")
+        weigh(nc.vector, weighed0[:], y0_ps[:, :2, :], 0)
+        quantize("h", 2, 3, woven_h2)
+        both = {}
+        for c in (3, 4):
+            first_layer(c)
+            both[c] = keep.tile([P, 2 * R], F32, name=f"factors{c}", align_bytes=64)
+            factors(c, both[c])
+        y2 = keep.tile([P, PAGES, CH], F32, name="y2")
+        nc.scalar.copy(y2[:], chunk_y(2, "u1")[:])
 
-        weigh(nc.gpsimd, weighed0b[:], y0b[:], 0)
-        weighed1 = keep.tile([P, R], F32, name="weighed1")
-        weigh(nc.gpsimd, weighed1[:], paged(y1[:], PAGES), 1)
-        between = keep.tile([P, 4 * R], BF16, name="y1", align_bytes=64)
-        woven_h34, woven1_67 = between[:, : 2 * R], between[:, 2 * R :]
-        y2a = paged(woven1_67[:, : 2 * CH].bitcast(F32), 1)
-        nc.scalar.copy(y2a, y2_ps[:, :1, :])
-        y2b = keep.tile([P, PAGES - 1, CH], F32, name="y2b")
-        nc.scalar.copy(y2b[:], y2_ps[:, 1:, :])
-        factors4 = keep.tile([P, 2 * R], F32, name="factors4")
-        factors(4, factors4)
-        gpsimd_h(factors3, woven_h34[:, :R])
-        weighed2a = keep.tile([P, CH], F32, name="weighed2a")
-        weigh(nc.gpsimd, weighed2a[:], y2a, 2)
-        gpsimd_h(factors4, woven_h34[:, R:])
-        weighed2b = keep.tile([P, 3 * CH], F32, name="factors4")
-        weigh(nc.gpsimd, weighed2b[:], y2b[:], 2)
-        weave(woven1_67, picked1, 6, 8)
-        for q in range(PAGES):
-            put(q, 0, 1, (weighed0a, weighed0b)[q // 2][:, q % 2 * CH : (q % 2 + 1) * CH])
-        for q in range(PAGES):
-            put(q, 1, 2, weighed1[:, q * CH : (q + 1) * CH])
-        put(0, 2, 3, weighed2a[:])
+        burst = keep.tile([P, 10 * CH], F32, name="burst", align_bytes=64)
+        weigh(nc.gpsimd, burst[:, : 4 * CH], y01_high[:], 0)
+        weigh(nc.gpsimd, burst[:, 4 * CH : 6 * CH], y1_low[:], 1)
+        woven_h34 = burst[:, 6 * CH :].bitcast(BF16)
+        for c in (3, 4):
+            gpsimd_h(both[c], woven_h34[:, (c - 3) * R : (c - 2) * R])
+        weighed2 = keep.tile([P, R], F32, name="weighed2")
+        weigh(nc.gpsimd, weighed2[:], y2[:], 2)
+        woven1_67 = keep.tile([P, 2 * R], BF16, name="factors3", align_bytes=64)
+        weave(woven1_67[:], picked1, 6, 8)
+        for q in range(2):
+            put(q, 0, 1, weighed0[:, q * CH : (q + 1) * CH])
+        for q in (2, 3):
+            put(q, 0, 2, burst[:, 2 * (q - 2) * CH : 2 * (q - 1) * CH])
+        for q in range(2):
+            put(q, 1, 2, burst[:, (4 + q) * CH : (5 + q) * CH])
         quantize("h", 3, 5, woven_h34)
-        quantize("x1", 6, 8, woven1_67)
+        quantize("x1", 6, 8, woven1_67[:])
         y34_ps = [psum.tile([P, 2, 2 * CH], F32, name="y34_ps", tag=bank) for bank in ("t1", "t0")]
         for q in range(PAGES):
             second_layer(y34_ps[q // 2][:, q % 2, :], q, 3, 5)
-        for q in range(1, PAGES):
-            put(q, 2, 3, weighed2b[:, (q - 1) * CH : q * CH])
+        for q in range(PAGES):
+            put(q, 2, 3, weighed2[:, q * CH : (q + 1) * CH])
 
         late = keep.tile([P, 3, 2 * R], F32, name="picked0")
         first_layer(5)
         factors(5, late[:, 0, :])
-        woven_end = keep.tile([P, 3 * R], BF16, name="y1", align_bytes=64)
+        burst = keep.tile([P, 10 * CH], F32, name="burst", align_bytes=64)
+        woven_end = burst[:, 4 * CH :].bitcast(BF16)
         gpsimd_h(late[:, 0, :], woven_end[:, :R])
-        y34 = keep.tile([P, 3, 2 * CH], F32, name="y34")
-        weighed34 = keep.tile([P, 3, 2 * CH], F32, name="weighed34")
-        nc.scalar.copy(y34[:, :2, :], y34_ps[0][:])
-        nc.scalar.copy(y34[:, 2, :], y34_ps[1][:, 0, :])
-        for q in range(3):
-            weigh(nc.gpsimd, weighed34[:, q, :], y34[:, q : q + 1, :], 3)
+        y34 = keep.tile([P, 2, 2 * CH], F32, name="y34")
+        nc.scalar.copy(y34[:], y34_ps[0][:])
+        weigh(nc.gpsimd, burst[:, : 4 * CH], y34[:], 3)
         for c in (6, 7):
             first_layer(c)
             factors(c, late[:, c - 5, :])
             gpsimd_h(late[:, c - 5, :], woven_end[:, (c - 5) * R : (c - 4) * R])
-        for q in range(3):
-            put(q, 3, 5, weighed34[:, q, :])
-        quantize("h", 5, 8, woven_end[:])
+        for q in range(2):
+            put(q, 3, 5, burst[:, 2 * q * CH : 2 * (q + 1) * CH])
+        quantize("h", 5, 8, woven_end)
+        y_end = keep.tile([P, PAGES, 5 * CH], F32, name="y_end")
+        nc.scalar.copy(y_end[:, 3, : 2 * CH], y34_ps[1][:, 1, :])
         filler = late[:, 2, : 2 * CH]
-        nc.scalar.copy(filler, y34_ps[1][:, 1, :])
-        put_weighed(3, 3, 5, filler)
-        y_end = keep.tile([P, PAGES, 3 * CH], F32, name="y_end")
+        nc.scalar.copy(filler, y34_ps[1][:, 0, :])
+        put_weighed(2, 3, 5, filler)
         for q, bank in enumerate(("g0", "u0", "g1", "u1")):
             y_ps = psum.tile([P, 3 * CH], F32, name="y_ps", tag=bank)
             second_layer(y_ps[:, :CH], q, 5, 6)
             second_layer(y_ps[:, CH:], q, 6, 8)
-            nc.scalar.copy(y_end[:, q, :], y_ps[:])
-        for q in range(PAGES):
-            put_weighed(q, 5, CHUNKS, y_end[:, q, :])
+            nc.scalar.copy(y_end[:, q, 2 * CH :], y_ps[:])
+        for q, first in enumerate((5, 5, 5, 3)):
+            put_weighed(q, first, CHUNKS, y_end[:, q, (first - 3) * CH :])
             nc.sync.dma_start(out[q * P : (q + 1) * P, :], pages[q][:])

@@ -235,8 +235,8 @@ def tile_list_relu_scat_kernel(
             nc.scalar.activation(words(both[:, :R]), by_pairs(sums[c][0]), RELU)
             nc.scalar.copy(words(both[:, R:]), by_pairs(sums[c][1]))
 
-        def gpsimd_h(both, woven):
-            nc.gpsimd.tensor_tensor(woven, both[:, R:], both[:, :R], MULT)
+        def gpsimd_h(both, woven, lo=0, hi=R):
+            nc.gpsimd.tensor_tensor(woven[:, lo:hi], both[:, R + lo : R + hi], both[:, lo:hi], MULT)
 
         def weigh(engine, dst, src, c0):
             count, width = src.shape[1], src.shape[2]
@@ -290,72 +290,79 @@ def tile_list_relu_scat_kernel(
         vector_h(2, woven_h2)
         weave(woven1_345, picked1, 3, 6, 2)
         quantize("x1", 3, 6, woven1_345)
-        y01_high = keep.tile([P, 2, 2 * CH], F32, name="y01_high")
-        y1_low = keep.tile([P, 2, CH], F32, name="y1_low")
-        nc.scalar.copy(y01_high[:, :, :CH], y0_ps[:, 2:, :])
-        nc.scalar.copy(y01_high[:, :, CH:], y1_ps[:, 2:, :])
-        nc.scalar.copy(y1_low[:], y1_ps[:, :2, :])
-        weighed0 = keep.tile([P, 2 * CH], F32, name="weighed0")
-        weigh(nc.vector, weighed0[:], y0_ps[:, :2, :], 0)
+        y0_high = keep.tile([P, 2, CH], F32, name="y0_high")
+        y1 = keep.tile([P, PAGES, CH], F32, name="y1", align_bytes=64)
+        nc.scalar.copy(y0_high[:], y0_ps[:, 2:, :])
+        nc.scalar.copy(y1[:], y1_ps[:])
+        weighed0_low = keep.tile([P, 2 * CH], F32, name="weighed0_low")
+        weigh(nc.vector, weighed0_low[:], y0_ps[:, :2, :], 0)
         quantize("h", 2, 3, woven_h2)
+        y2_ps = chunk_y(2, "t0")
         both = {}
         for c in (3, 4):
             first_layer(c)
             both[c] = keep.tile([P, 2 * R], F32, name=f"factors{c}", align_bytes=64)
-            factors(c, both[c])
-        y2 = keep.tile([P, PAGES, CH], F32, name="y2")
-        nc.scalar.copy(y2[:], chunk_y(2, "u1")[:])
 
-        burst = keep.tile([P, 10 * CH], F32, name="burst", align_bytes=64)
-        weigh(nc.gpsimd, burst[:, : 4 * CH], y01_high[:], 0)
-        weigh(nc.gpsimd, burst[:, 4 * CH : 6 * CH], y1_low[:], 1)
-        woven_h34 = burst[:, 6 * CH :].bitcast(BF16)
-        for c in (3, 4):
-            gpsimd_h(both[c], woven_h34[:, (c - 3) * R : (c - 2) * R])
-        weighed2 = keep.tile([P, R], F32, name="weighed2")
-        weigh(nc.gpsimd, weighed2[:], y2[:], 2)
-        woven1_67 = keep.tile([P, 2 * R], BF16, name="factors3", align_bytes=64)
-        weave(woven1_67[:], picked1, 6, 8)
-        for q in range(2):
-            put(q, 0, 1, weighed0[:, q * CH : (q + 1) * CH])
-        for q in (2, 3):
-            put(q, 0, 2, burst[:, 2 * (q - 2) * CH : 2 * (q - 1) * CH])
-        for q in range(2):
-            put(q, 1, 2, burst[:, (4 + q) * CH : (5 + q) * CH])
+        weighed01 = keep.tile([P, 6 * CH], F32, name="burst", align_bytes=64)
+        weigh(nc.gpsimd, weighed01[:, : 2 * CH], y0_high[:], 0)
+        weigh(nc.gpsimd, weighed01[:, 2 * CH :], y1[:], 1)
+        woven_h34 = keep.tile([P, 2 * R], BF16, name="y1", align_bytes=64)[:]
+        factors(3, both[3])
+        y2 = keep.tile([P, PAGES, CH], F32, name="y2")
+        nc.scalar.copy(y2[:], y2_ps[:])
+        factors(4, both[4])
+        gpsimd_h(both[3], woven_h34[:, :R])
+        weighed2_first = keep.tile([P, CH], F32, name="weighed2_first")
+        weigh(nc.gpsimd, weighed2_first[:], y2[:, :1, :], 2)
+        gpsimd_h(both[4], woven_h34[:, R:])
+        weighed2_rest = keep.tile([P, 3 * CH], F32, name="factors4", align_bytes=64)
+        weigh(nc.gpsimd, weighed2_rest[:], y2[:, 1:, :], 2)
+        woven1_67 = keep.tile([P, 2 * R], BF16, name="factors3", align_bytes=64)[:]
+        weave(woven1_67, picked1, 6, 8)
+        for q in range(PAGES):
+            put(q, 0, 1, (weighed0_low, weighed01)[q // 2][:, q % 2 * CH : (q % 2 + 1) * CH])
+        for q in range(PAGES):
+            put(q, 1, 2, weighed01[:, (2 + q) * CH : (3 + q) * CH])
+        put(0, 2, 3, weighed2_first[:])
         quantize("h", 3, 5, woven_h34)
-        quantize("x1", 6, 8, woven1_67[:])
+        quantize("x1", 6, 8, woven1_67)
         y34_ps = [psum.tile([P, 2, 2 * CH], F32, name="y34_ps", tag=bank) for bank in ("t1", "t0")]
         for q in range(PAGES):
             second_layer(y34_ps[q // 2][:, q % 2, :], q, 3, 5)
-        for q in range(PAGES):
-            put(q, 2, 3, weighed2[:, q * CH : (q + 1) * CH])
+        for q in range(1, PAGES):
+            put(q, 2, 3, weighed2_rest[:, (q - 1) * CH : q * CH])
 
         late = keep.tile([P, 3, 2 * R], F32, name="picked0")
         first_layer(5)
         factors(5, late[:, 0, :])
-        burst = keep.tile([P, 10 * CH], F32, name="burst", align_bytes=64)
-        woven_end = burst[:, 4 * CH :].bitcast(BF16)
-        gpsimd_h(late[:, 0, :], woven_end[:, :R])
+        woven_end = keep.tile([P, 3 * R], BF16, name="y1", align_bytes=64)
+        y34_first = woven_end[:, R // 2 : R // 2 + 4 * CH].bitcast(F32).unsqueeze(1)
         y34 = keep.tile([P, 2, 2 * CH], F32, name="y34")
-        nc.scalar.copy(y34[:], y34_ps[0][:])
-        weigh(nc.gpsimd, burst[:, : 4 * CH], y34[:], 3)
+        weighed34 = keep.tile([P, 3, 2 * CH], F32, name="weighed34")
+        nc.scalar.copy(y34_first, y34_ps[0][:, :1, :])
+        nc.scalar.copy(y34[:, 0, :], y34_ps[0][:, 1, :])
+        nc.scalar.copy(y34[:, 1, :], y34_ps[1][:, 0, :])
+        gpsimd_h(late[:, 0, :], woven_end[:, :R], 0, R // 2)
+        weigh(nc.gpsimd, weighed34[:, 0, :], y34_first, 3)
+        gpsimd_h(late[:, 0, :], woven_end[:, :R], R // 2, R)
+        for q in (1, 2):
+            weigh(nc.gpsimd, weighed34[:, q, :], y34[:, q - 1 : q, :], 3)
         for c in (6, 7):
             first_layer(c)
             factors(c, late[:, c - 5, :])
             gpsimd_h(late[:, c - 5, :], woven_end[:, (c - 5) * R : (c - 4) * R])
-        for q in range(2):
-            put(q, 3, 5, burst[:, 2 * q * CH : 2 * (q + 1) * CH])
-        quantize("h", 5, 8, woven_end)
-        y_end = keep.tile([P, PAGES, 5 * CH], F32, name="y_end")
-        nc.scalar.copy(y_end[:, 3, : 2 * CH], y34_ps[1][:, 1, :])
+        for q in range(3):
+            put(q, 3, 5, weighed34[:, q, :])
+        quantize("h", 5, 8, woven_end[:])
         filler = late[:, 2, : 2 * CH]
-        nc.scalar.copy(filler, y34_ps[1][:, 0, :])
-        put_weighed(2, 3, 5, filler)
+        nc.scalar.copy(filler, y34_ps[1][:, 1, :])
+        put_weighed(3, 3, 5, filler)
+        y_end = keep.tile([P, PAGES, 3 * CH], F32, name="y_end")
         for q, bank in enumerate(("g0", "u0", "g1", "u1")):
             y_ps = psum.tile([P, 3 * CH], F32, name="y_ps", tag=bank)
             second_layer(y_ps[:, :CH], q, 5, 6)
             second_layer(y_ps[:, CH:], q, 6, 8)
-            nc.scalar.copy(y_end[:, q, 2 * CH :], y_ps[:])
-        for q, first in enumerate((5, 5, 5, 3)):
-            put_weighed(q, first, CHUNKS, y_end[:, q, (first - 3) * CH :])
+            nc.scalar.copy(y_end[:, q, :], y_ps[:])
+        for q in range(PAGES):
+            put_weighed(q, 5, CHUNKS, y_end[:, q, :])
             nc.sync.dma_start(out[q * P : (q + 1) * P, :], pages[q][:])

@@ -235,8 +235,8 @@ def tile_list_relu_scat_kernel(
             nc.scalar.activation(words(both[:, :R]), by_pairs(sums[c][0]), RELU)
             nc.scalar.copy(words(both[:, R:]), by_pairs(sums[c][1]))
 
-        def gpsimd_h(both, woven, lo=0, hi=R):
-            nc.gpsimd.tensor_tensor(woven[:, lo:hi], both[:, R + lo : R + hi], both[:, lo:hi], MULT)
+        def gpsimd_h(both, product, lo=0, hi=R):
+            nc.gpsimd.tensor_tensor(product[:, lo:hi], both[:, R + lo : R + hi], both[:, lo:hi], MULT)
 
         def weigh(engine, dst, src, c0):
             count, width = src.shape[1], src.shape[2]
@@ -306,19 +306,21 @@ def tile_list_relu_scat_kernel(
         weighed01 = keep.tile([P, 6 * CH], F32, name="burst", align_bytes=64)
         weigh(nc.gpsimd, weighed01[:, : 2 * CH], y0_high[:], 0)
         weigh(nc.gpsimd, weighed01[:, 2 * CH :], y1[:], 1)
-        woven_h34 = keep.tile([P, 2 * R], BF16, name="y1", align_bytes=64)[:]
+        h3 = keep.tile([P, R], F32, name="y1", align_bytes=64)
+        woven_h34 = keep.tile([P, 2 * R], BF16, name="woven_h34", align_bytes=64)[:]
         factors(3, both[3])
         y2 = keep.tile([P, PAGES, CH], F32, name="y2")
         nc.scalar.copy(y2[:], y2_ps[:])
         factors(4, both[4])
-        gpsimd_h(both[3], woven_h34[:, :R])
+        gpsimd_h(both[3], h3[:])
         weighed2_first = keep.tile([P, CH], F32, name="weighed2_first")
         weigh(nc.gpsimd, weighed2_first[:], y2[:, :1, :], 2)
         gpsimd_h(both[4], woven_h34[:, R:])
-        weighed2_rest = keep.tile([P, 3 * CH], F32, name="factors4", align_bytes=64)
-        weigh(nc.gpsimd, weighed2_rest[:], y2[:, 1:, :], 2)
         woven1_67 = keep.tile([P, 2 * R], BF16, name="factors3", align_bytes=64)[:]
+        nc.scalar.copy(woven_h34[:, :R], h3[:])
         weave(woven1_67, picked1, 6, 8)
+        weighed2_rest = keep.tile([P, 3 * CH], F32, name="picked1")
+        weigh(nc.gpsimd, weighed2_rest[:], y2[:, 1:, :], 2)
         for q in range(PAGES):
             put(q, 0, 1, (weighed0_low, weighed01)[q // 2][:, q % 2 * CH : (q % 2 + 1) * CH])
         for q in range(PAGES):
@@ -335,22 +337,26 @@ def tile_list_relu_scat_kernel(
         late = keep.tile([P, 3, 2 * R], F32, name="picked0")
         first_layer(5)
         factors(5, late[:, 0, :])
-        woven_end = keep.tile([P, 3 * R], BF16, name="y1", align_bytes=64)
-        y34_first = woven_end[:, R // 2 : R // 2 + 4 * CH].bitcast(F32).unsqueeze(1)
+        h_end = keep.tile([P, 2 * R], F32, name="woven_h34", align_bytes=64)
+        woven_end = keep.tile([P, 3 * R], BF16, name="woven_end", align_bytes=64)
+        y34_first = h_end[:, R // 2 : R].unsqueeze(1)
         y34 = keep.tile([P, 2, 2 * CH], F32, name="y34")
         weighed34 = keep.tile([P, 3, 2 * CH], F32, name="weighed34")
         nc.scalar.copy(y34_first, y34_ps[0][:, :1, :])
         nc.scalar.copy(y34[:, 0, :], y34_ps[0][:, 1, :])
         nc.scalar.copy(y34[:, 1, :], y34_ps[1][:, 0, :])
-        gpsimd_h(late[:, 0, :], woven_end[:, :R], 0, R // 2)
+        gpsimd_h(late[:, 0, :], h_end[:, :R], 0, R // 2)
         weigh(nc.gpsimd, weighed34[:, 0, :], y34_first, 3)
-        gpsimd_h(late[:, 0, :], woven_end[:, :R], R // 2, R)
+        gpsimd_h(late[:, 0, :], h_end[:, :R], R // 2, R)
         for q in (1, 2):
             weigh(nc.gpsimd, weighed34[:, q, :], y34[:, q - 1 : q, :], 3)
         for c in (6, 7):
             first_layer(c)
             factors(c, late[:, c - 5, :])
-            gpsimd_h(late[:, c - 5, :], woven_end[:, (c - 5) * R : (c - 4) * R])
+        gpsimd_h(late[:, 1, :], h_end[:, R:])
+        gpsimd_h(late[:, 2, :], woven_end[:, 2 * R :])
+        for i in range(2):
+            nc.scalar.copy(woven_end[:, i * R : (i + 1) * R], h_end[:, i * R : (i + 1) * R])
         for q in range(3):
             put(q, 3, 5, weighed34[:, q, :])
         quantize("h", 5, 8, woven_end[:])

@@ -57,6 +57,7 @@ def tile_list_relu_scat_kernel(
         rows = keep.tile([P, CH], F32, name="rows")
 
         nc.gpsimd.memset(blank[:], 0.0)
+        nc.gpsimd.memset(rows[P // 2 :, :], 0.0)
         nc.gpsimd.affine_select(
             out=ident[:],
             in_=blank[:],
@@ -70,12 +71,9 @@ def tile_list_relu_scat_kernel(
         for scales in (*w_scales, wd_s):
             nc.vector.memset(scales[:].bitcast(I32), 0)
 
-        for w, weights in enumerate((wgt, wgo)):
-            nc.sync.dma_start(
-                rows[w * P // 2 : (w + 1) * P // 2, :], weights.rearrange("p (h n) -> (p h) n", h=2)[:: LANE + 1]
-            )
-        nc.sync.dma_start(planes[0][:], x_rows[0, 0])
+        nc.sync.dma_start(rows[: P // 2, :], wgt.rearrange("p (h n) -> (p h) n", h=2)[:: LANE + 1])
         nc.sync.dma_start(pick[:], offs)
+        nc.sync.dma_start(planes[0][:], x_rows[0, 0])
         nc.sync.dma_start(gain[:, : HEAD * CH], wgt[:, : HEAD * CH])
         for w, dram_scales in enumerate((wg_scales, wu_scales)):
             nc.scalar.dma_start(
@@ -130,6 +128,7 @@ def tile_list_relu_scat_kernel(
         wd_rows = wd_scales.bitcast(I32).rearrange("a (d r) n -> d r (a n)", r=SCALE_ROWS)
         for d in range(P // QUADRANT):
             nc.sync.dma_start(wd_s[QUADRANT * d : QUADRANT * d + SCALE_ROWS, :].bitcast(I32), wd_rows[d])
+        nc.sync.dma_start(gain_out[:], wgo)
 
         def gather(dst, m, c0, c1):
             nc.vector.tensor_tensor(
@@ -144,12 +143,16 @@ def tile_list_relu_scat_kernel(
 
         quantised = {}
 
-        def quantize(kind, c0, c1, woven, codes_name=None):
-            codes = keep.tile([P, (c1 - c0) * CH], U32, name=codes_name or f"{kind}_codes{c0}", align_bytes=64)
-            scales = keep.tile([P, (c1 - c0) * CH], U8, name=f"{kind}_scales{c0}", align_bytes=64)
+        def quantize(parts, woven, codes_name=None):
+            label = "%s_%d" % parts[0]
+            codes = keep.tile([P, len(parts) * CH], U32, name=codes_name or f"codes_{label}", align_bytes=64)
+            scales = keep.tile([P, len(parts) * CH], U8, name=f"scales_{label}", align_bytes=64)
             nc.vector.quantize_mx(out=codes[:].bitcast(FP8X4), scales=scales[:], in_=woven)
-            for c in range(c0, c1):
-                quantised[kind, c] = (codes, scales, (c - c0) * CH)
+            for i, part in enumerate(parts):
+                quantised[part] = (codes, scales, i * CH)
+
+        def run(kind, c0, c1):
+            return [(kind, c) for c in range(c0, c1)]
 
         def moving(kind, c0, c1):
             codes, scales, lo = quantised[kind, c0]
@@ -163,7 +166,6 @@ def tile_list_relu_scat_kernel(
             gather(picked0[:, t, :], t, 0, CHUNKS)
         for h in range(2):
             gather(picked0[:, PACK - 1, h * HALF : (h + 1) * HALF], PACK - 1, h * CHUNKS // 2, (h + 1) * CHUNKS // 2)
-        spread(1, gain_out, (0, CHUNKS // 2, CHUNKS), ("g0", "g1"), ("wide0", "wide4"))
         for q in range(2, PAGES):
             pages.append(keep.tile([P, T], F32, name=f"plane{q - 2}"))
             nc.gpsimd.memset(pages[q][:], 0.0)
@@ -180,7 +182,7 @@ def tile_list_relu_scat_kernel(
         picked1 = picked1_flat[:, : PACK * J].rearrange("p (t j) -> p t j", t=PACK)
         for t in range(PACK - 1):
             gather(picked1[:, t, :], PACK + t, 0, CHUNKS)
-        quantize("x0", 0, CHUNKS // 2, woven0[0][:])
+        quantize(run("x0", 0, CHUNKS // 2), woven0[0][:])
 
         sums = {}
 
@@ -268,15 +270,15 @@ def tile_list_relu_scat_kernel(
         gather(last[:, :CH], PLANES - 1, 0, 1)
         gather(last[:, 3 * CH : 5 * CH], PLANES - 1, 1, 3)
         weave(woven1_0[:], picked1, 0, 1, 2)
-        quantize("x1", 0, 1, woven1_0[:])
+        quantize(run("x1", 0, 1), woven1_0[:])
         first_layer(0, (1,))
         moved = picked1_flat[:, 2 * J + CH : 2 * J + CH + 2 * (J + 2 * CH)].rearrange("p (t j) -> p t j", t=2)
         nc.scalar.copy(
             woven1_12.rearrange("p (c i t) -> p c t i", i=4, t=PACK)[:, :, 2:, :],
             moved[:, :, : 2 * CH].rearrange("p t (c i) -> p c t i", i=4),
         )
-        quantize("x0", CHUNKS // 2, CHUNKS, woven0[1][:], codes_name="woven1_0")
-        quantize("x1", 1, 3, woven1_12)
+        quantize(run("x0", CHUNKS // 2, CHUNKS), woven0[1][:], codes_name="woven1_0")
+        quantize(run("x1", 1, 3), woven1_12)
         for w in range(2):
             for c in (1, 2):
                 first_layer(c, (1,), (w,))
@@ -285,18 +287,18 @@ def tile_list_relu_scat_kernel(
         for c in range(2):
             vector_h(c, woven_h[c])
         for c in range(2):
-            quantize("h", c, c + 1, woven_h[c])
+            quantize(run("h", c, c + 1), woven_h[c])
         y0_ps, y1_ps = chunk_y(0, "t0"), chunk_y(1, "t1")
         vector_h(2, woven_h2)
         weave(woven1_345, picked1, 3, 6, 2)
-        quantize("x1", 3, 6, woven1_345)
+        quantize(run("x1", 3, 6), woven1_345)
         y0_high = keep.tile([P, 2, CH], F32, name="y0_high")
         y1 = keep.tile([P, PAGES, CH], F32, name="y1", align_bytes=64)
         nc.scalar.copy(y0_high[:], y0_ps[:, 2:, :])
         nc.scalar.copy(y1[:], y1_ps[:])
         weighed0_low = keep.tile([P, 2 * CH], F32, name="weighed0_low")
         weigh(nc.vector, weighed0_low[:], y0_ps[:, :2, :], 0)
-        quantize("h", 2, 3, woven_h2)
+        quantize(run("h", 2, 3), woven_h2)
         y2_ps = chunk_y(2, "t0")
         both = {}
         for c in (3, 4):
@@ -326,8 +328,8 @@ def tile_list_relu_scat_kernel(
         for q in range(PAGES):
             put(q, 1, 2, weighed01[:, (2 + q) * CH : (3 + q) * CH])
         put(0, 2, 3, weighed2_first[:])
-        quantize("h", 3, 5, woven_h34)
-        quantize("x1", 6, 8, woven1_67)
+        quantize(run("h", 3, 5), woven_h34)
+        quantize(run("x1", 6, 8), woven1_67)
         y34_ps = [psum.tile([P, 2, 2 * CH], F32, name="y34_ps", tag=bank) for bank in ("t1", "t0")]
         for q in range(PAGES):
             second_layer(y34_ps[q // 2][:, q % 2, :], q, 3, 5)
@@ -359,7 +361,7 @@ def tile_list_relu_scat_kernel(
             nc.scalar.copy(woven_end[:, i * R : (i + 1) * R], h_end[:, i * R : (i + 1) * R])
         for q in range(3):
             put(q, 3, 5, weighed34[:, q, :])
-        quantize("h", 5, 8, woven_end[:])
+        quantize(run("h", 5, 8), woven_end[:])
         filler = late[:, 2, : 2 * CH]
         nc.scalar.copy(filler, y34_ps[1][:, 1, :])
         put_weighed(3, 3, 5, filler)

@@ -288,26 +288,28 @@ def tile_list_relu_scat_kernel(
             vector_h(c, woven_h[c])
         for c in range(2):
             quantize(run("h", c, c + 1), woven_h[c])
-        y0_ps, y1_ps = chunk_y(0, "t0"), chunk_y(1, "t1")
+        y01_ps = [psum.tile([P, 2, 2, CH], F32, name="y01_ps", tag=bank) for bank in ("t0", "t1")]
+        for half in range(2):
+            for c in range(2):
+                for side in range(2):
+                    second_layer(y01_ps[half][:, c, side, :], 2 * half + side, c, c + 1)
         vector_h(2, woven_h2)
         weave(woven1_345, picked1, 3, 6, 2)
         quantize(run("x1", 3, 6), woven1_345)
-        y0_high = keep.tile([P, 2, CH], F32, name="y0_high")
-        y1 = keep.tile([P, PAGES, CH], F32, name="y1", align_bytes=64)
-        nc.scalar.copy(y0_high[:], y0_ps[:, 2:, :])
-        nc.scalar.copy(y1[:], y1_ps[:])
-        weighed0_low = keep.tile([P, 2 * CH], F32, name="weighed0_low")
-        weigh(nc.vector, weighed0_low[:], y0_ps[:, :2, :], 0)
         quantize(run("h", 2, 3), woven_h2)
+        y1 = keep.tile([P, PAGES, CH], F32, name="y1", align_bytes=64)
+        weighed0 = keep.tile([P, PAGES * CH], F32, name="weighed0")
+        for half in range(2):
+            nc.scalar.copy(y1[:, 2 * half : 2 * half + 2, :], y01_ps[half][:, 1, :, :])
+            weigh(nc.vector, weighed0[:, 2 * half * CH : 2 * (half + 1) * CH], y01_ps[half][:, 0, :, :], 0)
         y2_ps = chunk_y(2, "t0")
         both = {}
         for c in (3, 4):
             first_layer(c)
             both[c] = keep.tile([P, 2 * R], F32, name=f"factors{c}", align_bytes=64)
 
-        weighed01 = keep.tile([P, 6 * CH], F32, name="burst", align_bytes=64)
-        weigh(nc.gpsimd, weighed01[:, : 2 * CH], y0_high[:], 0)
-        weigh(nc.gpsimd, weighed01[:, 2 * CH :], y1[:], 1)
+        weighed1 = keep.tile([P, PAGES * CH], F32, name="burst", align_bytes=64)
+        weigh(nc.gpsimd, weighed1[:], y1[:], 1)
         h3 = keep.tile([P, R], F32, name="y1", align_bytes=64)
         woven_h34 = keep.tile([P, 2 * R], BF16, name="woven_h34", align_bytes=64)[:]
         factors(3, both[3])
@@ -324,9 +326,9 @@ def tile_list_relu_scat_kernel(
         weighed2_rest = keep.tile([P, 3 * CH], F32, name="picked1")
         weigh(nc.gpsimd, weighed2_rest[:], y2[:, 1:, :], 2)
         for q in range(PAGES):
-            put(q, 0, 1, (weighed0_low, weighed01)[q // 2][:, q % 2 * CH : (q % 2 + 1) * CH])
+            put(q, 0, 1, weighed0[:, q * CH : (q + 1) * CH])
         for q in range(PAGES):
-            put(q, 1, 2, weighed01[:, (2 + q) * CH : (3 + q) * CH])
+            put(q, 1, 2, weighed1[:, q * CH : (q + 1) * CH])
         put(0, 2, 3, weighed2_first[:])
         quantize(run("h", 3, 5), woven_h34)
         quantize(run("x1", 6, 8), woven1_67)

@@ -38,6 +38,7 @@ def tile_list_relu_scat_kernel(
     nc = tc.nc
     with ExitStack() as ctx:
         keep = ctx.enter_context(tc.tile_pool(name="keep", bufs=1))
+        ring = ctx.enter_context(tc.tile_pool(name="ring", bufs=1))
         psum = ctx.enter_context(tc.psum_pool(name="psum", bufs=1))
 
         pick = keep.tile([P, J // LANE], U16, name="pick")
@@ -233,12 +234,16 @@ def tile_list_relu_scat_kernel(
             nc.scalar.activation(walk(gate[:]), by_pairs(sums[c][0]), RELU)
             nc.vector.tensor_tensor(words(woven), by_pairs(sums[c][1]), walk(gate[:]), MULT)
 
-        def factors(c, both):
-            nc.scalar.activation(words(both[:, :R]), by_pairs(sums[c][0]), RELU)
-            nc.scalar.copy(words(both[:, R:]), by_pairs(sums[c][1]))
+        gates, ups = {}, {}
 
-        def gpsimd_h(both, product, lo=0, hi=R):
-            nc.gpsimd.tensor_tensor(product[:, lo:hi], both[:, R + lo : R + hi], both[:, lo:hi], MULT)
+        def bring(c, up_buffer=None):
+            gates[c] = keep.tile([P, R], F32, name=f"gate{c}", align_bytes=64)
+            ups[c] = keep.tile([P, R], F32, name=up_buffer or f"up{c}", align_bytes=64)
+            nc.scalar.activation(words(gates[c][:]), by_pairs(sums[c][0]), RELU)
+            nc.scalar.copy(words(ups[c][:]), by_pairs(sums[c][1]))
+
+        def gpsimd_h(c, product):
+            nc.gpsimd.tensor_tensor(product, ups[c][:], gates[c][:], MULT)
 
         def weigh(engine, dst, src, c0):
             count, width = src.shape[1], src.shape[2]
@@ -258,14 +263,25 @@ def tile_list_relu_scat_kernel(
         def put_weighed(q, c0, c1, src):
             nc.vector.tensor_tensor(window(q, c0, c1), src, gain_out[:, c0 * CH : c1 * CH], MULT)
 
+        KIB = 1024
+        MID = 3 * KIB
+
+        def slot(s, parts):
+            width = len(parts) * R
+            first = MID if s % 2 == 0 else MID + KIB // 2 - 2 * width
+            return ring.tile([P, width], BF16, name=f"slot{s}", offset=first, align_bytes=64)
+
+        def y_tile(c, shape, name):
+            return ring.tile(shape, F32, name=name, offset=MID + KIB // 2 if c % 2 else MID - 2 * KIB, align_bytes=64)
+
         for c in range(BANKS):
             first_layer(c, (0,))
         last = picked1[:, PACK - 1, :]
         woven1_0 = keep.tile([P, R], BF16, name="woven1_0", align_bytes=64)
         woven1_12 = keep.tile([P, 2 * R], BF16, name="woven1_12", align_bytes=64)[:]
-        opening = keep.tile([P, 4 * R], BF16, name="burst", align_bytes=64)
-        woven_h2, woven1_345 = opening[:, :R], opening[:, R:]
-        for woven, c0, c1 in ((woven1_0[:], 0, 1), (woven1_12, 1, 3), (woven1_345, 3, 6)):
+        parts0 = [("h", 1), ("x1", 3), ("x1", 4)]
+        slot0 = slot(0, parts0)
+        for woven, c0, c1 in ((woven1_0[:], 0, 1), (woven1_12, 1, 3), (slot0[:, R:], 3, 5)):
             weave(woven, picked1, c0, c1, 0, 2)
         gather(last[:, :CH], PLANES - 1, 0, 1)
         gather(last[:, 3 * CH : 5 * CH], PLANES - 1, 1, 3)
@@ -279,100 +295,80 @@ def tile_list_relu_scat_kernel(
         )
         quantize(run("x0", CHUNKS // 2, CHUNKS), woven0[1][:], codes_name="woven1_0")
         quantize(run("x1", 1, 3), woven1_12)
-        for w in range(2):
-            for c in (1, 2):
-                first_layer(c, (1,), (w,))
+        first_layer(1, (1,))
+        first_layer(2, (1,))
         gather(last[:, 3 * CH :], PLANES - 1, 3, CHUNKS)
-        woven_h = [keep.tile([P, R], BF16, name=f"woven_h{c}", align_bytes=64)[:] for c in range(2)] + [woven_h2]
-        for c in range(2):
-            vector_h(c, woven_h[c])
-        for c in range(2):
-            quantize(run("h", c, c + 1), woven_h[c])
-        y01_ps = [psum.tile([P, 2, 2, CH], F32, name="y01_ps", tag=bank) for bank in ("t0", "t1")]
-        for half in range(2):
-            for c in range(2):
-                for side in range(2):
-                    second_layer(y01_ps[half][:, c, side, :], 2 * half + side, c, c + 1)
-        vector_h(2, woven_h2)
-        weave(woven1_345, picked1, 3, 6, 2)
-        quantize(run("x1", 3, 6), woven1_345)
-        quantize(run("h", 2, 3), woven_h2)
-        y1 = keep.tile([P, PAGES, CH], F32, name="y1", align_bytes=64)
-        weighed0 = keep.tile([P, PAGES * CH], F32, name="weighed0")
-        for half in range(2):
-            nc.scalar.copy(y1[:, 2 * half : 2 * half + 2, :], y01_ps[half][:, 1, :, :])
-            weigh(nc.vector, weighed0[:, 2 * half * CH : 2 * (half + 1) * CH], y01_ps[half][:, 0, :, :], 0)
-        y2_ps = chunk_y(2, "t0")
-        both = {}
-        for c in (3, 4):
-            first_layer(c)
-            both[c] = keep.tile([P, 2 * R], F32, name=f"factors{c}", align_bytes=64)
+        woven_h0 = keep.tile([P, R], BF16, name="woven_h0", align_bytes=64)
+        vector_h(0, woven_h0[:])
+        vector_h(1, slot0[:, :R])
+        weave(slot0[:, R:], picked1, 3, 5, 2)
+        quantize(run("h", 0, 1), woven_h0[:])
+        y_ps = chunk_y(0, "t0")
+        bring(2)
+        quantize(parts0, slot0[:])
 
-        weighed1 = keep.tile([P, PAGES * CH], F32, name="burst", align_bytes=64)
-        weigh(nc.gpsimd, weighed1[:], y1[:], 1)
-        h3 = keep.tile([P, R], F32, name="y1", align_bytes=64)
-        woven_h34 = keep.tile([P, 2 * R], BF16, name="woven_h34", align_bytes=64)[:]
-        factors(3, both[3])
-        y2 = keep.tile([P, PAGES, CH], F32, name="y2")
-        nc.scalar.copy(y2[:], y2_ps[:])
-        factors(4, both[4])
-        gpsimd_h(both[3], h3[:])
-        weighed2_first = keep.tile([P, CH], F32, name="weighed2_first")
-        weigh(nc.gpsimd, weighed2_first[:], y2[:, :1, :], 2)
-        gpsimd_h(both[4], woven_h34[:, R:])
-        woven1_67 = keep.tile([P, 2 * R], BF16, name="factors3", align_bytes=64)[:]
-        nc.scalar.copy(woven_h34[:, :R], h3[:])
-        weave(woven1_67, picked1, 6, 8)
-        weighed2_rest = keep.tile([P, 3 * CH], F32, name="picked1")
-        weigh(nc.gpsimd, weighed2_rest[:], y2[:, 1:, :], 2)
-        for q in range(PAGES):
-            put(q, 0, 1, weighed0[:, q * CH : (q + 1) * CH])
-        for q in range(PAGES):
-            put(q, 1, 2, weighed1[:, q * CH : (q + 1) * CH])
-        put(0, 2, 3, weighed2_first[:])
-        quantize(run("h", 3, 5), woven_h34)
-        quantize(run("x1", 6, 8), woven1_67)
-        y34_ps = [psum.tile([P, 2, 2 * CH], F32, name="y34_ps", tag=bank) for bank in ("t1", "t0")]
-        for q in range(PAGES):
-            second_layer(y34_ps[q // 2][:, q % 2, :], q, 3, 5)
-        for q in range(1, PAGES):
-            put(q, 2, 3, weighed2_rest[:, (q - 1) * CH : q * CH])
+        def weigh_split(engine, c, y):
+            three = keep.tile([P, 3 * CH], F32, name=f"three{c}", align_bytes=64)
+            one = keep.tile([P, CH], F32, name=f"one{c}")
+            weigh(engine, three[:], y[:, :3, :], c)
+            weigh(engine, one[:], y[:, 3:, :], c)
+            return [three[:, q * CH : (q + 1) * CH] for q in range(3)] + [one[:]]
 
-        late = keep.tile([P, 3, 2 * R], F32, name="picked0")
-        first_layer(5)
-        factors(5, late[:, 0, :])
-        h_end = keep.tile([P, 2 * R], F32, name="woven_h34", align_bytes=64)
-        woven_end = keep.tile([P, 3 * R], BF16, name="woven_end", align_bytes=64)
-        y34_first = h_end[:, R // 2 : R].unsqueeze(1)
-        y34 = keep.tile([P, 2, 2 * CH], F32, name="y34")
-        weighed34 = keep.tile([P, 3, 2 * CH], F32, name="weighed34")
-        nc.scalar.copy(y34_first, y34_ps[0][:, :1, :])
-        nc.scalar.copy(y34[:, 0, :], y34_ps[0][:, 1, :])
-        nc.scalar.copy(y34[:, 1, :], y34_ps[1][:, 0, :])
-        gpsimd_h(late[:, 0, :], h_end[:, :R], 0, R // 2)
-        weigh(nc.gpsimd, weighed34[:, 0, :], y34_first, 3)
-        gpsimd_h(late[:, 0, :], h_end[:, :R], R // 2, R)
-        for q in (1, 2):
-            weigh(nc.gpsimd, weighed34[:, q, :], y34[:, q - 1 : q, :], 3)
+        ready = weigh_split(nc.vector, 0, y_ps)
+        slot_parts = ([("x1", 5), ("h", 2)], [("h", 3), ("x1", 6), ("x1", 7)], [("h", 4)])
+        for c, parts in enumerate(slot_parts):
+            y_ps = chunk_y(c + 1, f"t{(c + 1) % 2}")
+            y = y_tile(c + 1, [P, PAGES, CH], f"y{c + 1}")
+            nc.scalar.copy(y[:], y_ps[:])
+            woven = slot(c + 1, parts)
+            h_at = parts.index(("h", c + 2)) * R
+            gpsimd_h(c + 2, woven[:, h_at : h_at + R])
+            coming = weigh_split(nc.gpsimd, c + 1, y)
+            for i, (kind, chunk) in enumerate(parts):
+                if kind == "x1":
+                    weave(woven[:, i * R : (i + 1) * R], picked1, chunk, chunk + 1)
+            first_layer(c + 3)
+            bring(c + 3)
+            for q in range(PAGES):
+                put(q, c, c + 1, ready[q])
+            quantize(parts, woven[:], codes_name=f"three{c}")
+            ready = coming
+
+        y_ps = chunk_y(4, "t0")
+        y4 = y_tile(4, [P, 3, CH], "y4")
+        nc.scalar.copy(y4[:], y_ps[:, :3, :])
+        woven = slot(4, run("h", 5, 8))
+        gpsimd_h(5, woven[:, :R])
+        weighed = keep.tile([P, 3 * CH], F32, name="weighed4")
+        weigh(nc.gpsimd, weighed[:], y4[:], 4)
+        first_layer(6)
+        bring(6, "three2")
+        first_layer(7)
+        bring(7)
         for c in (6, 7):
-            first_layer(c)
-            factors(c, late[:, c - 5, :])
-        gpsimd_h(late[:, 1, :], h_end[:, R:])
-        gpsimd_h(late[:, 2, :], woven_end[:, 2 * R :])
-        for i in range(2):
-            nc.scalar.copy(woven_end[:, i * R : (i + 1) * R], h_end[:, i * R : (i + 1) * R])
+            gpsimd_h(c, woven[:, (c - 5) * R : (c - 4) * R])
+        for q in range(PAGES):
+            put(q, 3, 4, ready[q])
         for q in range(3):
-            put(q, 3, 5, weighed34[:, q, :])
-        quantize(run("h", 5, 8), woven_end[:])
-        filler = late[:, 2, : 2 * CH]
-        nc.scalar.copy(filler, y34_ps[1][:, 1, :])
-        put_weighed(3, 3, 5, filler)
-        y_end = keep.tile([P, PAGES, 3 * CH], F32, name="y_end")
+            put(q, 4, 5, weighed[:, q * CH : (q + 1) * CH])
+        quantize(run("h", 5, 8), woven[:])
+        filler = ups[7][:, :CH]
+        nc.scalar.copy(filler, y_ps[:, 3, :])
+        put_weighed(3, 4, 5, filler)
+        y_end = keep.tile([P, PAGES, 3 * CH], F32, name="picked0")
+        y_lead = keep.tile([P, CH], F32, name="y_lead")
+        y_ps = psum.tile([P, CH], F32, name="y_ps", tag="t1")
+        second_layer(y_ps[:], 0, 5, 6)
+        nc.scalar.copy(y_lead[:], y_ps[:])
+        put_weighed(0, 5, 6, y_lead[:])
         for q, bank in enumerate(("g0", "u0", "g1", "u1")):
             y_ps = psum.tile([P, 3 * CH], F32, name="y_ps", tag=bank)
-            second_layer(y_ps[:, :CH], q, 5, 6)
+            if q > 0:
+                second_layer(y_ps[:, :CH], q, 5, 6)
             second_layer(y_ps[:, CH:], q, 6, 8)
-            nc.scalar.copy(y_end[:, q, :], y_ps[:])
+            lo = 0 if q > 0 else CH
+            nc.scalar.copy(y_end[:, q, lo:], y_ps[:, lo:])
         for q in range(PAGES):
-            put_weighed(q, 5, CHUNKS, y_end[:, q, :])
+            lo = 0 if q > 0 else 1
+            put_weighed(q, 5 + lo, CHUNKS, y_end[:, q, lo * CH :])
             nc.sync.dma_start(out[q * P : (q + 1) * P, :], pages[q][:])

@@ -15,6 +15,7 @@ FP8X4 = mybir.dt.float8_e4m3fn_x4
 FP4X4 = mybir.dt.float4_e2m1fn_x4
 MULT = mybir.AluOpType.mult
 RELU = mybir.ActivationFunctionType.Relu
+COPY = mybir.ActivationFunctionType.Copy
 
 P = 128
 PACK = 4
@@ -317,13 +318,18 @@ def tile_list_relu_scat_kernel(
         ready = weigh_split(nc.vector, 0, y_ps)
         slot_parts = ([("x1", 5), ("h", 2)], [("h", 3), ("x1", 6), ("x1", 7)], [("h", 4)])
         for c, parts in enumerate(slot_parts):
-            y_ps = chunk_y(c + 1, f"t{(c + 1) % 2}")
+            y_ps = chunk_y(c + 1, "t1")
             y = y_tile(c + 1, [P, PAGES, CH], f"y{c + 1}")
             nc.scalar.copy(y[:], y_ps[:])
             woven = slot(c + 1, parts)
             h_at = parts.index(("h", c + 2)) * R
             gpsimd_h(c + 2, woven[:, h_at : h_at + R])
-            coming = weigh_split(nc.gpsimd, c + 1, y)
+            if c < 2:
+                coming = weigh_split(nc.gpsimd, c + 1, y)
+            else:
+                whole = keep.tile([P, PAGES * CH], F32, name="weighed3")
+                weigh(nc.gpsimd, whole[:], y[:], c + 1)
+                coming = [whole[:, q * CH : (q + 1) * CH] for q in range(PAGES)]
             for i, (kind, chunk) in enumerate(parts):
                 if kind == "x1":
                     weave(woven[:, i * R : (i + 1) * R], picked1, chunk, chunk + 1)
@@ -334,41 +340,60 @@ def tile_list_relu_scat_kernel(
             quantize(parts, woven[:], codes_name=f"three{c}")
             ready = coming
 
-        y_ps = chunk_y(4, "t0")
-        y4 = y_tile(4, [P, 3, CH], "y4")
-        nc.scalar.copy(y4[:], y_ps[:, :3, :])
+        turned_out = psum.tile([P, P], F32, name="turned_out", tag="t0")
+        nc.tensor.transpose(turned_out[:], gain_out[:, 4 * CH : 5 * CH], ident[:])
+        by_pick = keep.tile([P, P // LANE], F32, name="by_pick")
+        nc.scalar.copy(by_pick[:], turned_out[:, ::LANE])
+        codes, scales, lo = quantised["h", 4]
+        across_ps = psum.tile([P, 2 * P], F32, name="across_ps", tag="t1")
+        nc.tensor.matmul_mx(
+            across_ps[:],
+            lhsT=codes[:, lo : lo + CH].bitcast(FP8X4),
+            lhsT_scale=scales[:, lo : lo + CH],
+            rhs=wd_w[:, : 4 * P].bitcast(FP4X4),
+            rhs_scale=wd_s[:, : 2 * P],
+            start=True,
+            stop=True,
+        )
+        y_ps = psum.tile([P, PAGES, CH], F32, name="y_ps", tag="t0")
+        for q in (2, 3):
+            second_layer(y_ps[:, q, :], q, 4, 5)
+        across = keep.tile([P, 2 * P], F32, name="across", align_bytes=64)
+        for g in range(P // LANE):
+            nc.scalar.activation(
+                across[:].rearrange("p (q g r) -> p g q r", q=2, r=LANE)[:, g],
+                across_ps[:].rearrange("p (q g r) -> p g q r", q=2, r=LANE)[:, g],
+                COPY,
+                scale=by_pick[:, g : g + 1],
+            )
+        back = psum.tile([P, 2, CH], F32, name="back", tag="u2")
+        for q in range(2):
+            nc.tensor.transpose(back[:, q, :], across[:, q * P : (q + 1) * P], ident[:])
+        weighed = keep.tile([P, 2 * CH], F32, name="weighed4")
+        nc.scalar.copy(weighed[:], back[:].rearrange("p q j -> p (q j)"))
         woven = slot(4, run("h", 5, 8))
         gpsimd_h(5, woven[:, :R])
-        weighed = keep.tile([P, 3 * CH], F32, name="weighed4")
-        weigh(nc.gpsimd, weighed[:], y4[:], 4)
         first_layer(6)
-        bring(6, "three2")
+        bring(6)
         first_layer(7)
         bring(7)
         for c in (6, 7):
             gpsimd_h(c, woven[:, (c - 5) * R : (c - 4) * R])
         for q in range(PAGES):
             put(q, 3, 4, ready[q])
-        for q in range(3):
+        for q in range(2):
             put(q, 4, 5, weighed[:, q * CH : (q + 1) * CH])
         quantize(run("h", 5, 8), woven[:])
-        filler = ups[7][:, :CH]
-        nc.scalar.copy(filler, y_ps[:, 3, :])
-        put_weighed(3, 4, 5, filler)
+        filler = ups[7][:, : 2 * CH]
+        nc.scalar.copy(filler, y_ps[:, 2:, :].rearrange("p q j -> p (q j)"))
+        for q in (2, 3):
+            put_weighed(q, 4, 5, filler[:, (q - 2) * CH : (q - 1) * CH])
         y_end = keep.tile([P, PAGES, 3 * CH], F32, name="picked0")
-        y_lead = keep.tile([P, CH], F32, name="y_lead")
-        y_ps = psum.tile([P, CH], F32, name="y_ps", tag="t1")
-        second_layer(y_ps[:], 0, 5, 6)
-        nc.scalar.copy(y_lead[:], y_ps[:])
-        put_weighed(0, 5, 6, y_lead[:])
         for q, bank in enumerate(("g0", "u0", "g1", "u1")):
             y_ps = psum.tile([P, 3 * CH], F32, name="y_ps", tag=bank)
-            if q > 0:
-                second_layer(y_ps[:, :CH], q, 5, 6)
+            second_layer(y_ps[:, :CH], q, 5, 6)
             second_layer(y_ps[:, CH:], q, 6, 8)
-            lo = 0 if q > 0 else CH
-            nc.scalar.copy(y_end[:, q, lo:], y_ps[:, lo:])
+            nc.scalar.copy(y_end[:, q, :], y_ps[:])
         for q in range(PAGES):
-            lo = 0 if q > 0 else 1
-            put_weighed(q, 5 + lo, CHUNKS, y_end[:, q, lo * CH :])
+            put_weighed(q, 5, CHUNKS, y_end[:, q, :])
             nc.sync.dma_start(out[q * P : (q + 1) * P, :], pages[q][:])

@@ -45,17 +45,17 @@ def tile_list_relu_scat_kernel(
         pick = keep.tile([P, J // LANE], U16, name="pick")
         place = keep.tile([P, J // LANE], U16, name="place")
         x_rows = xT.rearrange("(a p t) n -> a t p n", p=P, t=PACK)
-        planes = [keep.tile([P, T], F32, name=f"plane{m}") for m in range(PLANES)]
+        planes = [keep.tile([P, T], F32, name=f"plane{m}", align_bytes=256) for m in range(PLANES)]
         gain = keep.tile([P, J], F32, name="gain")
-        gain_out = keep.tile([P, J], F32, name="gain_out")
-        raw_w = [[keep.tile([P, R], U16, name=f"raw_w{w}{a}") for a in range(PASSES)] for w in range(2)]
+        gain_out = keep.tile([P, J], F32, name="gain_out", align_bytes=256)
+        raw_w = [[keep.tile([P, R], U16, name=f"raw_w{w}{a}", align_bytes=256) for a in range(PASSES)] for w in range(2)]
         w_words = [[keep.tile([P, 2 * R], U8, name=f"w_words{w}{a}", align_bytes=64) for a in range(PASSES)] for w in range(2)]
         w_scales = [keep.tile([P, PASSES * R], U8, name=f"w_scales{w}", align_bytes=64) for w in range(2)]
-        raw_s = keep.tile([P, R], U8, name="page1")
+        raw_s = keep.tile([P, R], U8, name="page1", align_bytes=256)
         wd_w = keep.tile([P, 2 * N], U8, name="wd_w", align_bytes=64)
         wd_s = keep.tile([P, N], U8, name="wd_s", align_bytes=64)
         ident = keep.tile([P, P], F32, name="ident")
-        blank = keep.tile([P, P], F32, name="page0")
+        blank = keep.tile([P, P], F32, name="page0", align_bytes=256)
         rows = keep.tile([P, CH], F32, name="rows")
 
         nc.gpsimd.memset(blank[:], 0.0)
@@ -105,7 +105,7 @@ def tile_list_relu_scat_kernel(
                 nc.scalar.copy(dst[:, i0 * CH : i1 * CH], back[:].rearrange("p i e -> p (i e)"))
 
         spread(0, gain, (HEAD, CHUNKS // 2, CHUNKS), ("u0", "u1"), ("wide1", "wide4"))
-        pages = [keep.tile([P, T], F32, name=f"page{q}") for q in range(2)]
+        pages = [keep.tile([P, T], F32, name=f"page{q}", align_bytes=256) for q in range(2)]
         for page in pages:
             nc.gpsimd.memset(page[:], 0.0)
 
@@ -169,7 +169,7 @@ def tile_list_relu_scat_kernel(
         for h in range(2):
             gather(picked0[:, PACK - 1, h * HALF : (h + 1) * HALF], PACK - 1, h * CHUNKS // 2, (h + 1) * CHUNKS // 2)
         for q in range(2, PAGES):
-            pages.append(keep.tile([P, T], F32, name=f"plane{q - 2}"))
+            pages.append(keep.tile([P, T], F32, name=f"plane{q - 2}", align_bytes=256))
             nc.gpsimd.memset(pages[q][:], 0.0)
         woven0 = [keep.tile([P, HALF * PACK], BF16, name=f"woven0_{h}", align_bytes=64) for h in range(2)]
         for h in range(2):

@@ -171,9 +171,9 @@ def tile_list_relu_scat_kernel(
         for q in range(2, PAGES):
             pages.append(keep.tile([P, T], F32, name=f"plane{q - 2}", align_bytes=256))
             nc.gpsimd.memset(pages[q][:], 0.0)
-        woven0 = [keep.tile([P, HALF * PACK], BF16, name=f"woven0_{h}", align_bytes=64) for h in range(2)]
-        for h in range(2):
-            weave(woven0[h][:], picked0[:], h * CHUNKS // 2, (h + 1) * CHUNKS // 2)
+        woven0 = {c0: keep.tile([P, (c1 - c0) * R], BF16, name=f"woven0_{c0}", align_bytes=64) for c0, c1 in ((0, 4), (4, 6), (6, 8))}
+        for c0, c1 in ((0, 4), (4, 6), (6, 8)):
+            weave(woven0[c0][:], picked0[:], c0, c1)
         for w, a in [WORDS_BEHIND[m] for m in sorted(WORDS_BEHIND)]:
             nc.scalar.copy(
                 w_words[w][a][:].bitcast(U16).rearrange("p (t m) -> p t m", t=PACK),
@@ -184,7 +184,8 @@ def tile_list_relu_scat_kernel(
         picked1 = picked1_flat[:, : PACK * J].rearrange("p (t j) -> p t j", t=PACK)
         for t in range(PACK - 1):
             gather(picked1[:, t, :], PACK + t, 0, CHUNKS)
-        quantize(run("x0", 0, CHUNKS // 2), woven0[0][:])
+        quantize(run("x0", 0, 4), woven0[0][:])
+        quantize(run("x0", 4, 6), woven0[4][:])
 
         sums = {}
 
@@ -237,11 +238,17 @@ def tile_list_relu_scat_kernel(
 
         gates, ups = {}, {}
 
-        def bring(c, up_buffer=None):
+        def bring_gate(c):
             gates[c] = keep.tile([P, R], F32, name=f"gate{c}", align_bytes=64)
-            ups[c] = keep.tile([P, R], F32, name=up_buffer or f"up{c}", align_bytes=64)
             nc.scalar.activation(words(gates[c][:]), by_pairs(sums[c][0]), RELU)
+
+        def bring_up(c, buffer):
+            ups[c] = keep.tile([P, R], F32, name=buffer, align_bytes=64)
             nc.scalar.copy(words(ups[c][:]), by_pairs(sums[c][1]))
+
+        def bring(c):
+            bring_gate(c)
+            bring_up(c, f"up{c}")
 
         def gpsimd_h(c, product):
             nc.gpsimd.tensor_tensor(product, ups[c][:], gates[c][:], MULT)
@@ -294,7 +301,7 @@ def tile_list_relu_scat_kernel(
             woven1_12.rearrange("p (c i t) -> p c t i", i=4, t=PACK)[:, :, 2:, :],
             moved[:, :, : 2 * CH].rearrange("p t (c i) -> p c t i", i=4),
         )
-        quantize(run("x0", CHUNKS // 2, CHUNKS), woven0[1][:], codes_name="woven1_0")
+        quantize(run("x0", 6, 8), woven0[6][:], codes_name="woven1_0")
         quantize(run("x1", 1, 3), woven1_12)
         first_layer(1, (1,))
         first_layer(2, (1,))
@@ -316,6 +323,10 @@ def tile_list_relu_scat_kernel(
             return [three[:, q * CH : (q + 1) * CH] for q in range(3)] + [one[:]]
 
         ready = weigh_split(nc.vector, 0, y_ps)
+        turned_out = psum.tile([P, P], F32, name="turned_out", tag="t0")
+        nc.tensor.transpose(turned_out[:], gain_out[:, 4 * CH : 5 * CH], ident[:])
+        by_pick = keep.tile([P, P // LANE], F32, name="by_pick")
+        nc.scalar.copy(by_pick[:], turned_out[:, ::LANE])
         slot_parts = ([("x1", 5), ("h", 2)], [("h", 3), ("x1", 6), ("x1", 7)], [("h", 4)])
         for c, parts in enumerate(slot_parts):
             y_ps = chunk_y(c + 1, "t1")
@@ -340,10 +351,10 @@ def tile_list_relu_scat_kernel(
             quantize(parts, woven[:], codes_name=f"three{c}")
             ready = coming
 
-        turned_out = psum.tile([P, P], F32, name="turned_out", tag="t0")
-        nc.tensor.transpose(turned_out[:], gain_out[:, 4 * CH : 5 * CH], ident[:])
-        by_pick = keep.tile([P, P // LANE], F32, name="by_pick")
-        nc.scalar.copy(by_pick[:], turned_out[:, ::LANE])
+        first_layer(6)
+        bring(6)
+        first_layer(7)
+        bring_gate(7)
         codes, scales, lo = quantised["h", 4]
         across_ps = psum.tile([P, 2 * P], F32, name="across_ps", tag="t1")
         nc.tensor.matmul_mx(
@@ -355,9 +366,6 @@ def tile_list_relu_scat_kernel(
             start=True,
             stop=True,
         )
-        y_ps = psum.tile([P, PAGES, CH], F32, name="y_ps", tag="t0")
-        for q in (2, 3):
-            second_layer(y_ps[:, q, :], q, 4, 5)
         across = keep.tile([P, 2 * P], F32, name="across", align_bytes=64)
         for g in range(P // LANE):
             nc.scalar.activation(
@@ -369,14 +377,15 @@ def tile_list_relu_scat_kernel(
         back = psum.tile([P, 2, CH], F32, name="back", tag="u2")
         for q in range(2):
             nc.tensor.transpose(back[:, q, :], across[:, q * P : (q + 1) * P], ident[:])
+        y_ps = psum.tile([P, PAGES, CH], F32, name="y_ps", tag="t0")
+        for q in (2, 3):
+            second_layer(y_ps[:, q, :], q, 4, 5)
         weighed = keep.tile([P, 2 * CH], F32, name="weighed4")
-        nc.scalar.copy(weighed[:], back[:].rearrange("p q j -> p (q j)"))
+        for q in range(2):
+            nc.scalar.copy(weighed[:, q * CH : (q + 1) * CH], back[:, q, :])
+        bring_up(7, "across")
         woven = slot(4, run("h", 5, 8))
         gpsimd_h(5, woven[:, :R])
-        first_layer(6)
-        bring(6)
-        first_layer(7)
-        bring(7)
         for c in (6, 7):
             gpsimd_h(c, woven[:, (c - 5) * R : (c - 4) * R])
         for q in range(PAGES):

@@ -175,15 +175,19 @@ def tile_list_relu_scat_kernel(
         for c0, c1 in ((0, 4), (4, 6), (6, 8)):
             weave(woven0[c0][:], picked0[:], c0, c1)
         for w, a in [WORDS_BEHIND[m] for m in sorted(WORDS_BEHIND)]:
+            t0 = 1 - a
             nc.scalar.copy(
-                w_words[w][a][:].bitcast(U16).rearrange("p (t m) -> p t m", t=PACK),
-                raw_w[w][a][:].rearrange("p (m t) -> p t m", t=PACK),
+                w_words[w][a][:].bitcast(U16).rearrange("p (t m) -> p t m", t=PACK)[:, t0:, :],
+                raw_w[w][a][:].rearrange("p (m t) -> p t m", t=PACK)[:, t0:, :],
             )
 
         picked1_flat = keep.tile([P, PACK * J + 5 * CH], F32, name="picked1")
         picked1 = picked1_flat[:, : PACK * J].rearrange("p (t j) -> p t j", t=PACK)
         for t in range(PACK - 1):
             gather(picked1[:, t, :], PACK + t, 0, CHUNKS)
+        first_words = keep.tile([P, 2, 2 * P], U8, name="plane5", align_bytes=256)
+        for w in range(2):
+            nc.scalar.copy(first_words[:, w, :].bitcast(U16), raw_w[w][0][:, ::PACK])
         quantize(run("x0", 0, 4), woven0[0][:])
         quantize(run("x0", 4, 6), woven0[4][:])
 
@@ -199,7 +203,7 @@ def tile_list_relu_scat_kernel(
                     for t in range(PACK):
                         nc.tensor.matmul_mx(
                             sums[c][w][:, t, :],
-                            lhsT=w_words[w][a][:, 2 * P * t : 2 * P * (t + 1)].bitcast(FP4X4),
+                            lhsT=(w_words[w][a][:, 2 * P * t : 2 * P * (t + 1)] if a or t else first_words[:, w, :]).bitcast(FP4X4),
                             lhsT_scale=w_scales[w][:, a * R + P * t : a * R + P * (t + 1)],
                             start=(a == 0 and t == 0),
                             stop=(a == PASSES - 1 and t == PACK - 1),

@@ -181,7 +181,7 @@ def tile_list_relu_scat_kernel(
                 raw_w[w][a][:].rearrange("p (m t) -> p t m", t=PACK)[:, t0:, :],
             )
 
-        picked1_flat = keep.tile([P, PACK * J + 5 * CH], F32, name="picked1")
+        picked1_flat = keep.tile([P, PACK * J + 7 * CH], F32, name="picked1")
         picked1 = picked1_flat[:, : PACK * J].rearrange("p (t j) -> p t j", t=PACK)
         for t in range(PACK - 1):
             gather(picked1[:, t, :], PACK + t, 0, CHUNKS)
@@ -296,11 +296,12 @@ def tile_list_relu_scat_kernel(
         for woven, c0, c1 in ((woven1_0[:], 0, 1), (woven1_12, 1, 3), (slot0[:, R:], 3, 5)):
             weave(woven, picked1, c0, c1, 0, 2)
         gather(last[:, :CH], PLANES - 1, 0, 1)
-        gather(last[:, 3 * CH : 5 * CH], PLANES - 1, 1, 3)
+        gather(last[:, 4 * CH : 6 * CH], PLANES - 1, 1, 3)
+        gather(last[:, 3 * CH : 4 * CH], PLANES - 1, 3, 4)
         weave(woven1_0[:], picked1, 0, 1, 2)
         quantize(run("x1", 0, 1), woven1_0[:])
         first_layer(0, (1,))
-        moved = picked1_flat[:, 2 * J + CH : 2 * J + CH + 2 * (J + 2 * CH)].rearrange("p (t j) -> p t j", t=2)
+        moved = picked1_flat[:, 2 * J + CH : 2 * J + CH + 2 * (J + 3 * CH)].rearrange("p (t j) -> p t j", t=2)
         nc.scalar.copy(
             woven1_12.rearrange("p (c i t) -> p c t i", i=4, t=PACK)[:, :, 2:, :],
             moved[:, :, : 2 * CH].rearrange("p t (c i) -> p c t i", i=4),
@@ -309,7 +310,7 @@ def tile_list_relu_scat_kernel(
         quantize(run("x1", 1, 3), woven1_12)
         first_layer(1, (1,))
         first_layer(2, (1,))
-        gather(last[:, 3 * CH :], PLANES - 1, 3, CHUNKS)
+        gather(last[:, 4 * CH :], PLANES - 1, 4, CHUNKS)
         woven_h0 = keep.tile([P, R], BF16, name="woven_h0", align_bytes=64)
         vector_h(0, woven_h0[:])
         vector_h(1, slot0[:, :R])

@@ -316,7 +316,11 @@ def tile_list_relu_scat_kernel(
         vector_h(1, slot0[:, :R])
         weave(slot0[:, R:], picked1, 3, 5, 2)
         quantize(run("h", 0, 1), woven_h0[:])
-        y_ps = chunk_y(0, "t0")
+        lead_ps = psum.tile([P, 1, CH], F32, name="lead_ps", tag="t1")
+        second_layer(lead_ps[:, 0, :], 0, 0, 1)
+        y_ps = psum.tile([P, 3, CH], F32, name="y_ps", tag="t0")
+        for q in range(1, PAGES):
+            second_layer(y_ps[:, q - 1, :], q, 0, 1)
         bring(2)
         quantize(parts0, slot0[:])
 
@@ -327,12 +331,18 @@ def tile_list_relu_scat_kernel(
             weigh(engine, one[:], y[:, 3:, :], c)
             return [three[:, q * CH : (q + 1) * CH] for q in range(3)] + [one[:]]
 
-        ready = weigh_split(nc.vector, 0, y_ps)
+        lead = keep.tile([P, CH], F32, name="lead0")
+        two = keep.tile([P, 2 * CH], F32, name="three0", align_bytes=64)
+        one = keep.tile([P, CH], F32, name="one0")
+        weigh(nc.vector, lead[:], lead_ps[:], 0)
+        weigh(nc.vector, two[:], y_ps[:, :2, :], 0)
+        weigh(nc.vector, one[:], y_ps[:, 2:, :], 0)
+        ready = [lead[:], two[:, :CH], two[:, CH:], one[:]]
         turned_out = psum.tile([P, P], F32, name="turned_out", tag="t0")
         nc.tensor.transpose(turned_out[:], gain_out[:, 4 * CH : 5 * CH], ident[:])
         by_pick = keep.tile([P, P // LANE], F32, name="by_pick")
         nc.scalar.copy(by_pick[:], turned_out[:, ::LANE])
-        slot_parts = ([("x1", 5), ("h", 2)], [("h", 3), ("x1", 6), ("x1", 7)], [("h", 4)])
+        slot_parts = ([("x1", 5), ("h", 2)], [("h", 3), ("x1", 6)], [("x1", 7), ("h", 4)])
         for c, parts in enumerate(slot_parts):
             y_ps = chunk_y(c + 1, "t1")
             y = y_tile(c + 1, [P, PAGES, CH], f"y{c + 1}")
@@ -358,8 +368,6 @@ def tile_list_relu_scat_kernel(
 
         first_layer(6)
         bring(6)
-        first_layer(7)
-        bring_gate(7)
         codes, scales, lo = quantised["h", 4]
         across_ps = psum.tile([P, 2 * P], F32, name="across_ps", tag="t1")
         nc.tensor.matmul_mx(
@@ -388,6 +396,8 @@ def tile_list_relu_scat_kernel(
         weighed = keep.tile([P, 2 * CH], F32, name="weighed4")
         for q in range(2):
             nc.scalar.copy(weighed[:, q * CH : (q + 1) * CH], back[:, q, :])
+        first_layer(7)
+        bring_gate(7)
         bring_up(7, "across")
         woven = slot(4, run("h", 5, 8))
         gpsimd_h(5, woven[:, :R])

@@ -302,19 +302,21 @@ def tile_list_relu_scat_kernel(
         quantize(run("x1", 0, 1), woven1_0[:])
         first_layer(0, (1,))
         moved = picked1_flat[:, 2 * J + CH : 2 * J + CH + 2 * (J + 3 * CH)].rearrange("p (t j) -> p t j", t=2)
-        nc.scalar.copy(
-            woven1_12.rearrange("p (c i t) -> p c t i", i=4, t=PACK)[:, :, 2:, :],
-            moved[:, :, : 2 * CH].rearrange("p t (c i) -> p c t i", i=4),
-        )
+        for half in range(2):
+            nc.scalar.copy(
+                woven1_12[:, half * R : (half + 1) * R].rearrange("p (c i t) -> p c t i", i=4, t=PACK)[:, :, 2:, :],
+                moved[:, :, half * CH : (half + 1) * CH].rearrange("p t (c i) -> p c t i", i=4),
+            )
         quantize(run("x0", 6, 8), woven0[6][:], codes_name="woven1_0")
-        quantize(run("x1", 1, 3), woven1_12)
-        first_layer(1, (1,))
-        first_layer(2, (1,))
+        for c in (1, 2):
+            quantize(run("x1", c, c + 1), woven1_12[:, (c - 1) * R : c * R])
+            first_layer(c, (1,))
         gather(last[:, 4 * CH :], PLANES - 1, 4, CHUNKS)
         woven_h0 = keep.tile([P, R], BF16, name="woven_h0", align_bytes=64)
         vector_h(0, woven_h0[:])
         vector_h(1, slot0[:, :R])
-        weave(slot0[:, R:], picked1, 3, 5, 2)
+        for c in (3, 4):
+            weave(slot0[:, (c - 2) * R : (c - 1) * R], picked1, c, c + 1, 2)
         quantize(run("h", 0, 1), woven_h0[:])
         lead_ps = psum.tile([P, 1, CH], F32, name="lead_ps", tag="t1")
         second_layer(lead_ps[:, 0, :], 0, 0, 1)

from contextlib import ExitStack

import concourse.mybir as mybir

K, R, N, T, J = 1024, 512, 512, 2048, 1024
FLOPS = 2 * (2 * K * R + R * N) * J

F32 = mybir.dt.float32
BF16 = mybir.dt.bfloat16
I32 = mybir.dt.int32
U32 = mybir.dt.uint32
U16 = mybir.dt.uint16
U8 = mybir.dt.uint8
FP8X4 = mybir.dt.float8_e4m3fn_x4
FP4X4 = mybir.dt.float4_e2m1fn_x4
MULT = mybir.AluOpType.mult
RELU = mybir.ActivationFunctionType.Relu
COPY = mybir.ActivationFunctionType.Copy

P = 128
PACK = 4
PASSES = K // (P * PACK)
PLANES = PASSES * PACK
CH = 128
CHUNKS = J // CH
PAGES = N // P
LANE = 16
QUADRANT = 32
SCALE_ROWS = 4
HALF = J // 2
BANKS = 3
HEAD = 1
WORDS_BEHIND = {2: (0, 1), 3: (1, 1), 4: (0, 0), 5: (1, 0)}


def tile_list_relu_scat_kernel(
    tc, xT, wgt, wg_words, wg_scales, wu_words, wu_scales, wd_words, wd_scales, wgo, offs, offs2, out
):
    nc = tc.nc
    with ExitStack() as ctx:
        keep = ctx.enter_context(tc.tile_pool(name="keep", bufs=1))
        ring = ctx.enter_context(tc.tile_pool(name="ring", bufs=1))
        psum = ctx.enter_context(tc.psum_pool(name="psum", bufs=1))

        pick = keep.tile([P, J // LANE], U16, name="pick")
        place = keep.tile([P, J // LANE], U16, name="place")
        x_rows = xT.rearrange("(a p t) n -> a t p n", p=P, t=PACK)
        planes = [keep.tile([P, T], F32, name=f"plane{m}", align_bytes=256) for m in range(PLANES)]
        gain = keep.tile([P, J], F32, name="gain")
        gain_out = keep.tile([P, J], F32, name="gain_out", align_bytes=256)
        raw_w = [[keep.tile([P, R], U16, name=f"raw_w{w}{a}", align_bytes=256) for a in range(PASSES)] for w in range(2)]
        w_words = [[keep.tile([P, 2 * R], U8, name=f"w_words{w}{a}", align_bytes=64) for a in range(PASSES)] for w in range(2)]
        w_scales = [keep.tile([P, PASSES * R], U8, name=f"w_scales{w}", align_bytes=64) for w in range(2)]
        raw_s = keep.tile([P, R], U8, name="page1", align_bytes=256)
        wd_w = keep.tile([P, 2 * N], U8, name="wd_w", align_bytes=64)
        wd_s = keep.tile([P, N], U8, name="wd_s", align_bytes=64)
        ident = keep.tile([P, P], F32, name="ident")
        blank = keep.tile([P, P], F32, name="page0", align_bytes=256)
        rows = keep.tile([P, CH], F32, name="rows")

        nc.gpsimd.memset(blank[:], 0.0)
        nc.gpsimd.memset(rows[P // 2 :, :], 0.0)
        nc.gpsimd.affine_select(
            out=ident[:],
            in_=blank[:],
            compare_op=mybir.AluOpType.not_equal,
            fill=1.0,
            base=0,
            pattern=[[-1, P]],
            channel_multiplier=1,
        )
        nc.vector.memset(raw_s[2 * QUADRANT :, :].bitcast(I32), 0)
        for scales in (*w_scales, wd_s):
            nc.vector.memset(scales[:].bitcast(I32), 0)

        nc.sync.dma_start(rows[: P // 2, :], wgt.rearrange("p (h n) -> (p h) n", h=2)[:: LANE + 1])
        nc.sync.dma_start(pick[:], offs)
        nc.sync.dma_start(planes[0][:], x_rows[0, 0])
        nc.sync.dma_start(gain[:, : HEAD * CH], wgt[:, : HEAD * CH])
        for w, dram_scales in enumerate((wg_scales, wu_scales)):
            nc.scalar.dma_start(
                raw_s[QUADRANT * w : QUADRANT * (w + 1), :].bitcast(I32),
                dram_scales.bitcast(I32).rearrange("a q n -> q a n"),
            )

        dealt_s = keep.tile([P, R], U8, name="dealt_s")
        nc.vector.tensor_copy(
            dealt_s[:].rearrange("p (t m) -> p t m", t=PACK), raw_s[:].rearrange("p (m t) -> p t m", t=PACK)
        )
        turned = psum.tile([P, P], F32, name="turned", tag="t0")
        nc.tensor.transpose(turned[:], rows[:], ident[:])

        def spread(w, dst, cuts, banks, names):
            groups = turned[:, w * P // 2 : (w + 1) * P // 2].rearrange("p (g i) -> p i g", i=CHUNKS)
            for i0, i1, bank, name in zip(cuts, cuts[1:], banks, names):
                step = i1 - i0
                wide = keep.tile([P, step, P], F32, name=name)
                back = psum.tile([P, step, CH], F32, name="back", tag=bank)
                nc.scalar.copy(
                    wide[:].rearrange("p i (g r) -> p i g r", r=LANE),
                    groups[:, i0:i1, :].unsqueeze(3).to_broadcast([P, step, P // LANE, LANE]),
                )
                for i in range(step):
                    nc.tensor.transpose(back[:, i, :], wide[:, i, :], ident[:])
                nc.scalar.copy(dst[:, i0 * CH : i1 * CH], back[:].rearrange("p i e -> p (i e)"))

        spread(0, gain, (HEAD, CHUNKS // 2, CHUNKS), ("u0", "u1"), ("wide1", "wide4"))
        pages = [keep.tile([P, T], F32, name=f"page{q}", align_bytes=256) for q in range(2)]
        for page in pages:
            nc.gpsimd.memset(page[:], 0.0)

        def move_scales(w):
            for d in range(P // QUADRANT):
                first = QUADRANT * w + 2 * SCALE_ROWS * d
                live = w_scales[w][QUADRANT * d : QUADRANT * d + SCALE_ROWS, :]
                nc.sync.dma_start(
                    live.bitcast(I32).rearrange("p (a n) -> p a n", a=PASSES),
                    dealt_s[first : first + 2 * SCALE_ROWS, :].bitcast(I32),
                )

        for m in range(1, PLANES):
            nc.sync.dma_start(planes[m][:], x_rows[m // PACK, m % PACK])
            if m in (1, 2):
                move_scales(m - 1)
            if m in WORDS_BEHIND:
                w, a = WORDS_BEHIND[m]
                nc.sync.dma_start(raw_w[w][a][:].bitcast(I32), (wg_words, wu_words)[w][a].bitcast(I32))
        nc.sync.dma_start(place[:], offs2)
        nc.sync.dma_start(wd_w[:].bitcast(I32), wd_words[0].bitcast(I32))
        wd_rows = wd_scales.bitcast(I32).rearrange("a (d r) n -> d r (a n)", r=SCALE_ROWS)
        for d in range(P // QUADRANT):
            nc.sync.dma_start(wd_s[QUADRANT * d : QUADRANT * d + SCALE_ROWS, :].bitcast(I32), wd_rows[d])
        nc.sync.dma_start(gain_out[:], wgo)

        def gather(dst, m, c0, c1):
            nc.vector.tensor_tensor(
                dst, planes[m][:].indirect(pick[:, c0 * CH // LANE : c1 * CH // LANE]), gain[:, c0 * CH : c1 * CH], MULT
            )

        def weave(woven, picked, c0, c1, t0=0, t1=PACK):
            nc.scalar.copy(
                woven.rearrange("p (c i t) -> p c t i", i=4, t=PACK)[:, :, t0:t1, :],
                picked[:, t0:t1, c0 * CH : c1 * CH].rearrange("p t (c i) -> p c t i", i=4),
            )

        quantised = {}

        def quantize(parts, woven, codes_name=None):
            label = "%s_%d" % parts[0]
            codes = keep.tile([P, len(parts) * CH], U32, name=codes_name or f"codes_{label}", align_bytes=64)
            scales = keep.tile([P, len(parts) * CH], U8, name=f"scales_{label}", align_bytes=64)
            nc.vector.quantize_mx(out=codes[:].bitcast(FP8X4), scales=scales[:], in_=woven)
            for i, part in enumerate(parts):
                quantised[part] = (codes, scales, i * CH)

        def run(kind, c0, c1):
            return [(kind, c) for c in range(c0, c1)]

        def moving(kind, c0, c1):
            codes, scales, lo = quantised[kind, c0]
            cols = slice(lo, lo + (c1 - c0) * CH)
            return dict(rhs=codes[:, cols].bitcast(FP8X4), rhs_scale=scales[:, cols])

        picked0 = keep.tile([P, PACK, J], F32, name="picked0")
        for c0, c1 in ((0, HEAD), (HEAD, CHUNKS // 2), (CHUNKS // 2, CHUNKS)):
            gather(picked0[:, 0, c0 * CH : c1 * CH], 0, c0, c1)
        for t in range(1, PACK - 1):
            gather(picked0[:, t, :], t, 0, CHUNKS)
        for h in range(2):
            gather(picked0[:, PACK - 1, h * HALF : (h + 1) * HALF], PACK - 1, h * CHUNKS // 2, (h + 1) * CHUNKS // 2)
        for q in range(2, PAGES):
            pages.append(keep.tile([P, T], F32, name=f"plane{q - 2}", align_bytes=256))
            nc.gpsimd.memset(pages[q][:], 0.0)
        woven0 = {c0: keep.tile([P, (c1 - c0) * R], BF16, name=f"woven0_{c0}", align_bytes=64) for c0, c1 in ((0, 4), (4, 6), (6, 8))}
        for c0, c1 in ((0, 4), (4, 6), (6, 8)):
            weave(woven0[c0][:], picked0[:], c0, c1)
        for w, a in [WORDS_BEHIND[m] for m in sorted(WORDS_BEHIND)]:
            t0 = 1 - a
            nc.scalar.copy(
                w_words[w][a][:].bitcast(U16).rearrange("p (t m) -> p t m", t=PACK)[:, t0:, :],
                raw_w[w][a][:].rearrange("p (m t) -> p t m", t=PACK)[:, t0:, :],
            )

        picked1_flat = keep.tile([P, PACK * J + 7 * CH], F32, name="picked1")
        picked1 = picked1_flat[:, : PACK * J].rearrange("p (t j) -> p t j", t=PACK)
        for t in range(PACK - 1):
            gather(picked1[:, t, :], PACK + t, 0, CHUNKS)
        first_words = keep.tile([P, 2, 2 * P], U8, name="plane5", align_bytes=256)
        for w in range(2):
            nc.scalar.copy(first_words[:, w, :].bitcast(U16), raw_w[w][0][:, ::PACK])
        quantize(run("x0", 0, 4), woven0[0][:])
        quantize(run("x0", 4, 6), woven0[4][:])

        sums = {}

        def first_layer(c, passes=range(PASSES), sides=range(2)):
            if 0 in passes:
                g_ps = psum.tile([P, PACK, CH], F32, name="g_ps", tag=f"g{c % BANKS}")
                u_ps = psum.tile([P, PACK, CH], F32, name="u_ps", tag=f"u{c % BANKS}")
                sums[c] = (g_ps, u_ps)
            for a in passes:
                for w in sides:
                    for t in range(PACK):
                        nc.tensor.matmul_mx(
                            sums[c][w][:, t, :],
                            lhsT=(w_words[w][a][:, 2 * P * t : 2 * P * (t + 1)] if a or t else first_words[:, w, :]).bitcast(FP4X4),
                            lhsT_scale=w_scales[w][:, a * R + P * t : a * R + P * (t + 1)],
                            start=(a == 0 and t == 0),
                            stop=(a == PASSES - 1 and t == PACK - 1),
                            **moving(f"x{a}", c, c + 1),
                        )

        def by_pairs(bank):
            return bank[:].rearrange("p t (c i) -> p c t i", i=2)

        def walk(ap):
            return ap.rearrange("p (c t i) -> p c t i", t=PACK, i=2)

        def words(ap):
            return ap.rearrange("p (c i t) -> p c t i", t=PACK, i=2)

        def second_layer(dst, q, c0, c1):
            nc.tensor.matmul_mx(
                dst,
                lhsT=wd_w[:, 2 * P * q : 2 * P * (q + 1)].bitcast(FP4X4),
                lhsT_scale=wd_s[:, P * q : P * (q + 1)],
                start=True,
                stop=True,
                **moving("h", c0, c1),
            )

        def chunk_y(c, bank):
            y_ps = psum.tile([P, PAGES, CH], F32, name="y_ps", tag=bank)
            for q in range(PAGES):
                second_layer(y_ps[:, q, :], q, c, c + 1)
            return y_ps

        def vector_h(c, woven):
            gate = keep.tile([P, R], F32, name=f"gate{c}", align_bytes=64)
            nc.scalar.activation(walk(gate[:]), by_pairs(sums[c][0]), RELU)
            nc.vector.tensor_tensor(words(woven), by_pairs(sums[c][1]), walk(gate[:]), MULT)

        gates, ups = {}, {}

        def bring_gate(c):
            gates[c] = keep.tile([P, R], F32, name=f"gate{c}", align_bytes=64)
            nc.scalar.activation(words(gates[c][:]), by_pairs(sums[c][0]), RELU)

        def bring_up(c, buffer):
            ups[c] = keep.tile([P, R], F32, name=buffer, align_bytes=64)
            nc.scalar.copy(words(ups[c][:]), by_pairs(sums[c][1]))

        def bring(c):
            bring_gate(c)
            bring_up(c, f"up{c}")

        def gpsimd_h(c, product):
            nc.gpsimd.tensor_tensor(product, ups[c][:], gates[c][:], MULT)

        def weigh(engine, dst, src, c0):
            count, width = src.shape[1], src.shape[2]
            engine.tensor_tensor(
                dst.rearrange("p (q j) -> p q j", q=count),
                src,
                gain_out[:, c0 * CH : c0 * CH + width].unsqueeze(1).to_broadcast([P, count, width]),
                MULT,
            )

        def window(q, c0, c1):
            return pages[q][:].indirect(place[:, c0 * CH // LANE : c1 * CH // LANE])

        def put(q, c0, c1, src):
            nc.vector.tensor_copy(window(q, c0, c1), src)

        def put_weighed(q, c0, c1, src):
            nc.vector.tensor_tensor(window(q, c0, c1), src, gain_out[:, c0 * CH : c1 * CH], MULT)

        KIB = 1024
        MID = 3 * KIB

        def slot(s, parts):
            width = len(parts) * R
            first = MID if s % 2 == 0 else MID + KIB // 2 - 2 * width
            return ring.tile([P, width], BF16, name=f"slot{s}", offset=first, align_bytes=64)

        def y_tile(c, shape, name):
            return ring.tile(shape, F32, name=name, offset=MID + KIB // 2 if c % 2 else MID - 2 * KIB, align_bytes=64)

        for c in range(BANKS):
            first_layer(c, (0,))
        last = picked1[:, PACK - 1, :]
        woven1_0 = keep.tile([P, R], BF16, name="woven1_0", align_bytes=64)
        woven1_12 = keep.tile([P, 2 * R], BF16, name="woven1_12", align_bytes=64)[:]
        parts0 = [("h", 1), ("x1", 3), ("x1", 4)]
        slot0 = slot(0, parts0)
        for woven, c0, c1 in ((woven1_0[:], 0, 1), (woven1_12, 1, 3), (slot0[:, R:], 3, 5)):
            weave(woven, picked1, c0, c1, 0, 2)
        gather(last[:, :CH], PLANES - 1, 0, 1)
        gather(last[:, 4 * CH : 6 * CH], PLANES - 1, 1, 3)
        gather(last[:, 3 * CH : 4 * CH], PLANES - 1, 3, 4)
        weave(woven1_0[:], picked1, 0, 1, 2)
        quantize(run("x1", 0, 1), woven1_0[:])
        first_layer(0, (1,))
        moved = picked1_flat[:, 2 * J + CH : 2 * J + CH + 2 * (J + 3 * CH)].rearrange("p (t j) -> p t j", t=2)
        for half in range(2):
            nc.scalar.copy(
                woven1_12[:, half * R : (half + 1) * R].rearrange("p (c i t) -> p c t i", i=4, t=PACK)[:, :, 2:, :],
                moved[:, :, half * CH : (half + 1) * CH].rearrange("p t (c i) -> p c t i", i=4),
            )
        quantize(run("x0", 6, 8), woven0[6][:], codes_name="woven1_0")
        for c in (1, 2):
            quantize(run("x1", c, c + 1), woven1_12[:, (c - 1) * R : c * R])
            first_layer(c, (1,))
        gather(last[:, 4 * CH :], PLANES - 1, 4, CHUNKS)
        woven_h0 = keep.tile([P, R], BF16, name="woven_h0", align_bytes=64)
        vector_h(0, woven_h0[:])
        vector_h(1, slot0[:, :R])
        for c in (3, 4):
            weave(slot0[:, (c - 2) * R : (c - 1) * R], picked1, c, c + 1, 2)
        quantize(run("h", 0, 1), woven_h0[:])
        lead_ps = psum.tile([P, 1, CH], F32, name="lead_ps", tag="t1")
        second_layer(lead_ps[:, 0, :], 0, 0, 1)
        y_ps = psum.tile([P, 3, CH], F32, name="y_ps", tag="t0")
        for q in range(1, PAGES):
            second_layer(y_ps[:, q - 1, :], q, 0, 1)
        bring(2)
        quantize(parts0, slot0[:])

        def weigh_split(engine, c, y):
            three = keep.tile([P, 3 * CH], F32, name=f"three{c}", align_bytes=64)
            one = keep.tile([P, CH], F32, name=f"one{c}")
            weigh(engine, three[:], y[:, :3, :], c)
            weigh(engine, one[:], y[:, 3:, :], c)
            return [three[:, q * CH : (q + 1) * CH] for q in range(3)] + [one[:]]

        lead = keep.tile([P, CH], F32, name="lead0")
        two = keep.tile([P, 2 * CH], F32, name="three0", align_bytes=64)
        one = keep.tile([P, CH], F32, name="one0")
        weigh(nc.vector, lead[:], lead_ps[:], 0)
        weigh(nc.vector, two[:], y_ps[:, :2, :], 0)
        weigh(nc.vector, one[:], y_ps[:, 2:, :], 0)
        ready = [lead[:], two[:, :CH], two[:, CH:], one[:]]
        turned_out = psum.tile([P, P], F32, name="turned_out", tag="t0")
        nc.tensor.transpose(turned_out[:], gain_out[:, 4 * CH : 5 * CH], ident[:])
        by_pick = keep.tile([P, P // LANE], F32, name="by_pick")
        nc.scalar.copy(by_pick[:], turned_out[:, ::LANE])
        slot_parts = ([("x1", 5), ("h", 2)], [("h", 3), ("x1", 6)], [("x1", 7), ("h", 4)])
        for c, parts in enumerate(slot_parts):
            y_ps = chunk_y(c + 1, "t1")
            y = y_tile(c + 1, [P, PAGES, CH], f"y{c + 1}")
            nc.scalar.copy(y[:], y_ps[:])
            woven = slot(c + 1, parts)
            h_at = parts.index(("h", c + 2)) * R
            gpsimd_h(c + 2, woven[:, h_at : h_at + R])
            if c < 2:
                coming = weigh_split(nc.gpsimd, c + 1, y)
            else:
                whole = keep.tile([P, PAGES * CH], F32, name="weighed3")
                weigh(nc.gpsimd, whole[:], y[:], c + 1)
                coming = [whole[:, q * CH : (q + 1) * CH] for q in range(PAGES)]
            for i, (kind, chunk) in enumerate(parts):
                if kind == "x1":
                    weave(woven[:, i * R : (i + 1) * R], picked1, chunk, chunk + 1)
            first_layer(c + 3)
            bring(c + 3)
            for q in range(PAGES):
                put(q, c, c + 1, ready[q])
            quantize(parts, woven[:], codes_name=f"three{c}")
            ready = coming

        first_layer(6)
        bring(6)
        codes, scales, lo = quantised["h", 4]
        across_ps = psum.tile([P, 2 * P], F32, name="across_ps", tag="t1")
        nc.tensor.matmul_mx(
            across_ps[:],
            lhsT=codes[:, lo : lo + CH].bitcast(FP8X4),
            lhsT_scale=scales[:, lo : lo + CH],
            rhs=wd_w[:, : 4 * P].bitcast(FP4X4),
            rhs_scale=wd_s[:, : 2 * P],
            start=True,
            stop=True,
        )
        across = keep.tile([P, 2 * P], F32, name="across", align_bytes=64)
        for g in range(P // LANE):
            nc.scalar.activation(
                across[:].rearrange("p (q g r) -> p g q r", q=2, r=LANE)[:, g],
                across_ps[:].rearrange("p (q g r) -> p g q r", q=2, r=LANE)[:, g],
                COPY,
                scale=by_pick[:, g : g + 1],
            )
        back = psum.tile([P, 2, CH], F32, name="back", tag="u2")
        for q in range(2):
            nc.tensor.transpose(back[:, q, :], across[:, q * P : (q + 1) * P], ident[:])
        y_ps = psum.tile([P, PAGES, CH], F32, name="y_ps", tag="t0")
        for q in (2, 3):
            second_layer(y_ps[:, q, :], q, 4, 5)
        weighed = keep.tile([P, 2 * CH], F32, name="weighed4")
        for q in range(2):
            nc.scalar.copy(weighed[:, q * CH : (q + 1) * CH], back[:, q, :])
        first_layer(7)
        bring_gate(7)
        bring_up(7, "across")
        woven = slot(4, run("h", 5, 8))
        gpsimd_h(5, woven[:, :R])
        for c in (6, 7):
            gpsimd_h(c, woven[:, (c - 5) * R : (c - 4) * R])
        for q in range(PAGES):
            put(q, 3, 4, ready[q])
        for q in range(2):
            put(q, 4, 5, weighed[:, q * CH : (q + 1) * CH])
        quantize(run("h", 5, 8), woven[:])
        filler = ups[7][:, : 2 * CH]
        nc.scalar.copy(filler, y_ps[:, 2:, :].rearrange("p q j -> p (q j)"))
        for q in (2, 3):
            put_weighed(q, 4, 5, filler[:, (q - 2) * CH : (q - 1) * CH])
        y_end = keep.tile([P, PAGES, 3 * CH], F32, name="picked0")
        for q, bank in enumerate(("g0", "u0", "g1", "u1")):
            y_ps = psum.tile([P, 3 * CH], F32, name="y_ps", tag=bank)
            second_layer(y_ps[:, :CH], q, 5, 6)
            second_layer(y_ps[:, CH:], q, 6, 8)
            nc.scalar.copy(y_end[:, q, :], y_ps[:])
        for q in range(PAGES):
            put_weighed(q, 5, CHUNKS, y_end[:, q, :])
            nc.sync.dma_start(out[q * P : (q + 1) * P, :], pages[q][:])
